import numpy as np, ml_dtypes
CORES = [16,18,20,22]
N = 4
BF = ml_dtypes.bfloat16
W, L, S, H, CP = 4096, 2048, 3, 2, 64
def parts(rng):
    x = np.minimum((128 * rng.random((N, 8, 16, W), dtype=np.float32) * (0.25 + 0.75 * rng.random((N, 8, 1, W), dtype=np.float32))).astype(np.int64), 127)
    share = np.zeros((N, 8, W)) + rng.choice(np.array([0.01, 0.03, 0.06]), (N, 8, 1))
    for t in range(S):
        B = W - 256 * (t + 1)
        share[:, :, B:B + 256] = rng.choice(np.array([0.3, 0.6, 0.9]) if t == 0 else np.array([0.1, 0.3, 0.5]), (N, 8, 1))
    mk = (rng.random((N, 8, W)) < share).astype(np.int64)
    return x, mk, rng.integers(0, 4096, (N, 8, 16, L)), rng.integers(0, 4096, (N, 8, S * 256)), rng.integers(0, 256, (N, 8, 16)), rng.choice(np.array([1, 8, 20, 40, 80]), (N, 8))
def pack(x, mk, oc, dl, wt, th):
    return {"xc": x.reshape(N, 128, W).astype(np.float32).astype(BF), "mk": mk.astype(np.float32).astype(BF), "oc": oc.reshape(N, 128, L).astype(np.int32),
            "dl": dl.astype(np.int32), "wt": wt.reshape(N, 128, 1).astype(np.int32), "th": th.reshape(N, 8, 1).astype(np.int32)}
def setup_inputs(rng):
    return pack(*parts(rng))
def setup_inputs_spread(rng):
    x, mk, oc, dl, wt, th = parts(rng)
    x = np.minimum((np.exp2(8 * rng.random((N, 8, 1, W))) * rng.random((N, 8, 16, W))).astype(np.int64), 127)
    mk = (rng.random((N, 8, W)) < np.exp2(-6 * rng.random((N, 8, 1)))).astype(np.int64)
    oc = np.minimum((4096 * rng.random((N, 8, 16, L)) ** 3).astype(np.int64), 4095)
    flip = rng.integers(0, 2, (N, 8, 1, 1)); oc = np.where(flip == 1, 4095 - oc, oc)
    wt = np.minimum((np.exp2(8 * rng.random((N, 8, 16))) - 1).astype(np.int64), 255)
    th = np.minimum(np.exp2(11 * rng.random((N, 8))).astype(np.int64), 2032)
    th[:, rng.integers(0, 8)] = 1
    return pack(x, mk, oc, dl, wt, th)
def setup_inputs_ends(rng):
    x, mk, oc, dl, wt, th = parts(rng)
    kind = rng.integers(0, 3, (N, 8, 1, W)); x = 127 * np.where(kind == 2, rng.integers(0, 2, (N, 8, 16, W)), kind)
    mk = rng.integers(0, 2, (N, 8, W))
    E = np.array([0] + [W - 256 * (t + 1) - 1 for t in range(S)])
    c = rng.integers(0, 3, (N, 8)); c[:, 0] = 2; c[N - 1, 7] = 1; c[N - 2, 7] = 0; c[0, 5] = 2
    for q in range(N):
        for g in range(8):
            x[q, g][:, E] = 127 * rng.integers(0, 2, (16, len(E))) if c[q, g] == 2 else 127 * c[q, g]
    x[:, :, :, W - 1] = 127; mk[:, :, W - 1] = 1; mk[N - 1, 7, E] = 1
    oc = 4095 * rng.integers(0, 2, (N, 8, 16, L)); oc[:, :, :15, ::7] = 0; oc[:, :, 15, ::7] = 4095; oc[:, :, :, L - 1] = 4095
    dl = 4095 * rng.integers(0, 2, dl.shape)
    wt = 255 * rng.integers(0, 2, wt.shape); wt[N - 1, 7] = 255; wt[0, 5] = 0; wt[:, 2, 0] = 0; wt[:, 2, 15] = 255
    th = np.where(rng.integers(0, 2, (N, 8)) == 1, 2032, 1); th[:, 0] = 1; th[:, 1] = 2032; th[N - 2, 7] = 2032
    return pack(x, mk, oc, dl, wt, th)
def setup_inputs_corners(rng):
    x, mk, oc, dl, wt, th = parts(rng); B = W - 256
    u = np.arange(4096); lv = ((u * u >> 5) + 37 * u) & (L - 1); top = int(np.argmax(lv)); place = int(lv[top])
    for q in range(N):
        for g in range(8):
            n = int((0, 1, CP - 1, CP, CP + 1, 256)[int(rng.integers(0, 6))])
            if q == 0: n = (CP, CP + 1, 256, CP, CP + 1, 256, CP, CP)[g]
            if q == 1: n = 0
            if q == 2: n = 63 if g == 7 else 0
            if q == 3: n = (CP - 1, 1, 0, CP, CP + 1, 256, CP - 1, CP)[g]
            o = rng.permutation(256); e = B + o[:n]; rest = B + o[n:]; T = (1, 127)[int(rng.integers(0, 2))]; th[q, g] = T
            xg = x[q, g]; xg[15, :B] = 0; xg[15, e] = 127; xg[:15, e[::2]] = 0; xg[:, rest] = 0
            if T == 127: xg[15, rest[::2]] = 126
            if g == 4: mk[q, g, :B] = 0
            if g == 6: mk[q, g, :B] = 1
            mk[q, g, e] = 1; mk[q, g, rest] = rng.integers(0, 2, 256 - n)
            if g == 0: wt[q, g] = 0
            if g == 1: wt[q, g] = 255
            if g == 2: oc[q, g] = 4095 * rng.integers(0, 2, (16, L))
            if g == 5: oc[q, g] = oc[q, g, :1].copy()
            if g % 4 == 3:
                wt[q, g] = 0; wt[q, g, 0] = 1; wt[q, g, 1] = 128
                xg[0, e[1::2]] = top & 127; xg[1, e[1::2]] = top >> 7
                oc[q, g, :, place] = 4095 * rng.integers(0, 2, 16); oc[q, g, :, 0] = 4095 * rng.integers(0, 2, 16)
    return pack(x, mk, oc, dl, wt, th)
def setup_inputs_crowd(rng):
    x, mk, oc, dl, wt, th = parts(rng); s = int(rng.integers(0, 8)); low = W - 256 * S
    for q in range(N):
        for g in range(8):
            kind = (g + s) % 8; xg = x[q, g]; odd = [W - 256 * (t + 1) + int(rng.integers(0, 256)) for t in range(S)]
            if kind == 7: continue
            mk[q, g, low:] = 1; th[q, g] = 1
            if kind in (0, 1, 4):
                keep = xg[:, odd].copy(); xg[:, low:] = xg[:, W - 1:W].copy()
                if kind == 1: xg[:, odd] = keep
                if kind == 4: mk[q, g, odd] = 0
            if kind == 2:
                three = xg[:, W - 3:].copy(); xg[:, low:] = three[:, rng.integers(0, 3, 256 * S)]
            if kind == 3: oc[q, g] = int(rng.integers(0, 4096))
            if kind in (5, 6): wt[q, g] = 0
            if kind == 6:
                wt[q, g, 15] = 1; xg[15, :] = 0; xg[15, odd] = 64
    return pack(x, mk, oc, dl, wt, th)
def setup_inputs_edges(rng):
    x, mk, oc, dl, wt, th = parts(rng); B = W - 256; low = W - 256 * S
    p = [int(a) for a in rng.permutation(8)]; z = p[0]; e = int(rng.integers(0, N)); s = (e + 1) % N
    u = np.arange(4096); lv = ((u * u >> 5) + 37 * u) & (L - 1); pl, first = np.unique(lv, return_index=True); first = first[pl >= 64]
    x[:, z, :, low:] = rng.integers(64, 128, (N, 16, 256 * S)); x[:, z, :, 0] = 0; x[:, z, :, W // 8:W // 2] = 0
    mk[:, z, W // 8:W // 2] = 0; oc[:, z, :, :64] = 0; wt[:, z] = 0
    for t in range(S):
        Bt = W - 256 * (t + 1); c = W // 2 - 1 - t
        x[:, z, :, c] = 127; dl[:, z, t * 256:(t + 1) * 256] = -((-c * 4096) // Bt); mk[:, z, Bt + 255] = 1
    for q in range(N):
        for g, pair in ((p[1], (257, 385)), (p[2], (513, 1001))):
            T = pair[int(rng.integers(0, 2))]; th[q, g] = T
            x[q, g, 4:, :B] = 0; x[q, g, :, B:] = 0; mk[q, g, B:] = rng.integers(0, 2, 256)
            o = B + rng.permutation(256)[:40]; tot = T - (np.arange(40) & 1); dv = rng.integers(-20, 21, (6, 40))
            v = np.concatenate([dv, -dv]) + tot // 12; v[11] += tot % 12
            x[q, g][4:, o] = v; mk[q, g, o] = 1
        g = p[3]; two = [int(a) for a in rng.permutation(low)[:2]]
        for k, c in ((0, two[0]), (int(rng.integers(1, 16)), two[1])):
            oc[q, g, k] = -((-c * 4096) // B); x[q, g, :, c] = 127; mk[q, g, c] = 1
        x[q, g, int(rng.integers(0, 16)), two[0]] = 126 * int(rng.integers(0, 2)); x[q, g, :, B::2] = 127; mk[q, g, B::2] = 1
        g = p[4]; us = rng.permutation(first)[:256]
        wt[q, g] = 0; wt[q, g, 0] = 1; wt[q, g, 1] = 128; x[q, g, :2, :B] = 0
        x[q, g, 0, B:] = us & 127; x[q, g, 1, B:] = us >> 7; mk[q, g, B:] = 1
        oc[q, g] = oc[q, g] & 4094; dl[q, g, :256] = dl[q, g, :256] | 1
    mk[s, p[:1] + p[3:], B:] = 0
    x[e, :, :, W - 512:W - 256] = 0
    return pack(x, mk, oc, dl, wt, th)
def check_inputs(d):
    bad = []
    for k, lo, hi in (("xc", 0, 127), ("mk", 0, 1), ("oc", 0, 4095), ("dl", 0, 4095), ("wt", 0, 255), ("th", 1, 2032)):
        v = np.asarray(d[k]).astype(np.float64)
        if not (np.min(v) >= lo and np.max(v) <= hi): bad.append("range of " + k)
        elif np.any(v != np.floor(v)): bad.append("whole numbers of " + k)
    return bad
def hop(y, x, m, o, w, A, B):
    n = y.shape[2]
    u = np.add.reduce(w[:, :, None] * y, axis=1) & 4095
    l = ((u * u >> 5) + 37 * u + A) & (L - 1)
    c = (np.take_along_axis(o, l[:, None, :], 2) * B) >> 12
    cc = c.reshape(8, 16 * n)
    v = np.take_along_axis(x, cc[:, None, :], 2).reshape(8, 16, 16, n)
    s = np.add.reduce(np.minimum(v, y[:, :, None, :]), axis=1) + 256 * np.take_along_axis(m, cc, 1).reshape(8, 16, n)
    k = np.argmax(s, axis=1)
    return l, s, np.take_along_axis(c, k[:, None, :], 1)[:, 0]
def reference(xc, mk, oc, dl, wt, th):
    x = xc.astype(np.float32).astype(np.int64).reshape(N, 8, 16, W); m = mk.astype(np.float32).astype(np.int64).reshape(N, 8, W)
    o = oc.astype(np.int64).reshape(N, 8, 16, L); w = wt.astype(np.int64).reshape(N, 8, 16); d = dl.astype(np.int64); lim = th.astype(np.int64).reshape(N, 8, 1)
    A = [0] * N; ya = np.full((N, 8, S, H, 256), -1, np.int64)
    for t in range(S):
        B = W - 256 * (t + 1)
        box = np.zeros((N, 8, 16, CP), np.int64); full = np.zeros((N, 8, CP), bool)
        for r in range(N):
            y = x[r, :, :, B:B + 256]; live = m[r, :, B:B + 256] == 1
            for h in range(H):
                l, s, a = hop(y, x[r], m[r], o[r], w[r], A[r], B)
                ya[r, :, t, h] = np.where(live, a, -1)
                for g in range(8): m[r, g, a[g][live[g]]] = 1
                y = np.maximum(y - np.take_along_axis(x[r], a[:, None, :], 2), 0)
            k = np.argmin(s, axis=1)
            go = live & (np.add.reduce(y, axis=1) >= lim[r])
            for g in range(8):
                i = np.flatnonzero(live[g]); i = i[np.unique(l[g, i], return_index=True)[1]]
                o[r, g, k[g, i], l[g, i]] = d[r, g, t * 256 + i]
                j = np.flatnonzero(go[g])[:CP]
                box[r, g, :, :len(j)] = y[g][:, j]; full[r, g, :len(j)] = True
        for r in range(N):
            q = (r - 1 - t % (N - 1)) % N
            l, s, a = hop(box[q], x[r], m[r], o[r], w[r], A[r], B)
            for g in range(8): m[r, g, a[g][full[q, g]]] = 1
            A[r] = int(np.count_nonzero(full[q])) & 63
    return {"ya": ya.reshape(N, 8, S * H * 256).astype(np.float32), "ym": m.astype(np.float32).astype(BF), "yo": o.reshape(N, 128, L).astype(np.float32)}

@@ -1,0 +1,669 @@
+from concourse.mybir import AluOpType, ActivationFunctionType
+
+A = AluOpType
+F = ActivationFunctionType
+W, L, S = 4096, 2048, 3
+
+SCRATCH = {
+    "X": ("sbuf", [128, 4096], "bfloat16"),
+    "OCI": ("sbuf", [128, 2048], "int32"),
+    "OC": ("sbuf", [128, 2064], "float32"),
+    "MT": ("sbuf", [128, 4112], "float32"),
+    "MN": ("sbuf", [128, 4096], "bfloat16"),
+    "MG": ("sbuf", [128, 4096], "bfloat16"),
+    "MNr": ("sbuf", [128, 1024], "bfloat16"),
+    "MGr": ("sbuf", [128, 1024], "bfloat16"),
+    "YR0": ("sbuf", [128, 4096], "bfloat16"),
+    "YR1": ("sbuf", [128, 4096], "bfloat16"),
+    "YR2": ("sbuf", [128, 4096], "bfloat16"),
+    "YRh": ("sbuf", [128, 4096], "bfloat16"),
+    "YRr": ("sbuf", [128, 1024], "bfloat16"),
+    "DL": ("sbuf", [128, 768], "int32"),
+    "WI": ("sbuf", [128, 8], "int32"),
+    "TI": ("sbuf", [128, 8], "int32"),
+    "YA": ("sbuf", [128, 1536], "float32"),
+    "box0": ("sbuf", [128, 528], "bfloat16"),
+    "box1": ("sbuf", [128, 528], "bfloat16"),
+    "box2": ("sbuf", [128, 528], "bfloat16"),
+    "land0": ("sbuf", [128, 80], "bfloat16"),
+    "land1": ("sbuf", [128, 80], "bfloat16"),
+    "land2": ("sbuf", [128, 80], "bfloat16"),
+    "AF": ("sbuf", [128, 8192], "float32"),
+    "AB": ("sbuf", [128, 12288], "bfloat16"),
+    "AI": ("sbuf", [128, 4096], "int32"),
+    "AU": ("sbuf", [128, 4096], "uint16"),
+    "K0": ("psum", [128, 512], "float32"),
+    "K1": ("psum", [128, 512], "float32"),
+    "Kr": ("psum", [128, 512], "float32"),
+    "PU": ("psum", [128, 512], "float32"),
+    "XX": ("psum", [128, 512], "float32"),
+    "X3": ("psum", [128, 512], "float32"),
+    "PL": ("psum", [128, 512], "float32"),
+    "SM": ("psum", [128, 512], "float32"),
+}
+SEMAPHORES = ["cV", "cA", "cP", "cG", "sent", "arr0", "arr1", "arr2"] + ["d%d" % i for i in range(24)]
+
+BANKS = ("K0", "K1", "Kr", "PU", "XX", "X3", "PL", "SM")
+SC = 16384.0
+OFFS = 65.0 / 512.0
+Z2 = 1.5498553
+BIG = 1048576.0
+PAR = {
+    "NH": 2,
+    "CH": [[4, 4, 4, 4], [4, 4, 4, 2, 2]],
+    "CHR": [6, 6, 2, 2],
+    "HELP": {},
+    "LAG": {(0, 0, 0): 4, (0, 0, 1): 8, (1, 0, 1): 8, (2, 0, 1): 8, (0, 1, 1): 8},
+    "LAGR": 0,
+    "REP0": "VVVVVVVVVVAAAGGG", "REP": "VVVVVVVVVVVVVVVV", "REPR": "VVVVVVVVVVAAAAAA",
+    "YA": "VV", "MTA": 6,
+    "SIG": 110.0, "GA": 1.56, "SCA": 3.8, "PE": 0.42, "ROUNDS": 1200, "SEED": 1, "NOISE": 1500.0,
+}
+NENG = 4
+
+
+def build(g, T, dst_of, topo, core):
+    ops = []
+    arena = {}
+    fill = {"AF": 0, "AB": 0, "AI": 0, "AU": 0}
+    NH, GA, SCA = PAR["NH"], PAR["GA"], PAR["SCA"]
+    N = 16 // NH
+    BW = 16 * N
+
+    def ap(kind, name, n, a=0, b=None, st=1):
+        if name not in arena:
+            arena[name] = fill[kind]
+            fill[kind] += (n + 15) // 16 * 16
+        o = arena[name]
+        b = n if b is None else b
+        return T[kind][:, o + a:o + b:st] if st != 1 else T[kind][:, o + a:o + b]
+
+    def op(eng, fn, cost, r=(), w=(), lat=0.0, dma=None):
+        ops.append({"e": eng, "fn": fn, "c": cost, "r": list(r), "w": list(w), "lat": lat, "dma": dma})
+
+    V, Ac, P = g.vector, g.scalar, g.tensor
+
+    def ts(out, in0, s1, s2, o0, o1, n, r, w, f=1.0):
+        if o1 is None:
+            op("V", lambda: V.tensor_scalar(out, in0, s1, None, o0), max(64, n * f), r, w)
+        else:
+            op("V", lambda: V.tensor_scalar(out, in0, s1, s2, o0, o1), max(64, n * f), r, w)
+
+    def tt(out, a, b, o, n, r, w, f=2.0):
+        op("V", lambda: V.tensor_tensor(out, a, b, o), max(64, n * f), r, w)
+
+    def tg(out, a, b, o, c, r, w):
+        op("V", lambda: V.tensor_tensor(out, a, b, o), c, r, w)
+
+    def cp(out, a, n, r, w, f=1.0):
+        op("V", lambda: V.tensor_copy(out, a), max(64, n * f), r, w)
+
+    def scan(out, d0, d1, o0, o1, n, r, w, f=1.0):
+        op("V", lambda: V.tensor_tensor_scan(out, d0, d1, 0.0, o0, o1), max(64, n * f), r, w)
+
+    def ms(a, v, n, w):
+        op("V", lambda: V.memset(a, v), max(64, n), [], w)
+
+    def act(out, a, fn, c, r, w, bias=0.0, scale=1.0):
+        kw = {}
+        if not (isinstance(bias, float) and bias == 0.0):
+            kw["bias"] = bias
+        if not (isinstance(scale, float) and scale == 1.0):
+            kw["scale"] = scale
+        op("A", lambda: Ac.activation(out, a, fn, **kw), c, r, w)
+
+    def rep(eng, out, a, sign, n, r, w):
+        if eng == "V":
+            ts(out, a, sign, None, A.mult, None, n, r, w, 0.5)
+        elif eng == "A":
+            act(out, a, F.Copy, 78 + n, r, w, scale=sign)
+        else:
+            op("G", lambda: g.affine_select(out, a, [[0, n]], A.is_gt, 0.0, 1, 0), 200 + 2 * n, r, w)
+
+    def mm(out, l, rh, st, sp, n, r, w):
+        op("P", lambda: P.matmul(out, l, rh, st, sp), max(64, n) * PAR["PE"] + 8, r, w)
+
+    def iota(out, pat, n, w, cm=0, fl=True):
+        if fl:
+            op("G", lambda: g.iota(out, pat, 0, cm, allow_small_or_imprecise_dtypes=True), 150 + 2 * n, [], w)
+        else:
+            op("G", lambda: g.iota(out, pat, 0, cm), 150 + 2 * n, [], w)
+
+    nd = [0]
+
+    def dma(eng, out, in_, r, w, lat, grp=None):
+        if grp is None:
+            grp = "d%d" % nd[0]
+            nd[0] += 1
+        q = {"S": g.sync, "A": g.scalar, "G": g}[eng]
+        op(eng, lambda: q.dma_start(out, in_), 900 if eng == "G" else 60, r, list(w) + ["~" + eng], lat=lat, dma=grp)
+
+    f = lambda name, n, *a: ap("AF", name, n, *a)
+    b = lambda name, n, *a: ap("AB", name, n, *a)
+    i = lambda name, n, *a: ap("AI", name, n, *a)
+    u = lambda name, n, *a: ap("AU", name, n, *a)
+
+    dma("S", T.X[:, 3328:4096], T.xc[:, 3328:4096], [], ["Xl"], 2200)
+    dma("A", T.WI[:, 0:1], T.wt[:], [], ["WI"], 2000)
+    dma("S", T.OCI[:, 0:1024], T.oc[:, 0:1024], [], ["OCI0"], 3800)
+    dma("S", T.OCI[:, 1024:2048], T.oc[:, 1024:2048], [], ["OCI1"], 5400)
+    dma("S", T.X[:, 0:3328], T.xc[:, 0:3328], [], ["Xr"], 8000)
+    for j in range(16):
+        dma("S", T.DL[j:128:16, :], T.dl[:], [], ["DL%d" % j], 9000, "d23")
+        dma("S", T.TI[j:128:16, 0:1], T.th[:], [], ["TI%d" % j], 9000, "d23")
+    DLT = ["DL%d" % j for j in range(16)] + ["TI%d" % j for j in range(16)]
+
+    iota(i("pi", 1), [[0, 1]], 1, ["pi"], 1, False)
+    iota(f("I144", 144), [[1, 144]], 144, ["I144"])
+    iota(f("IG", 128), [[16, 8], [0, 16]], 128, ["IG"])
+    iota(f("II", 256), [[0, 16], [1, 16]], 256, ["II"])
+    iota(b("IDX", 256), [[1, 256]], 256, ["IDX"])
+    iota(f("IDX2", 256), [[0, NH], [2, BW]], 256, ["IDX2"])
+    iota(f("SLOT", 64), [[1, 4], [4, 16]], 64, ["SLOT"])
+    iota(f("IT0", 16), [[BW, NH], [16 // N, N]], 16, ["IT0"])
+    iota(f("IN", 16), [[0, NH], [1, N]], 16, ["IN"])
+    iota(f("IT1", 16), [[BW, NH], [1, N]], 16, ["IT1"])
+    ts(i("ji", 1), i("pi", 1), 15, None, A.bitwise_and, None, 1, ["pi"], ["ji"])
+    ts(i("gi", 1), i("pi", 1), 112, None, A.bitwise_and, None, 1, ["pi"], ["gi"])
+    ts(i("jl", 1), i("pi", 1), N - 1, None, A.bitwise_and, None, 1, ["pi"], ["jl"])
+    ts(i("jh", 1), i("ji", 1), N.bit_length() - 1, None, A.arith_shift_right, None, 1, ["ji"], ["jh"])
+
+    def col(name, src, s1, o0):
+        ts(f(name, 1), i(src, 1), s1, None, o0, None, 1, [src], [name])
+
+    def acol(name, src, scale, bias, dep=()):
+        act(f(name, 1), f(src, 1), F.Identity, 80, [src] + list(dep), [name], bias=bias, scale=scale)
+
+    col("g15", "gi", 15.0, A.add)
+    col("jf", "ji", 1.0, A.mult)
+    col("jl16", "jl", 16.0, A.mult)
+    col("jhf", "jh", 1.0, A.mult)
+    col("r0", "ji", 0.0, A.is_equal)
+    col("r1", "ji", 1.0, A.is_equal)
+    col("r2", "ji", 2.0, A.is_equal)
+    acol("gf", "g15", 1.0, -15.0)
+    acol("jN", "jf", float(N), 0.0)
+    acol("j64", "jf", 64.0, 0.0)
+    acol("jB", "jf", float(BW), 0.0)
+    acol("j32", "jf", 1.0, 32.0)
+    acol("dumM", "jf", 1.0, 4096.0)
+    acol("dumL", "jf", 1.0, 2048.0)
+    acol("r0m", "r0", -65536.0, 0.0)
+    acol("r0l", "r0", -4096.0, 0.0)
+    acol("r0n", "r0", -1.0, 0.0)
+    acol("r0z", "r0", Z2, 0.0)
+    acol("nr0", "r0", -1.0, 1.0)
+    acol("r2s", "r2", 1.0 / SC, 0.0)
+    acol("r12s", "r1", 64.0 / SC, f("r2s", 1), ["r2s"])
+    tt(f("r12", 1), f("r1", 1), f("r2", 1), A.add, 1, ["r1", "r2"], ["r12"])
+    ts(f("r12x", 1), f("r12", 1), 32.0, None, A.mult, None, 1, ["r12"], ["r12x"])
+    cp(f("wp", 1), T.WI[:, 0:1], 1, ["WI"], ["wp"])
+    acol("wn", "wp", -1.0, 0.0)
+    cp(f("th", 1), T.TI[:, 0:1], 1, DLT, ["th"])
+    ms(f("A0", 1), -0.375, 1, ["A0"])
+
+    def Z(name, j):
+        return b(name, 144, 15 - j, 143 - j)
+
+    for name, val, dep in (("Zp", f("wp", 1), ["wp"]), ("Zs", -256.0, []), ("Zm", f("r0m", 1), ["r0m"])):
+        ts(b(name, 144), f("I144", 144), f("g15", 1), val, A.is_equal, A.mult, 144, ["I144", "g15"] + dep, [name])
+    act(b("Zn", 144), b("Zp", 144), F.Copy, 222, ["Zp"], ["Zn"], scale=-1.0)
+    ts(b("B1", 128), f("IG", 128), f("gf", 1), None, A.is_equal, None, 128, ["IG", "gf"], ["B1"])
+    for name, val in (("Ba", "r12s"), ("B0", "r0"), ("B0n", "r0n"), ("B2", "r2"), ("B0l", "r0l"), ("Bwn", "wn")):
+        act(b(name, 128), b("B1", 128), F.Copy, 206, ["B1", val], [name], scale=f(val, 1))
+    act(b("B1n", 128), b("B1", 128), F.Copy, 206, ["B1"], ["B1n"], scale=-1.0)
+    op("G", lambda: g.affine_select(b("ID", 128), b("B1", 128), [[-1, 128]], A.is_equal, 0.0, 0, 1), 456, ["B1"], ["ID"])
+    op("G", lambda: g.affine_select(b("TRI", 128), b("B1", 128), [[1, 128]], A.is_gt, 0.0, 0, -1), 456, ["B1"], ["TRI"])
+    ms(b("ON", 128), 1.0 / 16, 64, ["ON"])
+    ms(b("OF", 256), -OFFS, 128, ["OF"])
+    ts(b("eq", 256), f("II", 256), f("jf", 1), None, A.is_equal, None, 256, ["II", "jf"], ["eq"])
+    ts(b("gt", 256), f("II", 256), f("jf", 1), 4.0, A.is_gt, A.mult, 256, ["II", "jf"], ["gt"])
+    act(b("CC", 512, 0, 256), b("eq", 256), F.Identity, 334, ["eq"], ["C1"], bias=-4.0, scale=4.0 - OFFS)
+    act(b("CC", 512, 256, 512), b("gt", 256), F.Identity, 334, ["gt"], ["C2"], bias=4.0, scale=-(4.0 + OFFS) / 4.0)
+    act(b("MK", BW), b("eq", 256, 0, BW), F.Identity, 78 + BW, ["eq"], ["MK"], bias=-BIG, scale=BIG)
+    tt(b("C3", 256), b("gt", 256), b("eq", 256), A.subtract, 256, ["gt", "eq"], ["C3"])
+    act(b("R0", 256), f("II", 256), F.Sign, 334, ["II"], ["R0"])
+    act(f("RB", 256), b("R0", 256), F.Identity, 334, ["R0"], ["RB"], bias=8388608.0, scale=-8388608.0)
+    ts(u("T0", 16), f("IT0", 16), f("jl16", 1), f("jhf", 1), A.add, A.add, 16, ["IT0", "jl16", "jhf"], ["T0"])
+    ts(u("T1", 16), f("IT1", 16), f("jN", 1), None, A.add, None, 16, ["IT1", "jN"], ["T1"])
+    cp(u("Boff", 16), f("I144", 144, 0, 16), 16, ["I144"], ["Boff"])
+    ts(f("DD", 16), f("IT1", 16), f("jN", 1), 256.0, A.add, A.add, 16, ["IT1", "jN"], ["DD"])
+    ts(b("RN", 16), f("IN", 16), 0.0, None, A.not_equal, None, 16, ["IN"], ["RN"])
+    for t in range(S):
+        ms(T["box%d" % t][:, 0:80], 0.0, 40, ["box%d" % t, "bc%d" % t])
+
+    ts(f("st1", 8), f("I144", 144, 0, 8), f("r1", 1), None, A.mult, None, 8, ["I144", "r1"], ["st1"])
+    ts(f("st8", 8), f("I144", 144, 0, 8), f("r1", 1), 8.0, A.mult, A.mult, 8, ["I144", "r1"], ["st8"])
+    ts(f("seed", 64), f("I144", 144, 0, 64), f("r2", 1), f("r12x", 1), A.mult, A.add, 64, ["I144", "r2", "r12x"], ["seed"])
+    for k in range(8):
+        ts(T.MT[:, 64 * k:64 * k + 64], f("seed", 64), f("st1", 8, k, k + 1), None, A.add, None, 64, ["seed", "st1"], ["mta%d" % k])
+    base = ["mta%d" % k for k in range(8)]
+    for k in range(1, 8):
+        if k <= PAR["MTA"]:
+            act(T.MT[:, 512 * k:512 * k + 512], T.MT[:, 0:512], F.Identity, 600, base + ["st8"], ["mtb%d" % k], bias=f("st8", 8, k, k + 1))
+        else:
+            ts(T.MT[:, 512 * k:512 * k + 512], T.MT[:, 0:512], f("st8", 8, k, k + 1), None, A.add, None, 512, base + ["st8"], ["mtb%d" % k])
+    dma("G", T.MT[0:128:16, 0:4096], T.mk[:], [], base + ["mtb%d" % k for k in range(1, 8)] + ["MT"], 2500)
+    for k in range(4):
+        cp(T.OC[:, 512 * k:512 * k + 512], T.OCI[:, 512 * k:512 * k + 512], 512, ["OCI%d" % (k // 2)], ["OCp%d" % k])
+    OCP = ["OCp%d" % k for k in range(4)]
+
+    for t in range(S):
+        B = W - 256 * (t + 1)
+        act(b("yT%d" % t, 256), T.X[:, B:B + 256].indirect(u("T0", 16)), F.Copy, 78 + GA * 256, ["Xl", "T0"], ["yT%d" % t])
+    YRT = {}
+
+    def rep0(t):
+        YRT[t] = ["YR%d_%d" % (t, k) for k in range(16)]
+        for k in range(16):
+            rep(PAR["REP0"][k] if t == 0 else "G", T["YR%d" % t][:, k:4096:16], b("yT%d" % t, 256), 1.0, 256, ["yT%d" % t], [YRT[t][k]])
+
+    def square(tag, src, stok, n):
+        cp(i("ui" + tag, n), src, n, [stok], ["ui" + tag])
+        ts(i("u" + tag, n), i("ui" + tag, n), 4095, None, A.bitwise_and, None, n, ["ui" + tag], ["u" + tag])
+        ts(f("t" + tag, n), i("u" + tag, n), 1.0 / 32, 37.0, A.mult, A.add, n, ["u" + tag], ["t" + tag])
+        tt(f("q" + tag, n), i("u" + tag, n), f("t" + tag, n), A.mult, n, ["u" + tag, "t" + tag], ["q" + tag])
+
+    def u_part(tag, rhs, rtok, zname, n):
+        for x, r in enumerate(rhs):
+            for j in range(16):
+                mm(T.PU[:, x * n:x * n + n], Z(zname, j), r(j), j == 0, j == 15, n, [zname] + rtok, ["PU"])
+        n = n * len(rhs)
+        square(tag, T.PU[:, 0:n], "PU", n)
+
+    def place(tag, n, an, t, ctag, lt, a0, first=False, q0=0):
+        B = W - 256 * (t + 1)
+        l, lu = i("l" + lt, 16, a0, a0 + n), u("lu" + lt, 16, a0, a0 + n)
+        q, qt = f("q" + tag, n, q0, q0 + n), "q" + tag
+        tag = tag + lt[1:2] * (lt[0] == "a")
+        ts(i("li" + tag, n), q, f(an, 1), None, A.add, None, n, [qt, an], ["li" + tag])
+        ts(l, i("li" + tag, n), 2047, None, A.bitwise_and, None, n, ["li" + tag], ["l" + tag])
+        cp(lu, l, n, ["l" + tag], ["lu" + tag])
+        win = T.OCI[:, 0:2048] if first else T.OC[:, 0:2048]
+        op("V", lambda: V.tensor_scalar(u(ctag, 16 * n), win.indirect(lu), B / 4096.0, -15.0 / 32, A.mult, A.add),
+           60 + GA * 16 * n, ["lu" + tag] + (["OCI0", "OCI1"] if first else ["OC"] + OCP), [ctag])
+
+    def main(ctag, c0, n, K, mn, mg, yr, a0, yrt, chunks, help_, lag):
+        bw = 16 * n
+        o = T[K][:, 0:bw]
+        mm(o, b("ID", 128), b("IDX", 256, 0, bw), True, False, bw, ["ID", "IDX"], [K])
+        mchunks = []
+        for c in chunks:
+            a = sum(mchunks)
+            mchunks += [16 - help_ - a, a + c - 16 + help_] if a < 16 - help_ < a + c else [c]
+        a = 0
+        for c in chunks:
+            e = a + c
+            off = u(ctag, 16 * n, c0 + a * n, c0 + e * n)
+            sl = slice(a0 + a * bw, a0 + e * bw)
+            tg(T[mn][:, sl], T.X[:, 0:4096].indirect(off), T[yr][:, sl], A.min, 60 + GA * c * bw,
+               [ctag, "Xl", "Xr"] + yrt, ["%s%d_%d" % (mn, a0, x) for x in range(a, e)] + ["~mV"])
+            a = e
+        a = 0
+        for c in mchunks:
+            e = a + c
+            off = u(ctag, 16 * n, c0 + a * n, c0 + e * n)
+            sl = slice(a0 + a * bw, a0 + e * bw)
+            wt_ = ["%s%d_%d" % (mg, a0, x) for x in range(a, e)]
+            if e > 16 - help_:
+                op("V", lambda off=off, sl=sl: V.tensor_copy(T[mg][:, sl], T.MT[:, 0:4096].indirect(off)), 60 + GA * c * bw, [ctag, "MT"], wt_ + ["~mV"])
+            else:
+                act(T[mg][:, sl], T.MT[:, 0:4096].indirect(off), F.Copy, 78 + GA * c * bw, [ctag, "MT"], wt_ + ["~mA"])
+            a = e
+        ends, mends = [], []
+        for c in chunks:
+            ends += [len(ends) + c] * c
+        for c in mchunks:
+            a = len(mends)
+            mends += [a + c + lag + 0.5 if a < 16 - help_ else a + c + help_ + 0.25] * c
+        seq = sorted([(x, 0) for x in range(16)] + [(x, 1) for x in range(16)], key=lambda z: (mends if z[1] else ends)[z[0]])
+        for z, (x, m) in enumerate(seq):
+            src, zn = (mg, "Zm") if m else (mn, "Zs")
+            mm(o, Z(zn, x), T[src][:, a0 + x * bw:a0 + (x + 1) * bw], False, z == 31, bw, [zn, "%s%d_%d" % (src, a0, x)], [K])
+
+    def pick(tag, n, K, jn):
+        bw = 16 * n
+        scan(f("R" + K, bw), f("RB", 256, 0, bw), T[K][:, 0:bw], A.add, A.min, bw, ["RB", K], ["R" + K])
+        ts(i("ki" + tag, n), f("R" + K, bw, 15, bw, 16), BIG, None, A.add, None, n, ["R" + K], ["ki" + tag])
+        ts(i("kx" + tag, n), i("ki" + tag, n), 255, None, A.bitwise_and, None, n, ["ki" + tag], ["kx" + tag])
+        ts(u("ku" + tag, n), i("kx" + tag, n), f(jn, 1), None, A.add, None, n, ["kx" + tag, jn], ["ku" + tag])
+
+    def toks(name, a0):
+        return ["%s%d_%d" % (name, a0, x) for x in range(16)]
+
+    def mark(tag, n, mg, a0, nl, nlt, ag, s):
+        bw = 16 * n
+        at = "ag" + tag[0] + s
+        x1, x2 = T.XX[:, 0:bw], T.XX[:, bw:2 * bw]
+        mm(T.XX[:, 0:2 * bw], b("ID", 128), b("CC", 512, 256 - bw, 256 + bw), True, False, 2 * bw, ["ID", "C1", "C2"], ["XX"])
+        for x in (x1, x2):
+            mm(x, b("B0", 128), nl, False, False, bw, ["B0", nlt], ["XX"])
+        act(ag, T[mg][:, a0:a0 + 16 * bw].indirect(u("ku" + tag, n)), F.Copy, 78 + GA * bw, toks(mg, a0) + ["ku" + tag], [at])
+        mm(x1, b("Ba", 128), ag, False, False, bw, ["Ba", at], ["XX"])
+        mm(x2, b("Ba", 128), ag, False, True, bw, ["Ba", at], ["XX"])
+        act(f("agf" + s, bw), ag, F.Silu, 78 + bw, [at, "nr0", "r0z"], ["agf" + s], bias=f("r0z", 1), scale=f("nr0", 1))
+        scan(f("H" + s, bw), b("R0", 256, 0, bw), x1, A.mult, A.max, bw, ["R0", "XX"], ["H" + s])
+        tt(b("E" + s, bw), x2, f("H" + s, bw), A.is_equal, bw, ["XX", "H" + s], ["E" + s], 1.0)
+        scan(b("Fs" + s, bw), b("R0", 256, 0, bw), b("E" + s, bw), A.mult, A.max, bw, ["R0", "E" + s], ["Fs" + s], 0.5)
+        tt(f("G" + tag, n), b("Fs" + s, bw, 15, bw, 16), f("H" + s, bw, 15, bw, 16), A.max, n, ["Fs" + s, "H" + s], ["G" + tag])
+        ts(u("mo" + tag, 2 * n, 0, 2 * n, 2), f("G" + tag, n), SC, f("dumM", 1), A.mult, A.min, n, ["G" + tag, "dumM"], ["mo" + tag])
+        for c in range(n):
+            act(T.MT[:, 0:4112].indirect(u("mo" + tag, 2 * n, 2 * c, 2 * c + 1)), f("agf" + s, bw, 16 * c, 16 * c + 16), F.Silu,
+                78 + SCA * 16, ["mo" + tag, "agf" + s], ["MT"])
+
+    def lanes0(ts_):
+        def rhs(t, h, j):
+            a = W - 256 * (t + 1) + BW * h + 16 * (j % N) + j // N
+            return T.X[:, a:a + (N - 1) * NH + 1:NH]
+        u_part("a%d" % ts_[0], [lambda j, t=t, h=h: rhs(t, h, j) for t in ts_ for h in range(NH)], ["Xl"], "Zp", N)
+
+    def place0(t):
+        place("a%d" % min(t, 1), 16, "A%d" % t, t, "ca", "a%d" % t, 0, t == 0, 16 * max(t - 1, 0))
+
+    rep0(0)
+    lanes0([0])
+    place0(0)
+    lanes0([1, 2])
+    rep0(1)
+    for t in range(S):
+        B = W - 256 * (t + 1)
+        tr = "r%d" % t
+        nln, nlt = "NL%d" % t, "NT%d" % t
+        H = list(range(NH - 1, -1, -1))
+        part = lambda name, h: b(name, 256, BW * h, BW * h + BW)
+        act(b(nln, 256), T.MT[:, B:B + 256], F.Relu, 78 + 256, ["MT"], [nln], bias=1.0, scale=-2.0)
+        act(b(nlt, 256), T.MT[:, B:B + 256].indirect(u("T1", 16)), F.Relu, 78 + GA * 256, ["MT", "T1"], [nlt], bias=1.0, scale=-2.0)
+        for h in H:
+            main("ca", BW * h, N, "K%d" % h, "MN", "MG", "YR%d" % t, 16 * BW * h, YRT[t], PAR["CH"][NH - 1 - h],
+                 PAR["HELP"].get((t, 0, NH - 1 - h), 0), PAR["LAG"].get((t, 0, NH - 1 - h), 0))
+        yrt = {}
+        for h in H:
+            ta, tb, a0 = "a%d%d" % (t, h), "b%d%d" % (t, h), 16 * BW * h
+            pick(ta, N, "K%d" % h, "jB")
+            tg(part("y1n", h), T.MN[:, a0:a0 + 16 * BW].indirect(u("ku" + ta, N)), T.X[:, B + BW * h:B + BW * h + BW], A.subtract,
+               60 + GA * BW, toks("MN", a0) + ["ku" + ta, "Xl"], ["y1n%d" % h])
+            mark(ta, N, "MG", a0, part(nln, h), nln, part("aga", h), str(h))
+            u_part(tb, [lambda j: b("y1n", 256, BW * h + j, BW * h + BW, 16)], ["y1n%d" % h], "Zn", N)
+            yrt[h] = ["YRh%d_%d" % (h, k) for k in range(16)]
+            for k in range(16):
+                rep(PAR["REP"][k], T.YRh[:, a0 + k:a0 + 16 * BW:16], part("y1n", h), -1.0, BW, ["y1n%d" % h], [yrt[h][k]])
+            place(tb, N, "A%d" % t, t, "cb%d" % h, "b%d" % t, N * h)
+        Y1 = ["y1n%d" % h for h in H]
+        act(b("y1T", 256), b("y1n", 256).indirect(u("T1", 16)), F.Copy, 78 + GA * 256, Y1 + ["T1"], ["y1T"], scale=-1.0)
+        mm(T.X3[:, 0:256], b("ID", 128), b("OF", 256), True, False, 256, ["ID", "OF"], ["X3"])
+        mm(T.X3[:, 0:256], b("B0n", 128), b(nln, 256), False, False, 256, ["B0n", nln], ["X3"])
+        mm(T.X3[:, 0:256], b("Ba", 128), b("aga", 256), False, True, 256, ["Ba"] + ["aga%d" % h for h in H], ["X3"])
+        for h in H:
+            main("cb%d" % h, 0, N, "K%d" % h, "MN", "MG", "YRh", 16 * BW * h, yrt[h], PAR["CH"][NH - 1 - h],
+                 PAR["HELP"].get((t, 1, NH - 1 - h), 0), PAR["LAG"].get((t, 1, NH - 1 - h), 0))
+        tb = "b%d" % t
+        LU, LL = ["lu%s%d" % (tb, h) for h in H], ["l%s%d" % (tb, h) for h in H]
+        act(f("nn", 256), T.OC[:, 0:2048].indirect(u("lu" + tb, 16)), F.Copy, 78 + GA * 256, ["OC"] + OCP + LU, ["nn"])
+        act(b("lg", 256), T.MT[:, 0:2048].indirect(u("lu" + tb, 16)), F.Copy, 78 + GA * 256, ["MT"] + LU, ["lg"])
+        ts(f("ls" + tb, 16), i("l" + tb, 16), 1.0 / SC, None, A.mult, None, 16, LL, ["ls" + tb])
+        act(f("lb", 256), f("ls" + tb, 16).indirect(u("Boff", 16)), F.Identity, 78 + GA * 256, ["ls" + tb, "Boff"], ["lb"], bias=OFFS)
+        mm(T.PL[:, 0:256], b("ID", 128), b("C3", 256), True, False, 256, ["ID", "C3"], ["PL"])
+        mm(T.PL[:, 0:256], b("B0", 128), b(nln, 256), False, False, 256, ["B0", nln], ["PL"])
+        mm(T.PL[:, 0:256], b("Ba", 128), b("lg", 256), False, True, 256, ["Ba", "lg"], ["PL"])
+        tt(b("El", 256), T.PL[:, 0:256], f("lb", 256), A.is_equal, 256, ["PL", "lb"], ["El"], 1.0)
+        scan(b("Fl", 256), b("R0", 256), b("El", 256), A.mult, A.max, 256, ["R0", "El"], ["Fl"], 0.5)
+        tt(f("Gl", 16), b("Fl", 256, 15, 256, 16), f("ls" + tb, 16), A.max, 16, ["Fl", "ls" + tb], ["Gl"])
+        ts(u("no", 32, 0, 32, 2), f("Gl", 16), SC, f("dumL", 1), A.mult, A.min, 16, ["Gl", "dumL"], ["no"])
+        tt(f("dn", 256), T.DL[:, 256 * t:256 * t + 256], f("nn", 256), A.subtract, 256, DLT + ["nn"], ["dn"])
+        box, land = T["box%d" % t], T["land%d" % t]
+        back = lambda c, a: slice(a + BW * (c // N) + c % N, a + BW * (c // N) + BW, N)
+        for h in H:
+            tbh, a0, sh, K = "b%d%d" % (t, h), 16 * BW * h, str(h), "K%d" % h
+            sm = T.SM[:, BW * h:BW * h + BW]
+            c16 = lambda fn, name: fn(name, 16, N * h, N * h + N)
+            fp = lambda name: f(name, 256, BW * h, BW * h + BW)
+            mm(sm, b("ID", 128), b("MK", BW), True, False, BW, ["ID", "MK"], ["SM"])
+            mm(sm, b("B0l", 128), part(nlt, h), False, False, BW, ["B0l", nlt], ["SM"])
+            pick(tbh, N, K, "jB")
+            tg(part("y2n", h), T.MN[:, a0:a0 + 16 * BW].indirect(u("ku" + tbh, N)), part("y1T", h), A.subtract,
+               60 + GA * BW, toks("MN", a0) + ["ku" + tbh, "y1T"], ["y2n" + sh])
+            mm(sm, b("B1n", 128), part("y2n", h), False, True, BW, ["B1n", "y2n" + sh], ["SM"])
+            scan(fp("SR"), b("R0", 256, 0, BW), sm, A.mult, A.max, BW, ["R0", "SM"], ["SR" + sh])
+            tt(fp("K2"), f("IDX2", 256, 0, BW), T[K][:, 0:BW], A.subtract, BW, ["IDX2", K], ["K2" + sh], 1.0)
+            scan(fp("R2"), f("RB", 256, 0, BW), fp("K2"), A.add, A.min, BW, ["RB", "K2" + sh], ["R2" + sh])
+            cp(c16(i, "k2"), f("R2", 256, BW * h + 15, BW * h + BW, 16), N, ["R2" + sh], ["k2" + sh])
+            ts(c16(i, "k3"), c16(i, "k2"), 15, None, A.bitwise_and, None, N, ["k2" + sh], ["k3" + sh])
+            cp(c16(u, "k4"), c16(i, "k3"), N, ["k3" + sh], ["k4" + sh])
+            act(part("kg", h), f("seed", 64).indirect(c16(u, "k4")), F.Copy, 78 + GA * BW, ["seed", "k4" + sh], ["kg" + sh])
+            for c in range(N * h, N * h + N):
+                mm(T.PL[:, back(c, 256)], b("B2", 128), b("kg", 256, 16 * c, 16 * c + 16), True, True, 16, ["B2", "kg" + sh], ["PL"])
+            pl = T.PL[:, BW * h:BW * h + BW]
+            ts(pl, T.PL[:, 256 + BW * h:256 + BW * h + BW], f("j32", 1), None, A.is_equal, None, BW, ["PL", "j32"], ["PL"])
+            tt(fp("td"), pl, fp("dn"), A.mult, BW, ["PL", "dn"], ["td" + sh], 1.0)
+            for c in range(N * h + N - 1, N * h - 1, -1):
+                tg(T.OC[:, 0:2064].indirect(u("no", 32, 2 * c, 2 * c + 1)), f("nn", 256, 16 * c, 16 * c + 16), f("td", 256, 16 * c, 16 * c + 16),
+                   A.add, 60 + SCA * 16, ["no", "nn", "td" + sh], ["OC"] + (OCP if t == 0 and c == 15 else []))
+        ts(b("rdy", 16), f("SR", 256, 15, 256, 16), f("th", 1), None, A.is_ge, None, 16, ["SR%d" % h for h in H] + ["th"], ["rdy"])
+        scan(b("Pp", 16), b("RN", 16), b("rdy", 16), A.mult, A.add, 16, ["RN", "rdy"], ["Pp"])
+        end = lambda x: b("Pp", 16, N * x + N - 1, N * x + N)
+        for h in H:
+            for x in range(h + 1):
+                mm(T.SM[:, 256 + h:257 + h], b("TRI" if x == h else "B1", 128), end(x), x == 0, x == h, 1, ["TRI", "B1", "Pp"], ["SM"])
+        for x in range(NH):
+            mm(T.SM[:, 264:265], b("B1", 128), end(x), x == 0, x == NH - 1, 1, ["B1", "Pp"], ["SM"])
+        ts(f("nr", 16), b("rdy", 16), 0.0, None, A.is_equal, None, 16, ["rdy"], ["nr"])
+        tt(f("nrD", 16), f("nr", 16), f("DD", 16), A.mult, 16, ["nr", "DD"], ["nrD"])
+        for h in H:
+            ts(f("a1", 16, N * h, N * h + N), b("Pp", 16, N * h, N * h + N), T.SM[:, 256 + h:257 + h], -1.0, A.add, A.add, N, ["Pp", "SM"], ["a1%d" % h])
+        tt(f("a2", 16), f("a1", 16), f("nrD", 16), A.max, 16, ["a1%d" % h for h in H] + ["nrD"], ["a2"])
+        cp(u("so", 16), f("a2", 16), 16, ["a2"], ["so"])
+        ts(box[:, 8:9], T.SM[:, 264:265], 64.0, None, A.min, None, 1, ["SM"], ["bc%d" % t])
+        op("V", lambda box=box: V.tensor_copy(box[:, 16:528].indirect(u("so", 16)), b("y2n", 256)), 60 + SCA * 256,
+           ["so"] + ["y2n%d" % h for h in H], ["box%d" % t])
+        dst = dst_of(t)
+        rid, pid, _ = topo.addr(dst)
+        m = 0
+        for e in topo.engines(core, dst)[0::2][:NENG]:
+            m |= 1 << e
+        op("G", lambda box=box, land=land, t=t, pid=pid, rid=rid, m=m: g.remote_dma(land[:, 8:80], box[:, 8:80], T.sem["arr%d" % t], T.sem.sent, pid, rid, m),
+           300, ["box%d" % t, "bc%d" % t], ["land%d" % t], lat=2500, dma="arr%d" % t)
+        if t + 2 < S:
+            rep0(t + 2)
+        for h in H:
+            mark("b%d%d" % (t, h), N, "MG", 16 * BW * h, part(nlt, h), nlt, part("agb", h), str(h))
+        if t == S - 1:
+            dma("S", T.yo[:], T.OC[:, 0:2048], ["OC"], ["yo"], 5000)
+        mm(T.X3[:, 256:512], b("ID", 128), b("OF", 256), True, False, 256, ["ID", "OF"], ["X3"])
+        mm(T.X3[:, 256:512], b("B0n", 128), b(nln, 256), False, False, 256, ["B0n", nln], ["X3"])
+        for c in range(16):
+            mm(T.X3[:, back(c, 256)], b("Ba", 128), b("agb", 256, 16 * c, 16 * c + 16), False, c == 15, 16, ["Ba", "agb%d" % (c // N)], ["X3"])
+        for x in range(2):
+            ya = T.YA[:, 512 * t + 256 * x:512 * t + 256 * x + 256]
+            if PAR["YA"][x] == "A":
+                act(f("yat", 256), T.X3[:, 256 * x:256 * x + 256], F.Relu, 78 + 256, ["X3"], ["yat"], bias=1.0, scale=SC)
+                act(ya, f("yat", 256), F.Identity, 78 + 256, ["yat"], ["YA%d%d" % (t, x)], bias=-1.0)
+            else:
+                ts(ya, T.X3[:, 256 * x:256 * x + 256], SC, -1.0, A.mult, A.max, 256, ["X3"], ["YA%d%d" % (t, x)])
+        dma("S", T.ya[:, 512 * t:512 * t + 512], T.YA[0:128:16, 512 * t:512 * t + 512], ["YA%d0" % t, "YA%d1" % t], ["ya%d" % t], 2000)
+        lt = ["land%d" % t]
+        mm(T.PU[:, 0:64], b("ID", 128), b("MK", BW, 0, 64), True, False, 64, ["ID", "MK"], ["PU"])
+        mm(T.PU[:, 0:64], b("Bwn", 128), land[:, 16:80], False, True, 64, ["Bwn"] + lt, ["PU"])
+        scan(f("UR", 64), b("R0", 256, 0, 64), T.PU[:, 0:64], A.mult, A.max, 64, ["R0", "PU"], ["UR"])
+        square(tr, f("UR", 64, 15, 64, 16), "UR", 4)
+        yr = ["YRr%d" % k for k in range(16)]
+        for k in range(16):
+            rep(PAR["REPR"][k], T.YRr[:, k:1024:16], land[:, 16:80], -1.0, 64, lt, [yr[k]])
+        place(tr, 4, "A%d" % t, t, "cr", tr, 0)
+        ts(b("NR", 64), f("SLOT", 64), land[:, 8:9], None, A.is_ge, None, 64, ["SLOT"] + lt, ["NR"])
+        if t + 1 < S:
+            an = "A%d" % (t + 1)
+            mm(T.PU[:, 64:65], b("ON", 128), land[:, 8:9], True, True, 1, ["ON"] + lt, ["PU"])
+            cp(i("ai", 1), T.PU[:, 64:65], 1, ["PU"], ["ai"])
+            ts(i("aj", 1), i("ai", 1), 63, None, A.bitwise_and, None, 1, ["ai"], ["aj"])
+            ts(f(an, 1), i("aj", 1), -0.375, None, A.add, None, 1, ["aj"], [an])
+            place0(t + 1)
+        main("cr", 0, 4, "Kr", "MNr", "MGr", "YRr", 0, yr, PAR["CHR"], 0, PAR["LAGR"])
+        pick(tr, 4, "Kr", "j64")
+        mark(tr, 4, "MGr", 0, b("NR", 64), "NR", b("agr", 64), "r")
+    dma("G", T.ym[:], T.MT[0:128:16, 0:4096], ["MT"], ["ym"], 2500)
+    return ops
+
+
+def graph(ops):
+    lastw, readers, bank = {}, {}, {}
+    deps = []
+    for k, o in enumerate(ops):
+        d = set()
+        for x in o["r"] + o["w"]:
+            if x in lastw and x[0] != "~":
+                d.add(lastw[x])
+        for x in o["w"]:
+            d.update(readers.get(x, ()))
+        d = {a: not (ops[a]["e"] == "P" and o["e"] == "P") for a in d}
+        for x in sorted(set(o["r"] + o["w"])):
+            if x in BANKS or x[0] == "~":
+                if x in bank:
+                    d.setdefault(bank[x], ops[bank[x]]["e"] != o["e"])
+                bank[x] = k
+        for x in o["r"]:
+            readers.setdefault(x, []).append(k)
+        for x in o["w"]:
+            lastw[x] = k
+            readers[x] = []
+        d.pop(k, None)
+        deps.append(d)
+    return deps
+
+
+def place_all(ops, pred, key, first):
+    start = [0.0] * len(ops)
+    busy = {e: [] for e in "VAPGS"}
+    for k in sorted(range(len(ops)), key=key):
+        c = ops[k]["c"]
+        s = max([first[k]] + [start[a] + ops[a]["c"] + d for a, d in pred[k]])
+        iv = busy[ops[k]["e"]]
+        lo, hi = 0, len(iv)
+        while lo < hi:
+            mid = (lo + hi) // 2
+            if iv[mid][1] <= s:
+                lo = mid + 1
+            else:
+                hi = mid
+        while lo < len(iv) and iv[lo][0] < s + c:
+            s = max(s, iv[lo][1])
+            lo += 1
+        iv.insert(lo, (s, s + c))
+        start[k] = s
+    return start
+
+
+def order_key(pred, val):
+    val = list(val)
+    for k in range(len(val)):
+        for a, _ in pred[k]:
+            if val[k] < val[a]:
+                val[k] = val[a]
+    return lambda k: (val[k], k)
+
+
+def plan(ops, deps):
+    n = len(ops)
+    pred = [[(a, (ops[a]["lat"] + PAR["SIG"]) if w else 0.0) for a, w in deps[k].items()] for k in range(n)]
+    succ = [[] for _ in range(n)]
+    for k in range(n):
+        for a, d in pred[k]:
+            succ[a].append((k, d))
+    lat = [o["lat"] for o in ops]
+    zero = [0.0] * n
+    back = [0.0] * n
+    for k in range(n - 1, -1, -1):
+        back[k] = max([lat[k]] + [back[x] + ops[x]["c"] + d for x, d in succ[k]])
+    seed = [PAR["SEED"]]
+
+    def rnd():
+        seed[0] = (seed[0] * 1103515245 + 12345) % 2147483648
+        return seed[0] / 2147483648.0
+
+    def fwd(val):
+        fw = place_all(ops, pred, order_key(pred, val), zero)
+        return max(fw[k] + ops[k]["c"] + lat[k] for k in range(n)), fw
+
+    def again(fw):
+        bw = place_all(ops, succ, lambda k: (-(fw[k] + ops[k]["c"]), -k), lat)
+        return fwd([-(bw[k] + ops[k]["c"]) for k in range(n)])
+
+    best = fwd([-(back[k] + ops[k]["c"]) for k in range(n)])
+    names = [o["w"][0].rstrip("0123456789_") for o in ops]
+    for _ in range(PAR["ROUNDS"]):
+        t0, wd, amp = rnd() * best[0], 2000 + 10000 * rnd(), PAR["NOISE"] * (0.2 + 3 * rnd() ** 2)
+        sh = {}
+        val = []
+        for k in range(n):
+            s = best[1][k]
+            if t0 <= s < t0 + wd:
+                if names[k] not in sh:
+                    sh[names[k]] = amp * (rnd() - 0.5) if rnd() < 0.4 else 0.0
+                s += sh[names[k]]
+            val.append(s)
+        c = fwd(val)
+        if c[0] < best[0] + 600:
+            c2 = again(c[1])
+            if c2[0] < c[0]:
+                c = c2
+        if c[0] <= best[0]:
+            best = c
+    return best
+
+
+PLAN = {}
+
+
+def rank_program(g, core, T, topo):
+    rank = T.rank_of(core)
+    if rank is None:
+        return
+    n = len(T.cores)
+    ops = build(g, T, lambda t: T.cores[(rank + 1 + t % (n - 1)) % n], topo, core)
+    deps = graph(ops)
+    if "start" not in PLAN:
+        PLAN["start"] = plan(ops, deps)[1]
+    start = PLAN["start"]
+    order = sorted(range(len(ops)), key=lambda k: (start[k], k))
+    need = set(a for d in deps for a, w in d.items() if w)
+    queue = {"V": g.vector, "A": g.scalar, "P": g.tensor, "G": g, "S": g.sync}
+    total = {}
+    for o in ops:
+        if o["dma"] is not None:
+            total[o["dma"]] = total.get(o["dma"], 0) + (NENG if o["dma"].startswith("arr") else 16)
+    count = {"cV": 0, "cA": 0, "cP": 0, "cG": 0}
+    sig = {}
+    known = {e: {} for e in queue}
+    clock = {}
+    for k in order:
+        o = ops[k]
+        e = o["e"]
+        kn = known[e]
+        want = {}
+        for a, w in deps[k].items():
+            if w:
+                s, v = sig[a]
+                if v > want.get(s, (0, None))[0]:
+                    want[s] = (v, a)
+        for s, (v, a) in sorted(want.items(), key=lambda z: -start[z[1][1]]):
+            if kn.get(s, 0) < v:
+                queue[e].wait_ge(T.sem[s], v)
+                kn[s] = v
+                for s2, v2 in clock[a].items():
+                    if kn.get(s2, 0) < v2:
+                        kn[s2] = v2
+        ins = o["fn"]()
+        remote = o["dma"] is not None and o["dma"].startswith("arr")
+        clock[k] = {} if remote else dict(kn)
+        if o["dma"] is not None:
+            if not remote:
+                ins.then_inc(T.sem[o["dma"]], 16)
+            sig[k] = (o["dma"], total[o["dma"]])
+        elif k in need:
+            s = "c" + e
+            count[s] += 1
+            ins.then_inc(T.sem[s], 1)
+            sig[k] = (s, count[s])
+    for s, v in list(count.items()) + list(total.items()):
+        if known["G"].get(s, 0) < v:
+            g.wait_ge(T.sem[s], v)
+    g.wait_ge(T.sem.sent, S * NENG)

@@ -52,12 +52,12 @@ PAR = {
     "NH": 2,
     "CH": [[4, 4, 4, 4], [4, 4, 4, 2, 2]],
     "CHR": [6, 6, 2, 2],
-    "HELP": {},
+    "HELP": {(1, 0, 1): 4, (2, 0, 1): 4},
     "LAG": {(0, 0, 0): 4, (0, 0, 1): 8, (1, 0, 1): 8, (2, 0, 1): 8, (0, 1, 1): 8},
     "LAGR": 0,
-    "REP0": "VVVVVVVVVVAAAGGG", "REP": "VVVVVVVVVVVVVVVV", "REPR": "VVVVVVVVVVAAAAAA",
-    "YA": "VV", "MTA": 6,
-    "SIG": 110.0, "GA": 1.56, "SCA": 3.8, "PE": 0.42, "ROUNDS": 1200, "SEED": 1, "NOISE": 1500.0,
+    "REP0": "VVVVVVVVVVAAAGGG", "REP": "VVVVVVVVVVAAAAAA", "REPR": "VVVVVVVVAAAAAAAA",
+    "YA": "AA", "MTA": 6,
+    "SIG": 240.0, "GA": 1.56, "SCA": 3.8, "PE": 0.42, "ROUNDS": 1200, "SEED": 1, "NOISE": 1500.0,
 }
 NENG = 4
 

@@ -7,8 +7,8 @@ W, L, S = 4096, 2048, 3
 SCRATCH = {
     "X": ("sbuf", [128, 4096], "bfloat16"),
     "OCI": ("sbuf", [128, 2048], "int32"),
-    "OC": ("sbuf", [128, 2064], "float32"),
-    "MT": ("sbuf", [128, 4112], "float32"),
+    "OC": ("sbuf", [128, 2080], "float32"),
+    "MT": ("sbuf", [128, 4128], "float32"),
     "MN": ("sbuf", [128, 4096], "bfloat16"),
     "MG": ("sbuf", [128, 4096], "bfloat16"),
     "MNr": ("sbuf", [128, 1024], "bfloat16"),
@@ -55,11 +55,11 @@ PAR = {
     "HELP": {(1, 0, 1): 4, (2, 0, 1): 4},
     "LAG": {(0, 0, 0): 4, (0, 0, 1): 8, (1, 0, 1): 8, (2, 0, 1): 8, (0, 1, 1): 8},
     "LAGR": 0,
-    "REP0": "VVVVVVVVVVAAAGGG", "REP": "VVVVVVVVVVAAAAAA", "REPR": "VVVVVVVVAAAAAAAA",
-    "YA": "AA", "MTA": 6,
-    "SIG": 240.0, "GA": 1.56, "SCA": 3.8, "PE": 0.42, "ROUNDS": 1200, "SEED": 1, "NOISE": 1500.0,
+    "REP0": "VVVVVVVVVVAAAGGG", "REP": "VVVVVVVVVVVVAAAA", "REPR": "VVVVVVVVAAAAAAAA",
+    "YA": "AV", "MTA": 6,
+    "SIG": 220.0, "GA": 1.56, "SCA": 3.8, "PE": 0.42, "ROUNDS": 2400, "SEED": 1, "NOISE": 1500.0,
 }
-NENG = 4
+NENG = 8
 
 
 def build(g, T, dst_of, topo, core):
@@ -186,8 +186,9 @@ def build(g, T, dst_of, topo, core):
     acol("j64", "jf", 64.0, 0.0)
     acol("jB", "jf", float(BW), 0.0)
     acol("j32", "jf", 1.0, 32.0)
-    acol("dumM", "jf", 1.0, 4096.0)
-    acol("dumL", "jf", 1.0, 2048.0)
+    for e in range(2):
+        acol("dumM%d" % e, "jf", 1.0, 4096.0 + 16 * e)
+        acol("dumL%d" % e, "jf", 1.0, 2048.0 + 16 * e)
     acol("r0m", "r0", -65536.0, 0.0)
     acol("r0l", "r0", -4096.0, 0.0)
     acol("r0n", "r0", -1.0, 0.0)
@@ -216,18 +217,31 @@ def build(g, T, dst_of, topo, core):
     op("G", lambda: g.affine_select(b("TRI", 128), b("B1", 128), [[1, 128]], A.is_gt, 0.0, 0, -1), 456, ["B1"], ["TRI"])
     ms(b("ON", 128), 1.0 / 16, 64, ["ON"])
     ms(b("OF", 256), -OFFS, 128, ["OF"])
-    ts(b("eq", 256), f("II", 256), f("jf", 1), None, A.is_equal, None, 256, ["II", "jf"], ["eq"])
-    ts(b("gt", 256), f("II", 256), f("jf", 1), 4.0, A.is_gt, A.mult, 256, ["II", "jf"], ["gt"])
-    act(b("CC", 512, 0, 256), b("eq", 256), F.Identity, 334, ["eq"], ["C1"], bias=-4.0, scale=4.0 - OFFS)
-    act(b("CC", 512, 256, 512), b("gt", 256), F.Identity, 334, ["gt"], ["C2"], bias=4.0, scale=-(4.0 + OFFS) / 4.0)
-    act(b("MK", BW), b("eq", 256, 0, BW), F.Identity, 78 + BW, ["eq"], ["MK"], bias=-BIG, scale=BIG)
-    tt(b("C3", 256), b("gt", 256), b("eq", 256), A.subtract, 256, ["gt", "eq"], ["C3"])
+    iota(f("IJ", 384, 0, 256), [[0, 8], [1, 32]], 256, ["IJa"])
+    iota(f("IJ", 384, 256, 384), [[0, 8], [1, 16]], 128, ["IJb"])
+    op("G", lambda: g.iota(f("IL", 384, 0, 256), [[0, 8], [1, 32]], -16, 0, allow_small_or_imprecise_dtypes=True), 662, [], ["ILa"])
+    iota(f("IL", 384, 256, 384), [[0, 8], [1, 16]], 128, ["ILb"])
+    op("G", lambda: g.iota(f("IB", 24, 0, 16), [[2, 8], [0, 2]], 1, 0, allow_small_or_imprecise_dtypes=True), 182, [], ["IBa"])
+    iota(f("IB", 24, 16, 24), [[2, 8]], 8, ["IBb"])
+    ts(b("eq", 256), f("IJ", 384, 128, 384), f("jf", 1), None, A.is_equal, None, 256, ["IJa", "IJb", "jf"], ["eq"])
+    ts(b("gt", 192), f("IJ", 384, 128, 320), f("jf", 1), 4.0, A.is_gt, A.mult, 192, ["IJa", "IJb", "jf"], ["gt"])
+    for bw in (128, 64):
+        w = bw + bw // 2
+        act(b("CC%d" % bw, 2 * w, 0, w), b("eq", 256, 128 - bw, 128 - bw + w), F.Identity, 78 + w, ["eq"], ["CC%da" % bw], bias=-4.0, scale=4.0 - OFFS)
+        act(b("CC%d" % bw, 2 * w, w, 2 * w), b("gt", 192, 128 - bw, 128 - bw + w), F.Identity, 78 + w, ["gt"], ["CC%db" % bw], bias=4.0, scale=-(4.0 + OFFS) / 4.0)
+    act(b("MK", BW), b("eq", 256, 128, 256), F.Identity, 78 + BW, ["eq"], ["MK"], bias=-BIG, scale=BIG)
+    act(b("RL", 384), f("IJ", 384), F.Sign, 462, ["IJa", "IJb"], ["RL"])
+    act(b("RX", 192), f("IJ", 384, 128, 320), F.Sign, 270, ["IJa", "IJb"], ["RX"])
+    ts(b("eqL", 384), f("IL", 384), f("jf", 1), None, A.is_equal, None, 384, ["ILa", "ILb", "jf"], ["eqL"])
+    ts(b("gtL", 384), f("IL", 384), f("jf", 1), 4.0, A.is_gt, A.mult, 384, ["ILa", "ILb", "jf"], ["gtL"])
+    tt(b("C3", 384), b("gtL", 384), b("eqL", 384), A.subtract, 384, ["gtL", "eqL"], ["C3"])
     act(b("R0", 256), f("II", 256), F.Sign, 334, ["II"], ["R0"])
     act(f("RB", 256), b("R0", 256), F.Identity, 334, ["R0"], ["RB"], bias=8388608.0, scale=-8388608.0)
     ts(u("T0", 16), f("IT0", 16), f("jl16", 1), f("jhf", 1), A.add, A.add, 16, ["IT0", "jl16", "jhf"], ["T0"])
     ts(u("T1", 16), f("IT1", 16), f("jN", 1), None, A.add, None, 16, ["IT1", "jN"], ["T1"])
-    cp(u("Boff", 16), f("I144", 144, 0, 16), 16, ["I144"], ["Boff"])
-    ts(f("DD", 16), f("IT1", 16), f("jN", 1), 256.0, A.add, A.add, 16, ["IT1", "jN"], ["DD"])
+    cp(u("Boff", 24), f("IB", 24), 24, ["IBa", "IBb"], ["Boff"])
+    ts(f("D0", 16), f("IT1", 16), f("jN", 1), -256.0, A.add, A.add, 16, ["IT1", "jN"], ["D0"])
+    act(f("DD", 16), f("D0", 16), F.Copy, 94, ["D0"], ["DD"], scale=-1.0)
     ts(b("RN", 16), f("IN", 16), 0.0, None, A.not_equal, None, 16, ["IN"], ["RN"])
     for t in range(S):
         ms(T["box%d" % t][:, 0:80], 0.0, 40, ["box%d" % t, "bc%d" % t])
@@ -334,22 +348,33 @@ def build(g, T, dst_of, topo, core):
     def mark(tag, n, mg, a0, nl, nlt, ag, s):
         bw = 16 * n
         at = "ag" + tag[0] + s
-        x1, x2 = T.XX[:, 0:bw], T.XX[:, bw:2 * bw]
-        mm(T.XX[:, 0:2 * bw], b("ID", 128), b("CC", 512, 256 - bw, 256 + bw), True, False, 2 * bw, ["ID", "C1", "C2"], ["XX"])
-        for x in (x1, x2):
-            mm(x, b("B0", 128), nl, False, False, bw, ["B0", nlt], ["XX"])
-        act(ag, T[mg][:, a0:a0 + 16 * bw].indirect(u("ku" + tag, n)), F.Copy, 78 + GA * bw, toks(mg, a0) + ["ku" + tag], [at])
-        mm(x1, b("Ba", 128), ag, False, False, bw, ["Ba", at], ["XX"])
-        mm(x2, b("Ba", 128), ag, False, True, bw, ["Ba", at], ["XX"])
-        act(f("agf" + s, bw), ag, F.Silu, 78 + bw, [at, "nr0", "r0z"], ["agf" + s], bias=f("r0z", 1), scale=f("nr0", 1))
-        scan(f("H" + s, bw), b("R0", 256, 0, bw), x1, A.mult, A.max, bw, ["R0", "XX"], ["H" + s])
-        tt(b("E" + s, bw), x2, f("H" + s, bw), A.is_equal, bw, ["XX", "H" + s], ["E" + s], 1.0)
-        scan(b("Fs" + s, bw), b("R0", 256, 0, bw), b("E" + s, bw), A.mult, A.max, bw, ["R0", "E" + s], ["Fs" + s], 0.5)
-        tt(f("G" + tag, n), b("Fs" + s, bw, 15, bw, 16), f("H" + s, bw, 15, bw, 16), A.max, n, ["Fs" + s, "H" + s], ["G" + tag])
-        ts(u("mo" + tag, 2 * n, 0, 2 * n, 2), f("G" + tag, n), SC, f("dumM", 1), A.mult, A.min, n, ["G" + tag, "dumM"], ["mo" + tag])
-        for c in range(n):
-            act(T.MT[:, 0:4112].indirect(u("mo" + tag, 2 * n, 2 * c, 2 * c + 1)), f("agf" + s, bw, 16 * c, 16 * c + 16), F.Silu,
-                78 + SCA * 16, ["mo" + tag, "agf" + s], ["MT"])
+        w = bw + bw // 2
+        cc = "CC%d" % bw
+        rx = b("RX", 192, 128 - bw, 128 - bw + w)
+        x1, x2 = T.XX[:, 0:w], T.XX[:, w:2 * w]
+
+        def spread(mat, src, tok, last):
+            for x in (0, w):
+                mm(T.XX[:, x:x + bw], b(mat, 128), src(0, bw), False, False, bw, [mat, tok], ["XX"])
+                for c in range(n // 2):
+                    mm(T.XX[:, x + bw + 16 * c:x + bw + 16 * c + 16], b(mat, 128), src(32 * c + 16, 32 * c + 32), False,
+                       last and x == w and c == n // 2 - 1, 16, [mat, tok], ["XX"])
+
+        mm(T.XX[:, 0:2 * w], b("ID", 128), b(cc, 2 * w), True, False, 2 * w, ["ID", cc + "a", cc + "b"], ["XX"])
+        spread("B0", nl, nlt, False)
+        act(ag(0, bw), T[mg][:, a0:a0 + 16 * bw].indirect(u("ku" + tag, n)), F.Copy, 78 + GA * bw, toks(mg, a0) + ["ku" + tag], [at])
+        spread("Ba", ag, at, True)
+        act(f("agf" + s, bw), ag(0, bw), F.Silu, 78 + bw, [at, "nr0", "r0z"], ["agf" + s], bias=f("r0z", 1), scale=f("nr0", 1))
+        scan(f("H" + s, w), rx, x1, A.mult, A.max, w, ["RX", "XX"], ["H" + s])
+        tt(b("E" + s, w), x2, f("H" + s, w), A.is_equal, w, ["XX", "H" + s], ["E" + s], 1.0)
+        scan(b("Fs" + s, w), rx, b("E" + s, w), A.mult, A.max, w, ["RX", "E" + s], ["Fs" + s], 0.5)
+        for e, (lo, hi, st) in enumerate(((31, bw, 32), (bw + 15, w, 16))):
+            gt_ = "G%d" % e + tag
+            tt(f(gt_, n // 2), b("Fs" + s, w, lo, hi, st), f("H" + s, w, lo, hi, st), A.max, n, ["Fs" + s, "H" + s], [gt_])
+            ts(u("mo" + tag, n, e, n, 2), f(gt_, n // 2), SC, f("dumM%d" % e, 1), A.mult, A.min, n, [gt_, "dumM%d" % e], ["mo%d" % e + tag])
+        for c in range(n // 2):
+            act(T.MT[:, 0:4128].indirect(u("mo" + tag, n, 2 * c, 2 * c + 2)), f("agf" + s, bw, 32 * c, 32 * c + 32), F.Silu,
+                78 + SCA * 32, ["mo0" + tag, "mo1" + tag, "agf" + s], ["MT"])
 
     def lanes0(ts_):
         def rhs(t, h, j):
@@ -371,6 +396,7 @@ def build(g, T, dst_of, topo, core):
         nln, nlt = "NL%d" % t, "NT%d" % t
         H = list(range(NH - 1, -1, -1))
         part = lambda name, h: b(name, 256, BW * h, BW * h + BW)
+        sub = lambda name, h: (lambda x, y: b(name, 256, BW * h + x, BW * h + y))
         act(b(nln, 256), T.MT[:, B:B + 256], F.Relu, 78 + 256, ["MT"], [nln], bias=1.0, scale=-2.0)
         act(b(nlt, 256), T.MT[:, B:B + 256].indirect(u("T1", 16)), F.Relu, 78 + GA * 256, ["MT", "T1"], [nlt], bias=1.0, scale=-2.0)
         for h in H:
@@ -382,7 +408,7 @@ def build(g, T, dst_of, topo, core):
             pick(ta, N, "K%d" % h, "jB")
             tg(part("y1n", h), T.MN[:, a0:a0 + 16 * BW].indirect(u("ku" + ta, N)), T.X[:, B + BW * h:B + BW * h + BW], A.subtract,
                60 + GA * BW, toks("MN", a0) + ["ku" + ta, "Xl"], ["y1n%d" % h])
-            mark(ta, N, "MG", a0, part(nln, h), nln, part("aga", h), str(h))
+            mark(ta, N, "MG", a0, sub(nln, h), nln, sub("aga", h), str(h))
             u_part(tb, [lambda j: b("y1n", 256, BW * h + j, BW * h + BW, 16)], ["y1n%d" % h], "Zn", N)
             yrt[h] = ["YRh%d_%d" % (h, k) for k in range(16)]
             for k in range(16):
@@ -401,14 +427,17 @@ def build(g, T, dst_of, topo, core):
         act(f("nn", 256), T.OC[:, 0:2048].indirect(u("lu" + tb, 16)), F.Copy, 78 + GA * 256, ["OC"] + OCP + LU, ["nn"])
         act(b("lg", 256), T.MT[:, 0:2048].indirect(u("lu" + tb, 16)), F.Copy, 78 + GA * 256, ["MT"] + LU, ["lg"])
         ts(f("ls" + tb, 16), i("l" + tb, 16), 1.0 / SC, None, A.mult, None, 16, LL, ["ls" + tb])
-        act(f("lb", 256), f("ls" + tb, 16).indirect(u("Boff", 16)), F.Identity, 78 + GA * 256, ["ls" + tb, "Boff"], ["lb"], bias=OFFS)
-        mm(T.PL[:, 0:256], b("ID", 128), b("C3", 256), True, False, 256, ["ID", "C3"], ["PL"])
-        mm(T.PL[:, 0:256], b("B0", 128), b(nln, 256), False, False, 256, ["B0", nln], ["PL"])
-        mm(T.PL[:, 0:256], b("Ba", 128), b("lg", 256), False, True, 256, ["Ba", "lg"], ["PL"])
-        tt(b("El", 256), T.PL[:, 0:256], f("lb", 256), A.is_equal, 256, ["PL", "lb"], ["El"], 1.0)
-        scan(b("Fl", 256), b("R0", 256), b("El", 256), A.mult, A.max, 256, ["R0", "El"], ["Fl"], 0.5)
-        tt(f("Gl", 16), b("Fl", 256, 15, 256, 16), f("ls" + tb, 16), A.max, 16, ["Fl", "ls" + tb], ["Gl"])
-        ts(u("no", 32, 0, 32, 2), f("Gl", 16), SC, f("dumL", 1), A.mult, A.min, 16, ["Gl", "dumL"], ["no"])
+        act(f("lb", 384), f("ls" + tb, 16).indirect(u("Boff", 24)), F.Identity, 78 + GA * 384, ["ls" + tb, "Boff"], ["lb"], bias=OFFS)
+        mm(T.PL[:, 0:384], b("ID", 128), b("C3", 384), True, False, 384, ["ID", "C3"], ["PL"])
+        for mat, src in (("B0", nln), ("Ba", "lg")):
+            mm(T.PL[:, 0:256], b(mat, 128), b(src, 256), False, False, 256, [mat, src], ["PL"])
+            for c in range(8):
+                mm(T.PL[:, 256 + 16 * c:272 + 16 * c], b(mat, 128), b(src, 256, 32 * c, 32 * c + 16), False, mat == "Ba" and c == 7, 16, [mat, src], ["PL"])
+        tt(b("El", 384), T.PL[:, 0:384], f("lb", 384), A.is_equal, 384, ["PL", "lb"], ["El"], 1.0)
+        scan(b("Fl", 384), b("RL", 384), b("El", 384), A.mult, A.max, 384, ["RL", "El"], ["Fl"], 0.5)
+        for e, (lo, hi, st) in enumerate(((271, 384, 16), (31, 256, 32))):
+            tt(f("Gl%d" % e, 8), b("Fl", 384, lo, hi, st), f("ls" + tb, 16, e, 16, 2), A.max, 8, ["Fl", "ls" + tb], ["Gl%d" % e])
+            ts(u("no", 16, e, 16, 2), f("Gl%d" % e, 8), SC, f("dumL%d" % e, 1), A.mult, A.min, 8, ["Gl%d" % e, "dumL%d" % e], ["no%d" % e])
         tt(f("dn", 256), T.DL[:, 256 * t:256 * t + 256], f("nn", 256), A.subtract, 256, DLT + ["nn"], ["dn"])
         box, land = T["box%d" % t], T["land%d" % t]
         back = lambda c, a: slice(a + BW * (c // N) + c % N, a + BW * (c // N) + BW, N)
@@ -435,9 +464,9 @@ def build(g, T, dst_of, topo, core):
             pl = T.PL[:, BW * h:BW * h + BW]
             ts(pl, T.PL[:, 256 + BW * h:256 + BW * h + BW], f("j32", 1), None, A.is_equal, None, BW, ["PL", "j32"], ["PL"])
             tt(fp("td"), pl, fp("dn"), A.mult, BW, ["PL", "dn"], ["td" + sh], 1.0)
-            for c in range(N * h + N - 1, N * h - 1, -1):
-                tg(T.OC[:, 0:2064].indirect(u("no", 32, 2 * c, 2 * c + 1)), f("nn", 256, 16 * c, 16 * c + 16), f("td", 256, 16 * c, 16 * c + 16),
-                   A.add, 60 + SCA * 16, ["no", "nn", "td" + sh], ["OC"] + (OCP if t == 0 and c == 15 else []))
+            for c in range(N * h + N - 2, N * h - 1, -2):
+                tg(T.OC[:, 0:2080].indirect(u("no", 16, c, c + 2)), f("nn", 256, 16 * c, 16 * c + 32), f("td", 256, 16 * c, 16 * c + 32),
+                   A.add, 60 + SCA * 32, ["no0", "no1", "nn", "td" + sh], ["OC"] + (OCP if t == 0 and c == 14 else []))
         ts(b("rdy", 16), f("SR", 256, 15, 256, 16), f("th", 1), None, A.is_ge, None, 16, ["SR%d" % h for h in H] + ["th"], ["rdy"])
         scan(b("Pp", 16), b("RN", 16), b("rdy", 16), A.mult, A.add, 16, ["RN", "rdy"], ["Pp"])
         end = lambda x: b("Pp", 16, N * x + N - 1, N * x + N)
@@ -446,15 +475,14 @@ def build(g, T, dst_of, topo, core):
                 mm(T.SM[:, 256 + h:257 + h], b("TRI" if x == h else "B1", 128), end(x), x == 0, x == h, 1, ["TRI", "B1", "Pp"], ["SM"])
         for x in range(NH):
             mm(T.SM[:, 264:265], b("B1", 128), end(x), x == 0, x == NH - 1, 1, ["B1", "Pp"], ["SM"])
-        ts(f("nr", 16), b("rdy", 16), 0.0, None, A.is_equal, None, 16, ["rdy"], ["nr"])
+        ts(f("nr", 16), f("SR", 256, 15, 256, 16), f("th", 1), None, A.is_lt, None, 16, ["SR%d" % h for h in H] + ["th"], ["nr"])
         tt(f("nrD", 16), f("nr", 16), f("DD", 16), A.mult, 16, ["nr", "DD"], ["nrD"])
+        tt(f("a1", 16), b("Pp", 16), f("nrD", 16), A.add, 16, ["Pp", "nrD"], ["a1"])
         for h in H:
-            ts(f("a1", 16, N * h, N * h + N), b("Pp", 16, N * h, N * h + N), T.SM[:, 256 + h:257 + h], -1.0, A.add, A.add, N, ["Pp", "SM"], ["a1%d" % h])
-        tt(f("a2", 16), f("a1", 16), f("nrD", 16), A.max, 16, ["a1%d" % h for h in H] + ["nrD"], ["a2"])
-        cp(u("so", 16), f("a2", 16), 16, ["a2"], ["so"])
+            ts(u("so", 16, N * h, N * h + N), f("a1", 16, N * h, N * h + N), T.SM[:, 256 + h:257 + h], -1.0, A.add, A.add, N, ["a1", "SM"], ["so%d" % h])
         ts(box[:, 8:9], T.SM[:, 264:265], 64.0, None, A.min, None, 1, ["SM"], ["bc%d" % t])
-        op("V", lambda box=box: V.tensor_copy(box[:, 16:528].indirect(u("so", 16)), b("y2n", 256)), 60 + SCA * 256,
-           ["so"] + ["y2n%d" % h for h in H], ["box%d" % t])
+        op("V", lambda box=box: V.tensor_copy(box[:, 16:272].indirect(u("so", 16)), b("y2n", 256)), 60 + SCA * 256,
+           ["so%d" % h for h in H] + ["y2n%d" % h for h in H], ["box%d" % t])
         dst = dst_of(t)
         rid, pid, _ = topo.addr(dst)
         m = 0
@@ -465,7 +493,7 @@ def build(g, T, dst_of, topo, core):
         if t + 2 < S:
             rep0(t + 2)
         for h in H:
-            mark("b%d%d" % (t, h), N, "MG", 16 * BW * h, part(nlt, h), nlt, part("agb", h), str(h))
+            mark("b%d%d" % (t, h), N, "MG", 16 * BW * h, sub(nlt, h), nlt, sub("agb", h), str(h))
         if t == S - 1:
             dma("S", T.yo[:], T.OC[:, 0:2048], ["OC"], ["yo"], 5000)
         mm(T.X3[:, 256:512], b("ID", 128), b("OF", 256), True, False, 256, ["ID", "OF"], ["X3"])
@@ -499,7 +527,7 @@ def build(g, T, dst_of, topo, core):
             place0(t + 1)
         main("cr", 0, 4, "Kr", "MNr", "MGr", "YRr", 0, yr, PAR["CHR"], 0, PAR["LAGR"])
         pick(tr, 4, "Kr", "j64")
-        mark(tr, 4, "MGr", 0, b("NR", 64), "NR", b("agr", 64), "r")
+        mark(tr, 4, "MGr", 0, lambda x, y: b("NR", 64, x, y), "NR", lambda x, y: b("agr", 64, x, y), "r")
     dma("G", T.ym[:], T.MT[0:128:16, 0:4096], ["MT"], ["ym"], 2500)
     return ops
 

@@ -8,7 +8,9 @@ SCRATCH = {
     "X": ("sbuf", [128, 4096], "bfloat16"),
     "OCI": ("sbuf", [128, 2048], "int32"),
     "OC": ("sbuf", [128, 2080], "float32"),
-    "MT": ("sbuf", [128, 4128], "float32"),
+    "MT": ("sbuf", [128, 4160], "float32"),
+    "YM": ("sbuf", [128, 4160], "bfloat16"),
+    "DF": ("sbuf", [128, 784], "float32"),
     "MN": ("sbuf", [128, 4096], "bfloat16"),
     "MG": ("sbuf", [128, 4096], "bfloat16"),
     "MNr": ("sbuf", [128, 1024], "bfloat16"),
@@ -18,9 +20,8 @@ SCRATCH = {
     "YR2": ("sbuf", [128, 4096], "bfloat16"),
     "YRh": ("sbuf", [128, 4096], "bfloat16"),
     "YRr": ("sbuf", [128, 1024], "bfloat16"),
-    "DL": ("sbuf", [128, 768], "int32"),
+    "DL": ("sbuf", [128, 784], "int32"),
     "WI": ("sbuf", [128, 8], "int32"),
-    "TI": ("sbuf", [128, 8], "int32"),
     "YA": ("sbuf", [128, 1536], "float32"),
     "box0": ("sbuf", [128, 528], "bfloat16"),
     "box1": ("sbuf", [128, 528], "bfloat16"),
@@ -29,46 +30,53 @@ SCRATCH = {
     "land1": ("sbuf", [128, 80], "bfloat16"),
     "land2": ("sbuf", [128, 80], "bfloat16"),
     "AF": ("sbuf", [128, 8192], "float32"),
-    "AB": ("sbuf", [128, 12288], "bfloat16"),
-    "AI": ("sbuf", [128, 4096], "int32"),
+    "AB": ("sbuf", [128, 14336], "bfloat16"),
+    "AI": ("sbuf", [128, 2048], "int32"),
     "AU": ("sbuf", [128, 4096], "uint16"),
     "K0": ("psum", [128, 512], "float32"),
     "K1": ("psum", [128, 512], "float32"),
-    "Kr": ("psum", [128, 512], "float32"),
+    "X0": ("psum", [128, 512], "float32"),
+    "X1": ("psum", [128, 512], "float32"),
     "PU": ("psum", [128, 512], "float32"),
-    "XX": ("psum", [128, 512], "float32"),
     "X3": ("psum", [128, 512], "float32"),
     "PL": ("psum", [128, 512], "float32"),
     "SM": ("psum", [128, 512], "float32"),
 }
 SEMAPHORES = ["cV", "cA", "cP", "cG", "sent", "arr0", "arr1", "arr2"] + ["d%d" % i for i in range(24)]
 
-BANKS = ("K0", "K1", "Kr", "PU", "XX", "X3", "PL", "SM")
+BANKS = ("K0", "K1", "X0", "X1", "PU", "X3", "PL", "SM")
 SC = 16384.0
-OFFS = 65.0 / 512.0
-Z2 = 1.5498553
-BIG = 1048576.0
+OFFS = 2080.0
+Z2 = 1.28125
+BIG = 2097152.0
+KS = 1.0 / 131072
+AOFF = -10952.390625
 PAR = {
-    "NH": 2,
-    "CH": [[4, 4, 4, 4], [4, 4, 4, 2, 2]],
-    "CHR": [6, 6, 2, 2],
-    "HELP": {(1, 0, 1): 4, (2, 0, 1): 4},
-    "LAG": {(0, 0, 0): 4, (0, 0, 1): 8, (1, 0, 1): 8, (2, 0, 1): 8, (0, 1, 1): 8},
-    "LAGR": 0,
-    "REP0": "VVVVVVVVVVAAAGGG", "REP": "VVVVVVVVVVVVAAAA", "REPR": "VVVVVVVVAAAAAAAA",
-    "YA": "AV", "MTA": 6,
-    "SIG": 220.0, "GA": 1.56, "SCA": 3.8, "PE": 0.42, "ROUNDS": 2400, "SEED": 1, "NOISE": 1500.0,
+    "NS": [10, 6],
+    "CX": {(0, 0): [1, 1, 2, 2, 2, 4, 4], (0, 1): [1] * 12 + [2, 2], (1, 0): [2, 2, 4, 4, 4], (1, 1): [6, 6, 2, 2]},
+    "CM": {(0, 0): [4, 4, 4, -2, -2], (0, 1): [4, 4, 4, 2, 2], (1, 0): [4, 4, 4, 2, 2], (1, 1): [4, 4, 4, 2, 2]},
+    "CX0": [[6, 6, 4], [6, 6, 2, 2]], "CM0": [[4, 4, 4, 2, 2], [6, 6, 2, 2]],
+    "CXR": [6, 6, 2, 2], "CMR": [6, 6, 2, 2],
+    "REP": [8, 12], "REPR": 8, "NT": "A", "Y1T": "G", "YA": "AA", "ORD": False,
+    "SIG": 220.0, "GA": 1.56, "SCA": 3.8, "PE": 0.45, "GF": 1.0, "UV": "ar", "ODD": 6,
+    "ELSE": [{"GA": 1.1, "SCA": 2.5, "SIG": 160.0, "PE": 0.5}, {"GA": 1.9, "SCA": 5.0, "SIG": 300.0, "PE": 0.45}],
+    "ROUNDS": 3400, "SEED": 1, "NOISE": 800.0, "TEMP": 60.0, "WIN": 200, "W2": 1.0, "PICK": 0.5, "WELSE": 0.5, "SKIP": 300.0,
+    "TRIES": 5, "TOP": 12, "SOFT": 0.1, "EARLY": 0.05, "HINT": {"MN": 0.0, "MG": 0.2},
+    "FIRST": [("ca", 0, "MNr", 0)],
 }
 NENG = 8
 
 
-def build(g, T, dst_of, topo, core):
+def build(g, T, dst_of, topo, core, PAR):
     ops = []
+    now = [-1]
     arena = {}
     fill = {"AF": 0, "AB": 0, "AI": 0, "AU": 0}
-    NH, GA, SCA = PAR["NH"], PAR["GA"], PAR["SCA"]
-    N = 16 // NH
-    BW = 16 * N
+    NS, GA, SCA = PAR["NS"], PAR["GA"], PAR["SCA"]
+    NH, WM = len(NS), 16 * max(NS)
+    H = list(range(NH))
+    C0 = [sum(NS[:h]) for h in H]
+    hof = [h for h in H for _ in range(NS[h])]
 
     def ap(kind, name, n, a=0, b=None, st=1):
         if name not in arena:
@@ -78,8 +86,16 @@ def build(g, T, dst_of, topo, core):
         b = n if b is None else b
         return T[kind][:, o + a:o + b:st] if st != 1 else T[kind][:, o + a:o + b]
 
-    def op(eng, fn, cost, r=(), w=(), lat=0.0, dma=None):
-        ops.append({"e": eng, "fn": fn, "c": cost, "r": list(r), "w": list(w), "lat": lat, "dma": dma})
+    def op(eng, fn, cost, r=(), w=(), lat=0.0, dma=None, acc=None):
+        cost *= PAR["GF"] if eng == "G" else 1.0
+        ops.append({"e": eng, "fn": fn, "c": cost, "r": list(r), "w": list(w), "lat": lat, "dma": dma, "acc": acc, "alt": [], "t": now[0]})
+
+    def either(*calls):
+        for c in calls:
+            c()
+        o = ops[-len(calls)]
+        o["alt"] = [(x["e"], x["c"], x["fn"]) for x in ops[-len(calls):]]
+        del ops[len(ops) - len(calls) + 1:]
 
     V, Ac, P = g.vector, g.scalar, g.tensor
 
@@ -112,16 +128,32 @@ def build(g, T, dst_of, topo, core):
             kw["scale"] = scale
         op("A", lambda: Ac.activation(out, a, fn, **kw), c, r, w)
 
-    def rep(eng, out, a, sign, n, r, w):
-        if eng == "V":
-            ts(out, a, sign, None, A.mult, None, n, r, w, 0.5)
+    def rep(eng, out, a, sign, n, r, w, f=0.5):
+        if len(eng) > 1:
+            either(*[lambda e=e: rep(e, out, a, sign, n, r, w, f) for e in eng])
+        elif eng == "V":
+            ts(out, a, sign, None, A.mult, None, n, r, w, f)
         elif eng == "A":
             act(out, a, F.Copy, 78 + n, r, w, scale=sign)
         else:
             op("G", lambda: g.affine_select(out, a, [[0, n]], A.is_gt, 0.0, 1, 0), 200 + 2 * n, r, w)
 
-    def mm(out, l, rh, st, sp, n, r, w):
-        op("P", lambda: P.matmul(out, l, rh, st, sp), max(64, n) * PAR["PE"] + 8, r, w)
+    def mm(out, l, rh, st, sp, n, r, w, f=1.0):
+        fn, c = (lambda: P.matmul(out, l, rh, st, sp)), max(64, n) * PAR["PE"] * f + 8
+        o = ops[-1]
+        if o["e"] == "P" and o["acc"] is None and o["r"] == list(r) and o["w"] == list(w) and o["n"] < 16:
+            o["fn"] = lambda a=o["fn"]: (a(), fn())[1]
+            o["c"] += c
+            o["n"] += 1
+        else:
+            op("P", fn, c, r, w)
+            ops[-1]["n"] = 1
+
+    nacc = [0]
+
+    def mma(out, pairs, n, r, w):
+        fn = lambda sp: [P.matmul(out, l, rh, False, sp and z == len(pairs) - 1) for z, (l, rh) in enumerate(pairs)][-1]
+        op("P", fn, len(pairs) * (max(64, n) * PAR["PE"] + 8), r, w, acc=nacc[0])
 
     def iota(out, pat, n, w, cm=0, fl=True):
         if fl:
@@ -142,107 +174,126 @@ def build(g, T, dst_of, topo, core):
     b = lambda name, n, *a: ap("AB", name, n, *a)
     i = lambda name, n, *a: ap("AI", name, n, *a)
     u = lambda name, n, *a: ap("AU", name, n, *a)
+    MT = lambda x, y: T.MT[:, 32 + x:32 + y]
 
     dma("S", T.X[:, 3328:4096], T.xc[:, 3328:4096], [], ["Xl"], 2200)
     dma("A", T.WI[:, 0:1], T.wt[:], [], ["WI"], 2000)
+    dma("A", T.YM[0:8, 0:4096], T.mk[:], [], ["mk"], 2400)
     dma("S", T.OCI[:, 0:1024], T.oc[:, 0:1024], [], ["OCI0"], 3800)
     dma("S", T.OCI[:, 1024:2048], T.oc[:, 1024:2048], [], ["OCI1"], 5400)
     dma("S", T.X[:, 0:3328], T.xc[:, 0:3328], [], ["Xr"], 8000)
-    for j in range(16):
-        dma("S", T.DL[j:128:16, :], T.dl[:], [], ["DL%d" % j], 9000, "d23")
-        dma("S", T.TI[j:128:16, 0:1], T.th[:], [], ["TI%d" % j], 9000, "d23")
-    DLT = ["DL%d" % j for j in range(16)] + ["TI%d" % j for j in range(16)]
+    dma("A", T.DL[0:8, 0:768], T.dl[:], [], ["DL0"], 2200, "d23")
+    dma("A", T.DL[0:8, 776:777], T.th[:], [], ["DL1"], 2200, "d23")
 
     iota(i("pi", 1), [[0, 1]], 1, ["pi"], 1, False)
     iota(f("I144", 144), [[1, 144]], 144, ["I144"])
     iota(f("IG", 128), [[16, 8], [0, 16]], 128, ["IG"])
     iota(f("II", 256), [[0, 16], [1, 16]], 256, ["II"])
-    iota(b("IDX", 256), [[1, 256]], 256, ["IDX"])
-    iota(f("IDX2", 256), [[0, NH], [2, BW]], 256, ["IDX2"])
+    iota(b("I32", WM), [[32, WM // 16], [0, 16]], WM, ["I32"])
     iota(f("SLOT", 64), [[1, 4], [4, 16]], 64, ["SLOT"])
-    iota(f("IT0", 16), [[BW, NH], [16 // N, N]], 16, ["IT0"])
-    iota(f("IN", 16), [[0, NH], [1, N]], 16, ["IN"])
-    iota(f("IT1", 16), [[BW, NH], [1, N]], 16, ["IT1"])
     ts(i("ji", 1), i("pi", 1), 15, None, A.bitwise_and, None, 1, ["pi"], ["ji"])
     ts(i("gi", 1), i("pi", 1), 112, None, A.bitwise_and, None, 1, ["pi"], ["gi"])
-    ts(i("jl", 1), i("pi", 1), N - 1, None, A.bitwise_and, None, 1, ["pi"], ["jl"])
-    ts(i("jh", 1), i("ji", 1), N.bit_length() - 1, None, A.arith_shift_right, None, 1, ["ji"], ["jh"])
 
     def col(name, src, s1, o0):
         ts(f(name, 1), i(src, 1), s1, None, o0, None, 1, [src], [name])
 
+    def lin(out, a, scale, bias, n, r, w):
+        either(lambda: ts(out, a, scale, bias, A.mult, A.add, n, r, w), lambda: act(out, a, F.Identity, 78 + n, r, w, bias=bias, scale=scale))
+
     def acol(name, src, scale, bias, dep=()):
-        act(f(name, 1), f(src, 1), F.Identity, 80, [src] + list(dep), [name], bias=bias, scale=scale)
+        lin(f(name, 1), f(src, 1), scale, bias, 1, [src] + list(dep), [name])
 
     col("g15", "gi", 15.0, A.add)
     col("jf", "ji", 1.0, A.mult)
-    col("jl16", "jl", 16.0, A.mult)
-    col("jhf", "jh", 1.0, A.mult)
     col("r0", "ji", 0.0, A.is_equal)
     col("r1", "ji", 1.0, A.is_equal)
     col("r2", "ji", 2.0, A.is_equal)
+    col("r3", "ji", 3.0, A.is_equal)
     acol("gf", "g15", 1.0, -15.0)
-    acol("jN", "jf", float(N), 0.0)
-    acol("j64", "jf", 64.0, 0.0)
-    acol("jB", "jf", float(BW), 0.0)
-    acol("j32", "jf", 1.0, 32.0)
+    for n in sorted(set(NS + [4])):
+        acol("jB%d" % n, "jf", 16.0 * n, 0.0)
+    for h in H:
+        acol("jN%d" % h, "jf", float(NS[h]), 16.0 * C0[h])
     for e in range(2):
-        acol("dumM%d" % e, "jf", 1.0, 4096.0 + 16 * e)
+        acol("dumA%d" % e, "jf", 1.0, 16.0 * e)
+        acol("dumM%d" % e, "jf", 1.0, 4128.0 + 16 * e)
         acol("dumL%d" % e, "jf", 1.0, 2048.0 + 16 * e)
-    acol("r0m", "r0", -65536.0, 0.0)
-    acol("r0l", "r0", -4096.0, 0.0)
-    acol("r0n", "r0", -1.0, 0.0)
-    acol("r0z", "r0", Z2, 0.0)
-    acol("nr0", "r0", -1.0, 1.0)
-    acol("r2s", "r2", 1.0 / SC, 0.0)
-    acol("r12s", "r1", 64.0 / SC, f("r2s", 1), ["r2s"])
+    acol("r3m", "r3", -KS, 0.0)
+    acol("r0m", "r0", -1.0, f("r3m", 1), ["r3m"])
+    acol("r03", "r0", 1.0, f("r3", 1), ["r3"])
+    acol("r0l", "r0", 4096.0, 0.0)
+    acol("r0n", "r0", 8192.0, 0.0)
+    acol("r0p", "r0", -8192.0, 0.0)
+    acol("r0z", "r03", Z2, 0.0)
+    acol("nr0", "r03", -1.0, 1.0)
+    acol("r12s", "r1", 64.0, f("r2", 1), ["r2"])
     tt(f("r12", 1), f("r1", 1), f("r2", 1), A.add, 1, ["r1", "r2"], ["r12"])
     ts(f("r12x", 1), f("r12", 1), 32.0, None, A.mult, None, 1, ["r12"], ["r12x"])
     cp(f("wp", 1), T.WI[:, 0:1], 1, ["WI"], ["wp"])
-    acol("wn", "wp", -1.0, 0.0)
-    cp(f("th", 1), T.TI[:, 0:1], 1, DLT, ["th"])
-    ms(f("A0", 1), -0.375, 1, ["A0"])
+    ms(f("A0", 1), AOFF, 1, ["A0"])
 
     def Z(name, j):
         return b(name, 144, 15 - j, 143 - j)
 
-    for name, val, dep in (("Zp", f("wp", 1), ["wp"]), ("Zs", -256.0, []), ("Zm", f("r0m", 1), ["r0m"])):
+    for name, val, dep in (("Zp", f("wp", 1), ["wp"]), ("Zs", -1.0 / 256, []), ("Zm", f("r0m", 1), ["r0m"])):
         ts(b(name, 144), f("I144", 144), f("g15", 1), val, A.is_equal, A.mult, 144, ["I144", "g15"] + dep, [name])
-    act(b("Zn", 144), b("Zp", 144), F.Copy, 222, ["Zp"], ["Zn"], scale=-1.0)
+    rep("VA", b("Zn", 144), b("Zp", 144), -1.0, 144, ["Zp"], ["Zn"])
     ts(b("B1", 128), f("IG", 128), f("gf", 1), None, A.is_equal, None, 128, ["IG", "gf"], ["B1"])
-    for name, val in (("Ba", "r12s"), ("B0", "r0"), ("B0n", "r0n"), ("B2", "r2"), ("B0l", "r0l"), ("Bwn", "wn")):
-        act(b(name, 128), b("B1", 128), F.Copy, 206, ["B1", val], [name], scale=f(val, 1))
-    act(b("B1n", 128), b("B1", 128), F.Copy, 206, ["B1"], ["B1n"], scale=-1.0)
+    for name, val in (("Ba", "r12s"), ("B0", "r0p"), ("B0n", "r0n"), ("B0l", "r0l")):
+        rep("VA", b(name, 128), b("B1", 128), f(val, 1), 128, ["B1", val], [name])
     op("G", lambda: g.affine_select(b("ID", 128), b("B1", 128), [[-1, 128]], A.is_equal, 0.0, 0, 1), 456, ["B1"], ["ID"])
     op("G", lambda: g.affine_select(b("TRI", 128), b("B1", 128), [[1, 128]], A.is_gt, 0.0, 0, -1), 456, ["B1"], ["TRI"])
+    ts(b("I2k", WM), f("II", 256, 0, WM), 2.0, 1.0, A.mult, A.add, WM, ["II"], ["I2k"])
+    for name, val in (("IK", KS), ("I4n", -4096.0), ("I8", 8192.0), ("I8n", -8192.0)):
+        rep("VA", b(name, 128), b("ID", 128), val, 128, ["ID"], [name])
+    rep("VAG", f("IF", 128), b("ID", 128), 1.0, 128, ["ID"], ["IF"], 1.0)
     ms(b("ON", 128), 1.0 / 16, 64, ["ON"])
-    ms(b("OF", 256), -OFFS, 128, ["OF"])
+    ms(b("on1", 32), 1.0, 64, ["on1"])
+    ms(f("one", 128), 1.0, 128, ["one"])
+    op("G", lambda: g.affine_select(f("G8", 128)[0:8, :], f("one", 128)[0:8, :], [[1, 8], [0, 16]], A.is_equal, 0.0, 0, -1), 456, ["one"], ["G8"])
+    ts(T.DF[0:8, 0:768], T.DL[0:8, 0:768], -8192.0, None, A.add, None, 768, ["DL0", "DL1"], ["DF0"])
+    cp(T.DF[0:8, 776:777], T.DL[0:8, 776:777], 1, ["DL0", "DL1"], ["DF1"])
+    mm(T.SM[:, 300:301], f("G8", 128)[0:8, :], T.DF[0:8, 776:777], True, True, 1, ["G8", "DF1"], ["SM"], 4.0)
+    ts(f("n256", 1), T.SM[:, 300:301], -1.0 / 256, 1.0, A.mult, A.add, 1, ["SM"], ["n256"])
+    op("G", lambda: g.iota(f("IO", 16, 0, 15), [[-1, 15]], 14, 0, allow_small_or_imprecise_dtypes=True), 180, [], ["IOa"])
+    ms(f("IO", 16, 15, 16), 15.0, 1, ["IOb"])
+    ts(b("OH", 16), f("IO", 16), f("jf", 1), None, A.is_equal, None, 16, ["IOa", "IOb", "jf"], ["OH"])
     iota(f("IJ", 384, 0, 256), [[0, 8], [1, 32]], 256, ["IJa"])
     iota(f("IJ", 384, 256, 384), [[0, 8], [1, 16]], 128, ["IJb"])
     op("G", lambda: g.iota(f("IL", 384, 0, 256), [[0, 8], [1, 32]], -16, 0, allow_small_or_imprecise_dtypes=True), 662, [], ["ILa"])
     iota(f("IL", 384, 256, 384), [[0, 8], [1, 16]], 128, ["ILb"])
     op("G", lambda: g.iota(f("IB", 24, 0, 16), [[2, 8], [0, 2]], 1, 0, allow_small_or_imprecise_dtypes=True), 182, [], ["IBa"])
     iota(f("IB", 24, 16, 24), [[2, 8]], 8, ["IBb"])
-    ts(b("eq", 256), f("IJ", 384, 128, 384), f("jf", 1), None, A.is_equal, None, 256, ["IJa", "IJb", "jf"], ["eq"])
-    ts(b("gt", 192), f("IJ", 384, 128, 320), f("jf", 1), 4.0, A.is_gt, A.mult, 192, ["IJa", "IJb", "jf"], ["gt"])
-    for bw in (128, 64):
-        w = bw + bw // 2
-        act(b("CC%d" % bw, 2 * w, 0, w), b("eq", 256, 128 - bw, 128 - bw + w), F.Identity, 78 + w, ["eq"], ["CC%da" % bw], bias=-4.0, scale=4.0 - OFFS)
-        act(b("CC%d" % bw, 2 * w, w, 2 * w), b("gt", 192, 128 - bw, 128 - bw + w), F.Identity, 78 + w, ["gt"], ["CC%db" % bw], bias=4.0, scale=-(4.0 + OFFS) / 4.0)
-    act(b("MK", BW), b("eq", 256, 128, 256), F.Identity, 78 + BW, ["eq"], ["MK"], bias=-BIG, scale=BIG)
-    act(b("RL", 384), f("IJ", 384), F.Sign, 462, ["IJa", "IJb"], ["RL"])
-    act(b("RX", 192), f("IJ", 384, 128, 320), F.Sign, 270, ["IJa", "IJb"], ["RX"])
-    ts(b("eqL", 384), f("IL", 384), f("jf", 1), None, A.is_equal, None, 384, ["ILa", "ILb", "jf"], ["eqL"])
-    ts(b("gtL", 384), f("IL", 384), f("jf", 1), 4.0, A.is_gt, A.mult, 384, ["ILa", "ILb", "jf"], ["gtL"])
-    tt(b("C3", 384), b("gtL", 384), b("eqL", 384), A.subtract, 384, ["gtL", "eqL"], ["C3"])
-    act(b("R0", 256), f("II", 256), F.Sign, 334, ["II"], ["R0"])
-    act(f("RB", 256), b("R0", 256), F.Identity, 334, ["R0"], ["RB"], bias=8388608.0, scale=-8388608.0)
-    ts(u("T0", 16), f("IT0", 16), f("jl16", 1), f("jhf", 1), A.add, A.add, 16, ["IT0", "jl16", "jhf"], ["T0"])
-    ts(u("T1", 16), f("IT1", 16), f("jN", 1), None, A.add, None, 16, ["IT1", "jN"], ["T1"])
+    ts(b("eq", 160), f("IJ", 384, 0, 160), f("jf", 1), None, A.is_equal, None, 160, ["IJa", "jf"], ["eq"])
+    ts(b("eq16", 160), f("II", 256, 0, 160), f("jf", 1), None, A.is_equal, None, 160, ["II", "jf"], ["eq16"])
+    lin(b("CC", 480, 0, 160), b("eq", 160), SC, 6144.0 - SC, 160, ["eq"], ["CCa"])
+    lin(b("CC", 480, 160, 320), b("eq16", 160), SC, 6144.0 - SC, 160, ["eq16"], ["CCb"])
+    ms(f("C5", 160), 6144.0, 160, ["C5"])
+    act(b("CC", 480, 320, 480), f("C5", 160), F.Silu, 1650 + 160, ["C5"], ["C6"])
+    rep("GAV", b("CD", 480, 0, 240), b("CC", 480, 0, 240), 1.0, 240, ["CCa", "CCb"], ["CDa"])
+    ms(b("CD", 480, 240, 480), 6144.0, 120, ["CDb"])
+    lin(b("MK", WM), b("eq16", 160, 0, WM), BIG - 4096, -BIG, WM, ["eq16"], ["MK"])
+    rep("VA", b("B1n", 128), b("B1", 128), -1.0, 128, ["B1"], ["B1n"])
+    either(lambda: act(b("RL", 384), f("IJ", 384), F.Sign, 462, ["IJa", "IJb"], ["RL"]),
+           lambda: ts(b("RL", 384), f("IJ", 384), 1.0, None, A.min, None, 384, ["IJa", "IJb"], ["RL"]))
+    ts(b("eqL", 384), f("IL", 384), f("jf", 1), -8192.0, A.is_equal, A.mult, 384, ["ILa", "ILb", "jf"], ["eqL"])
+    ts(b("gtL", 384), f("IL", 384), f("jf", 1), SC, A.is_gt, A.mult, 384, ["ILa", "ILb", "jf"], ["gtL"])
+    ts(b("R0", WM), f("II", 256, 0, WM), 1.0, None, A.min, None, WM, ["II"], ["R0"])
+    lin(b("RB", WM), b("R0", WM), -64.0, 64.0, WM, ["R0"], ["RB"])
+    lin(f("RC", WM), b("R0", WM), 64.0 + 4 * KS, -64.0, WM, ["R0"], ["RC"])
+    for h in H:
+        n, sh = NS[h], str(h)
+        c16 = lambda fn, name: fn(name, 16, C0[h], C0[h] + n)
+        ts(c16(f, "jj"), f("I144", 144, 0, n), 16.0, f("jf", 1), A.mult, A.add, n, ["I144", "jf"], ["jj" + sh])
+        ts(c16(i, "jq"), c16(f, "jj"), -(n - 1) / 2.0, 1.0 / n, A.add, A.mult, n, ["jj" + sh], ["jq" + sh])
+        ts(c16(f, "jr"), c16(i, "jq"), (1.0 - 16 * n) / 16, float(C0[h]), A.mult, A.add, n, ["jq" + sh], ["jr" + sh])
+        tt(c16(f, "js"), c16(f, "jr"), c16(f, "jj"), A.add, n, ["jr" + sh, "jj" + sh], ["js" + sh])
+        ts(c16(u, "T0"), c16(f, "js"), 16.0, None, A.mult, None, n, ["js" + sh], ["T0" + sh])
+        ts(c16(f, "D0"), f("I144", 144, 0, n), f("jN" + sh, 1), -256.0, A.add, A.add, n, ["I144", "jN" + sh], ["D0" + sh])
+        ts(c16(u, "T1"), c16(f, "D0"), 256.0, None, A.add, None, n, ["D0" + sh], ["T1" + sh])
+        rep("VA", c16(b, "DD"), c16(f, "D0"), -1.0, n, ["D0" + sh], ["DD" + sh])
+    T0, T1 = ["T0%d" % h for h in H], ["T1%d" % h for h in H]
     cp(u("Boff", 24), f("IB", 24), 24, ["IBa", "IBb"], ["Boff"])
-    ts(f("D0", 16), f("IT1", 16), f("jN", 1), -256.0, A.add, A.add, 16, ["IT1", "jN"], ["D0"])
-    act(f("DD", 16), f("D0", 16), F.Copy, 94, ["D0"], ["DD"], scale=-1.0)
-    ts(b("RN", 16), f("IN", 16), 0.0, None, A.not_equal, None, 16, ["IN"], ["RN"])
     for t in range(S):
         ms(T["box%d" % t][:, 0:80], 0.0, 40, ["box%d" % t, "bc%d" % t])
 
@@ -250,185 +301,223 @@ def build(g, T, dst_of, topo, core):
     ts(f("st8", 8), f("I144", 144, 0, 8), f("r1", 1), 8.0, A.mult, A.mult, 8, ["I144", "r1"], ["st8"])
     ts(f("seed", 64), f("I144", 144, 0, 64), f("r2", 1), f("r12x", 1), A.mult, A.add, 64, ["I144", "r2", "r12x"], ["seed"])
     for k in range(8):
-        ts(T.MT[:, 64 * k:64 * k + 64], f("seed", 64), f("st1", 8, k, k + 1), None, A.add, None, 64, ["seed", "st1"], ["mta%d" % k])
-    base = ["mta%d" % k for k in range(8)]
-    for k in range(1, 8):
-        if k <= PAR["MTA"]:
-            act(T.MT[:, 512 * k:512 * k + 512], T.MT[:, 0:512], F.Identity, 600, base + ["st8"], ["mtb%d" % k], bias=f("st8", 8, k, k + 1))
-        else:
-            ts(T.MT[:, 512 * k:512 * k + 512], T.MT[:, 0:512], f("st8", 8, k, k + 1), None, A.add, None, 512, base + ["st8"], ["mtb%d" % k])
-    dma("G", T.MT[0:128:16, 0:4096], T.mk[:], [], base + ["mtb%d" % k for k in range(1, 8)] + ["MT"], 2500)
-    for k in range(4):
-        cp(T.OC[:, 512 * k:512 * k + 512], T.OCI[:, 512 * k:512 * k + 512], 512, ["OCI%d" % (k // 2)], ["OCp%d" % k])
-    OCP = ["OCp%d" % k for k in range(4)]
+        lin(b("m0", 512, 64 * k, 64 * k + 64), f("seed", 64), 1.0, f("st1", 8, k, k + 1), 64, ["seed", "st1"], ["mta%d" % k])
+    ts(f("I03", 128), f("II", 256, 0, 128), -1.5, None, A.add, None, 128, ["II"], ["I03"])
+    tt(f("I04", 128), f("I03", 128), f("I03", 128), A.mult, 128, ["I03"], ["I04"])
+    ts(f("I05", 128), f("I04", 128), 2.25, None, A.is_equal, None, 128, ["I04"], ["I05"])
+    op("G", lambda: g.affine_select(b("S8", 128)[0:8, :], f("I05", 128)[0:8, :], [[1, 8], [0, 16]], A.is_equal, 0.0, 0, -1), 456, ["I05"], ["S8"])
+    for k in range(7, -1, -1):
+        bank, o, st = ("K0", "K1", "X3", "PL")[k % 4], MT(512 * k, 512 * k + 512), f("st8", 8, k, k + 1)
+        mm(T[bank][:], b("S8", 128)[0:8, :], T.YM[0:8, 512 * k:512 * k + 512], True, False, 512, ["S8", "mk"], [bank])
+        mm(T[bank][:], b("ID", 128), b("m0", 512), False, True, 512, ["ID"] + ["mta%d" % x for x in range(8)], [bank])
+        either(lambda: act(o, T[bank][:], F.Identity, 78 + 512, [bank, "st8"], ["mtb%d" % k], bias=st),
+               lambda: ts(o, T[bank][:], st, None, A.add, None, 512, [bank, "st8"], ["mtb%d" % k]))
+    MTB = ["mtb%d" % k for k in range(8)]
+    for k in range(8):
+        rep("GV", T.OC[:, 256 * k:256 * k + 256], T.OCI[:, 256 * k:256 * k + 256], 1.0, 256, ["OCI%d" % (k // 4)], ["OCp%d" % k], 1.0)
+    OCP = ["OCp%d" % k for k in range(8)]
 
     for t in range(S):
         B = W - 256 * (t + 1)
-        act(b("yT%d" % t, 256), T.X[:, B:B + 256].indirect(u("T0", 16)), F.Copy, 78 + GA * 256, ["Xl", "T0"], ["yT%d" % t])
+        act(b("yT%d" % t, 256), T.X[:, B:B + 256].indirect(u("T0", 16)), F.Copy, 78 + GA * 256, ["Xl"] + T0, ["yT%d" % t])
     YRT = {}
 
     def rep0(t):
         YRT[t] = ["YR%d_%d" % (t, k) for k in range(16)]
         for k in range(16):
-            rep(PAR["REP0"][k] if t == 0 else "G", T["YR%d" % t][:, k:4096:16], b("yT%d" % t, 256), 1.0, 256, ["yT%d" % t], [YRT[t][k]])
+            rep("VAG" if t == 0 else "G", T["YR%d" % t][:, k:4096:16], b("yT%d" % t, 256), 1.0, 256, ["yT%d" % t], [YRT[t][k]])
 
-    def square(tag, src, stok, n):
-        cp(i("ui" + tag, n), src, n, [stok], ["ui" + tag])
-        ts(i("u" + tag, n), i("ui" + tag, n), 4095, None, A.bitwise_and, None, n, ["ui" + tag], ["u" + tag])
-        ts(f("t" + tag, n), i("u" + tag, n), 1.0 / 32, 37.0, A.mult, A.add, n, ["u" + tag], ["t" + tag])
-        tt(f("q" + tag, n), i("u" + tag, n), f("t" + tag, n), A.mult, n, ["u" + tag, "t" + tag], ["q" + tag])
-
-    def u_part(tag, rhs, rtok, zname, n):
-        for x, r in enumerate(rhs):
+    def u_part(tag, r, rtok, zname, m):
+        if tag[0] in PAR["UV"]:
             for j in range(16):
-                mm(T.PU[:, x * n:x * n + n], Z(zname, j), r(j), j == 0, j == 15, n, [zname] + rtok, ["PU"])
-        n = n * len(rhs)
-        square(tag, T.PU[:, 0:n], "PU", n)
+                mm(T.PU[:, 0:m], Z(zname, j), r(j), j == 0, j == 15, m, [zname] + rtok, ["PU"])
+            act(b("fl" + tag, m), T.PU[:, 0:m], F.Identity, 78 + m, ["PU"], ["fl" + tag], bias=-128.5 * 4096 - 0.5, scale=-1.0)
+            tt(f("w" + tag, m), T.PU[:, 0:m], b("fl" + tag, m), A.add, m, ["PU", "fl" + tag], ["w" + tag])
+            act(f("q" + tag, m), f("w" + tag, m), F.Square, 78 + m, ["w" + tag], ["q" + tag], bias=592.0 + 129 * 4096)
+            return
+        for bank in ("PU", "PL"):
+            for j in range(16):
+                mm(T[bank][:, 0:m], Z(zname, j), r(j), j == 0, bank == "PU" and j == 15, m, [zname] + rtok, [bank])
+        act(b("fl" + tag, m), T.PU[:, 0:m], F.Identity, 78 + m, ["PU"], ["fl" + tag], bias=128.5 + 1.0 / 8192, scale=1.0 / 4096)
+        mm(T.PL[:, 0:m], b("I4n", 128), b("fl" + tag, m), False, True, m, ["I4n", "fl" + tag], ["PL"])
+        act(f("q" + tag, m), T.PL[:, 0:m], F.Square, 78 + m, ["PL"], ["q" + tag], bias=592.0 + 129 * 4096)
 
-    def place(tag, n, an, t, ctag, lt, a0, first=False, q0=0):
+    def place(tag, n, an, t, ctag, lt, a0, first=False):
         B = W - 256 * (t + 1)
         l, lu = i("l" + lt, 16, a0, a0 + n), u("lu" + lt, 16, a0, a0 + n)
-        q, qt = f("q" + tag, n, q0, q0 + n), "q" + tag
-        tag = tag + lt[1:2] * (lt[0] == "a")
-        ts(i("li" + tag, n), q, f(an, 1), None, A.add, None, n, [qt, an], ["li" + tag])
+        q, qt = f("q" + tag, n), "q" + tag
+        ts(i("li" + tag, n), q, 1.0 / 32, f(an, 1), A.mult, A.add, n, [qt, an], ["li" + tag])
         ts(l, i("li" + tag, n), 2047, None, A.bitwise_and, None, n, ["li" + tag], ["l" + tag])
         cp(lu, l, n, ["l" + tag], ["lu" + tag])
         win = T.OCI[:, 0:2048] if first else T.OC[:, 0:2048]
-        op("V", lambda: V.tensor_scalar(u(ctag, 16 * n), win.indirect(lu), B / 4096.0, -15.0 / 32, A.mult, A.add),
+        c = u(ctag, 16 * n)
+        op("V", lambda: V.tensor_scalar(c, win.indirect(lu), B / 4096.0, -15.0 / 32, A.mult, A.add),
            60 + GA * 16 * n, ["lu" + tag] + (["OCI0", "OCI1"] if first else ["OC"] + OCP), [ctag])
 
-    def main(ctag, c0, n, K, mn, mg, yr, a0, yrt, chunks, help_, lag):
+    def keys(K, bw):
+        return T.SM[:, 320:320 + bw] if K == "SM" else T[K][:, 0:bw]
+
+    def main(ctag, c0, n, K, mn, mg, yr, a0, yrt, chunks, mchunks):
         bw = 16 * n
-        o = T[K][:, 0:bw]
-        mm(o, b("ID", 128), b("IDX", 256, 0, bw), True, False, bw, ["ID", "IDX"], [K])
-        mchunks = []
-        for c in chunks:
-            a = sum(mchunks)
-            mchunks += [16 - help_ - a, a + c - 16 + help_] if a < 16 - help_ < a + c else [c]
+        o = keys(K, bw)
+        mm(o, b("IK", 128), b("I32", WM, 0, bw), True, False, bw, ["IK", "I32", "I2k"], [K])
+        mm(o, b("IK", 128), b("I2k", WM, 0, bw), False, False, bw, ["IK", "I32", "I2k"], [K])
+        oV = ["~mV"] if PAR["ORD"] else []
         a = 0
         for c in chunks:
             e = a + c
             off = u(ctag, 16 * n, c0 + a * n, c0 + e * n)
             sl = slice(a0 + a * bw, a0 + e * bw)
             tg(T[mn][:, sl], T.X[:, 0:4096].indirect(off), T[yr][:, sl], A.min, 60 + GA * c * bw,
-               [ctag, "Xl", "Xr"] + yrt, ["%s%d_%d" % (mn, a0, x) for x in range(a, e)] + ["~mV"])
+               [ctag, "Xl", "Xr"] + yrt, ["%s%d_%d" % (mn, a0, x) for x in range(a, e)] + oV)
             a = e
         a = 0
         for c in mchunks:
-            e = a + c
+            e = a + abs(c)
             off = u(ctag, 16 * n, c0 + a * n, c0 + e * n)
             sl = slice(a0 + a * bw, a0 + e * bw)
             wt_ = ["%s%d_%d" % (mg, a0, x) for x in range(a, e)]
-            if e > 16 - help_:
-                op("V", lambda off=off, sl=sl: V.tensor_copy(T[mg][:, sl], T.MT[:, 0:4096].indirect(off)), 60 + GA * c * bw, [ctag, "MT"], wt_ + ["~mV"])
+            o1, src = T[mg][:, sl], MT(0, 4096).indirect(off)
+            onV = lambda: op("V", lambda o1=o1, src=src: V.tensor_copy(o1, src), 60 + GA * abs(c) * bw, [ctag, "MT"] + MTB, wt_)
+            if c < 0:
+                onV()
             else:
-                act(T[mg][:, sl], T.MT[:, 0:4096].indirect(off), F.Copy, 78 + GA * c * bw, [ctag, "MT"], wt_ + ["~mA"])
+                either(lambda: act(o1, src, F.Copy, 78 + GA * c * bw, [ctag, "MT"] + MTB, wt_), onV)
             a = e
-        ends, mends = [], []
-        for c in chunks:
-            ends += [len(ends) + c] * c
-        for c in mchunks:
-            a = len(mends)
-            mends += [a + c + lag + 0.5 if a < 16 - help_ else a + c + help_ + 0.25] * c
-        seq = sorted([(x, 0) for x in range(16)] + [(x, 1) for x in range(16)], key=lambda z: (mends if z[1] else ends)[z[0]])
-        for z, (x, m) in enumerate(seq):
-            src, zn = (mg, "Zm") if m else (mn, "Zs")
-            mm(o, Z(zn, x), T[src][:, a0 + x * bw:a0 + (x + 1) * bw], False, z == 31, bw, [zn, "%s%d_%d" % (src, a0, x)], [K])
+        nacc[0] += 1
+        for src, zn, cs in ((mn, "Zs", chunks), (mg, "Zm", mchunks)):
+            a = 0
+            for c in cs:
+                e = a + abs(c)
+                mma(o, [(Z(zn, x), T[src][:, a0 + x * bw:a0 + (x + 1) * bw]) for x in range(a, e)], bw,
+                    [zn] + ["%s%d_%d" % (src, a0, x) for x in range(a, e)], [K])
+                a = e
 
-    def pick(tag, n, K, jn):
-        bw = 16 * n
-        scan(f("R" + K, bw), f("RB", 256, 0, bw), T[K][:, 0:bw], A.add, A.min, bw, ["RB", K], ["R" + K])
-        ts(i("ki" + tag, n), f("R" + K, bw, 15, bw, 16), BIG, None, A.add, None, n, ["R" + K], ["ki" + tag])
-        ts(i("kx" + tag, n), i("ki" + tag, n), 255, None, A.bitwise_and, None, n, ["ki" + tag], ["kx" + tag])
+    def pick(tag, n, K):
+        bw, jn = 16 * n, "jB%d" % n
+        scan(f("R" + K, bw), b("RB", WM, 0, bw), keys(K, bw), A.add, A.min, bw, ["RB", K], ["R" + K])
+        ts(i("ki" + tag, n), f("R" + K, bw, 15, bw, 16), 1 / KS, BIG, A.mult, A.add, n, ["R" + K], ["ki" + tag])
+        ts(i("kx" + tag, n), i("ki" + tag, n), 1, 255, A.arith_shift_right, A.bitwise_and, n, ["ki" + tag], ["kx" + tag])
         ts(u("ku" + tag, n), i("kx" + tag, n), f(jn, 1), None, A.add, None, n, ["kx" + tag, jn], ["ku" + tag])
 
     def toks(name, a0):
         return ["%s%d_%d" % (name, a0, x) for x in range(16)]
 
-    def mark(tag, n, mg, a0, nl, nlt, ag, s):
+    def mark(tag, n, mg, a0, nl, nlt, ag, s, XX, final=False):
         bw = 16 * n
         at = "ag" + tag[0] + s
-        w = bw + bw // 2
-        cc = "CC%d" % bw
-        rx = b("RX", 192, 128 - bw, 128 - bw + w)
-        x1, x2 = T.XX[:, 0:w], T.XX[:, w:2 * w]
+        X_ = T[XX]
+        odd = n > PAR["ODD"]
+        wb = bw // 2 if odd else bw
+        x1 = [X_[:, 0:bw], X_[:, 160:160 + wb]]
+        x2 = [X_[:, 320:320 + bw], X_[:, 240:240 + wb] if odd else X_[:, 320:320 + bw]]
 
         def spread(mat, src, tok, last):
-            for x in (0, w):
-                mm(T.XX[:, x:x + bw], b(mat, 128), src(0, bw), False, False, bw, [mat, tok], ["XX"])
-                for c in range(n // 2):
-                    mm(T.XX[:, x + bw + 16 * c:x + bw + 16 * c + 16], b(mat, 128), src(32 * c + 16, 32 * c + 32), False,
-                       last and x == w and c == n // 2 - 1, 16, [mat, tok], ["XX"])
+            for c in range(n // 2 * odd):
+                for x in (160, 240):
+                    mm(X_[:, x + 16 * c:x + 16 * c + 16], b(mat, 128), src(32 * c + 16, 32 * c + 32), False, False, 16, [mat] + tok, [XX])
+            for x in ((0, 320) if odd else (0, 160, 320)):
+                mm(X_[:, x:x + bw], b(mat, 128), src(0, bw), False, last and x == 320, bw, [mat] + tok, [XX])
 
-        mm(T.XX[:, 0:2 * w], b("ID", 128), b(cc, 2 * w), True, False, 2 * w, ["ID", cc + "a", cc + "b"], ["XX"])
+        cc = "CD" if odd else "CC"
+        mm(X_[:, 0:320 + bw], b("ID", 128), b(cc, 480, 0, 320 + bw), True, False, 320 + bw, ["ID", "CCa", "CCb", "C6", "CDa", "CDb"], [XX])
         spread("B0", nl, nlt, False)
-        act(ag(0, bw), T[mg][:, a0:a0 + 16 * bw].indirect(u("ku" + tag, n)), F.Copy, 78 + GA * bw, toks(mg, a0) + ["ku" + tag], [at])
-        spread("Ba", ag, at, True)
-        act(f("agf" + s, bw), ag(0, bw), F.Silu, 78 + bw, [at, "nr0", "r0z"], ["agf" + s], bias=f("r0z", 1), scale=f("nr0", 1))
-        scan(f("H" + s, w), rx, x1, A.mult, A.max, w, ["RX", "XX"], ["H" + s])
-        tt(b("E" + s, w), x2, f("H" + s, w), A.is_equal, w, ["XX", "H" + s], ["E" + s], 1.0)
-        scan(b("Fs" + s, w), rx, b("E" + s, w), A.mult, A.max, w, ["RX", "E" + s], ["Fs" + s], 0.5)
-        for e, (lo, hi, st) in enumerate(((31, bw, 32), (bw + 15, w, 16))):
-            gt_ = "G%d" % e + tag
-            tt(f(gt_, n // 2), b("Fs" + s, w, lo, hi, st), f("H" + s, w, lo, hi, st), A.max, n, ["Fs" + s, "H" + s], [gt_])
-            ts(u("mo" + tag, n, e, n, 2), f(gt_, n // 2), SC, f("dumM%d" % e, 1), A.mult, A.min, n, [gt_, "dumM%d" % e], ["mo%d" % e + tag])
+        act(ag(0, bw), T[mg][:, a0:a0 + 16 * bw].indirect(u("ku" + tag, n)), F.Identity, 78 + GA * bw, toks(mg, a0) + ["ku" + tag, "nr0", "r0z"], [at],
+            bias=f("r0z", 1), scale=f("nr0", 1))
+        spread("Ba", ag, [at], True)
+        if not final:
+            rep("GAV", f("agf" + s, bw), ag(0, bw), 1.0, bw, [at], ["agf" + s], 1.0)
+        for e, w, st, rx in ((0, bw, 32, b("RL", 384, 0, bw)), (1, wb, 16 if odd else 32, b("RL", 384, 256, 256 + wb))):
+            z = "%d%s" % (e, s)
+            scan(f("H" + z, w), rx, x1[e], A.mult, A.max, w, ["RL", XX], ["H" + z])
+            tt(b("E" + z, w), x2[e], f("H" + z, w), A.not_equal, w, [XX, "H" + z], ["E" + z], 1.0)
+            scan(f("Fs" + z, w), b("E" + z, w), x1[e], A.mult, A.max, w, [XX, "E" + z], ["Fs" + z])
+            ts(u("mo" + tag, n, e, n, 2), f("Fs" + z, w, st - 1, w, st), f("dumA%d" % e, 1), f("dumM%d" % e, 1), A.max, A.min, n,
+               ["Fs" + z, "dumA%d" % e, "dumM%d" % e], ["mo%d" % e + tag])
         for c in range(n // 2):
-            act(T.MT[:, 0:4128].indirect(u("mo" + tag, n, 2 * c, 2 * c + 2)), f("agf" + s, bw, 32 * c, 32 * c + 32), F.Silu,
-                78 + SCA * 32, ["mo0" + tag, "mo1" + tag, "agf" + s], ["MT"])
+            off = u("mo" + tag, n, 2 * c, 2 * c + 2)
+            if final:
+                op("V", lambda off=off: V.tensor_copy(T.YM[:, 0:4160].indirect(off), b("on1", 32)), 60 + SCA * 32,
+                   ["mo0" + tag, "mo1" + tag, "on1"], ["YM"] + ["YM%d" % k for k in range(8)])
+            else:
+                act(T.MT[:, 0:4160].indirect(off), f("agf" + s, bw, 32 * c, 32 * c + 32), F.Silu,
+                    78 + SCA * 32, ["mo0" + tag, "mo1" + tag, "agf" + s], ["MT"] + MTB)
+                del MTB[:]
 
-    def lanes0(ts_):
-        def rhs(t, h, j):
-            a = W - 256 * (t + 1) + BW * h + 16 * (j % N) + j // N
-            return T.X[:, a:a + (N - 1) * NH + 1:NH]
-        u_part("a%d" % ts_[0], [lambda j, t=t, h=h: rhs(t, h, j) for t in ts_ for h in range(NH)], ["Xl"], "Zp", N)
+    def turn(eng, name, src, stok):
+        if eng == "A":
+            act(b(name, 256), b(src, 256).indirect(u("T1", 16)), F.Copy, 78 + GA * 256, sorted(set(stok)) + T1, [name])
+            return [[name]] * NH
+        for c in range(16):
+            rep(eng, b(name, 256, 16 * c, 16 * c + 16), b(src, 256)[:, back(c)], 1.0, 16, [stok[hof[c]]], [name + "_%d" % c])
+        return [[name + "_%d" % c for c in range(16) if hof[c] == h] for h in H]
+
+    def back(c, a=0):
+        h = hof[c]
+        return slice(a + 15 * C0[h] + c, a + 16 * (C0[h] + NS[h]), NS[h])
+
+    def lanes0(t):
+        u_part("a%d" % t, lambda j: b("yT%d" % t, 256, j, 256, 16), ["yT%d" % t], "Zp", 16)
 
     def place0(t):
-        place("a%d" % min(t, 1), 16, "A%d" % t, t, "ca", "a%d" % t, 0, t == 0, 16 * max(t - 1, 0))
+        place("a%d" % t, 16, "A%d" % t, t, "ca", "a%d" % t, 0, t == 0)
 
     rep0(0)
-    lanes0([0])
+    lanes0(0)
     place0(0)
-    lanes0([1, 2])
     rep0(1)
     for t in range(S):
         B = W - 256 * (t + 1)
         tr = "r%d" % t
+        now[0] = t
         nln, nlt = "NL%d" % t, "NT%d" % t
-        H = list(range(NH - 1, -1, -1))
-        part = lambda name, h: b(name, 256, BW * h, BW * h + BW)
-        sub = lambda name, h: (lambda x, y: b(name, 256, BW * h + x, BW * h + y))
-        act(b(nln, 256), T.MT[:, B:B + 256], F.Relu, 78 + 256, ["MT"], [nln], bias=1.0, scale=-2.0)
-        act(b(nlt, 256), T.MT[:, B:B + 256].indirect(u("T1", 16)), F.Relu, 78 + GA * 256, ["MT", "T1"], [nlt], bias=1.0, scale=-2.0)
+        part = lambda name, h: b(name, 256, 16 * C0[h], 16 * (C0[h] + NS[h]))
+        sub = lambda name, h: (lambda x, y: b(name, 256, 16 * C0[h] + x, 16 * C0[h] + y))
+        rep("GAV", b(nln, 256), MT(B, B + 256), 1.0, 256, ["MT"] + MTB, [nln], 1.0)
+        NT = turn(PAR["NT"], nlt, nln, [nln] * NH)
         for h in H:
-            main("ca", BW * h, N, "K%d" % h, "MN", "MG", "YR%d" % t, 16 * BW * h, YRT[t], PAR["CH"][NH - 1 - h],
-                 PAR["HELP"].get((t, 0, NH - 1 - h), 0), PAR["LAG"].get((t, 0, NH - 1 - h), 0))
+            main("ca", 16 * C0[h], NS[h], "K%d" % h, "MN", "MG", "YR%d" % t, 256 * C0[h], YRT[t], PAR["CX"][0, h] if t else PAR["CX0"][h],
+                 PAR["CM"][0, h] if t else PAR["CM0"][h])
+        if t + 1 < S:
+            lanes0(t + 1)
         yrt = {}
         for h in H:
-            ta, tb, a0 = "a%d%d" % (t, h), "b%d%d" % (t, h), 16 * BW * h
-            pick(ta, N, "K%d" % h, "jB")
-            tg(part("y1n", h), T.MN[:, a0:a0 + 16 * BW].indirect(u("ku" + ta, N)), T.X[:, B + BW * h:B + BW * h + BW], A.subtract,
+            N, BW, L0 = NS[h], 16 * NS[h], 16 * C0[h]
+            ta, tb, a0 = "a%d%d" % (t, h), "b%d%d" % (t, h), 16 * L0
+            pick(ta, N, "K%d" % h)
+            tg(part("y1n", h), T.MN[:, a0:a0 + 16 * BW].indirect(u("ku" + ta, N)), T.X[:, B + L0:B + L0 + BW], A.subtract,
                60 + GA * BW, toks("MN", a0) + ["ku" + ta, "Xl"], ["y1n%d" % h])
-            mark(ta, N, "MG", a0, sub(nln, h), nln, sub("aga", h), str(h))
-            u_part(tb, [lambda j: b("y1n", 256, BW * h + j, BW * h + BW, 16)], ["y1n%d" % h], "Zn", N)
+            mark(ta, N, "MG", a0, sub(nln, h), [nln], sub("aga", h), str(h), "X%d" % h)
+            u_part(tb, lambda j: b("y1n", 256, L0 + j, L0 + BW, 16), ["y1n%d" % h], "Zn", N)
             yrt[h] = ["YRh%d_%d" % (h, k) for k in range(16)]
+            rep("AV", part("y1p", h), part("y1n", h), -1.0, BW, ["y1n%d" % h], ["y1p%d" % h])
             for k in range(16):
-                rep(PAR["REP"][k], T.YRh[:, a0 + k:a0 + 16 * BW:16], part("y1n", h), -1.0, BW, ["y1n%d" % h], [yrt[h][k]])
-            place(tb, N, "A%d" % t, t, "cb%d" % h, "b%d" % t, N * h)
-        Y1 = ["y1n%d" % h for h in H]
-        act(b("y1T", 256), b("y1n", 256).indirect(u("T1", 16)), F.Copy, 78 + GA * 256, Y1 + ["T1"], ["y1T"], scale=-1.0)
-        mm(T.X3[:, 0:256], b("ID", 128), b("OF", 256), True, False, 256, ["ID", "OF"], ["X3"])
-        mm(T.X3[:, 0:256], b("B0n", 128), b(nln, 256), False, False, 256, ["B0n", nln], ["X3"])
+                e, src, sign = ("GAV", "y1p", 1.0) if k < PAR["REP"][h] else ("AV", "y1n", -1.0)
+                rep(e, T.YRh[:, a0 + k:a0 + 16 * BW:16], part(src, h), sign, BW, [src + str(h)], [yrt[h][k]])
+            place(tb, N, "A%d" % t, t, "cb%d" % h, "b%d" % t, C0[h])
+        Y1T = turn(PAR["Y1T"], "y1T", "y1n", ["y1n%d" % h for h in H])
+        mm(T.X3[:, 0:256], b("B0n", 128), b(nln, 256), True, False, 256, ["B0n", nln], ["X3"])
         mm(T.X3[:, 0:256], b("Ba", 128), b("aga", 256), False, True, 256, ["Ba"] + ["aga%d" % h for h in H], ["X3"])
+
+        def ya_out(x):
+            ya = T.YA[:, 512 * t + 256 * x:512 * t + 256 * x + 256]
+            if PAR["YA"][x] == "A":
+                act(f("yat", 256), T.X3[:, 256 * x:256 * x + 256], F.Relu, 78 + 256, ["X3"], ["yat"], bias=1.0 - OFFS - 8192)
+                act(ya, f("yat", 256), F.Identity, 78 + 256, ["yat"], ["YA%d%d" % (t, x)], bias=-1.0)
+            else:
+                ts(ya, T.X3[:, 256 * x:256 * x + 256], -OFFS - 8192, -1.0, A.add, A.max, 256, ["X3"], ["YA%d%d" % (t, x)])
+
+        ya_out(0)
         for h in H:
-            main("cb%d" % h, 0, N, "K%d" % h, "MN", "MG", "YRh", 16 * BW * h, yrt[h], PAR["CH"][NH - 1 - h],
-                 PAR["HELP"].get((t, 1, NH - 1 - h), 0), PAR["LAG"].get((t, 1, NH - 1 - h), 0))
+            main("cb%d" % h, 0, NS[h], "K%d" % h, "MN", "MG", "YRh", 256 * C0[h], yrt[h], PAR["CX"][1, h], PAR["CM"][1, h])
         tb = "b%d" % t
         LU, LL = ["lu%s%d" % (tb, h) for h in H], ["l%s%d" % (tb, h) for h in H]
         act(f("nn", 256), T.OC[:, 0:2048].indirect(u("lu" + tb, 16)), F.Copy, 78 + GA * 256, ["OC"] + OCP + LU, ["nn"])
-        act(b("lg", 256), T.MT[:, 0:2048].indirect(u("lu" + tb, 16)), F.Copy, 78 + GA * 256, ["MT"] + LU, ["lg"])
+        act(b("lg", 256), MT(0, 2048).indirect(u("lu" + tb, 16)), F.Copy, 78 + GA * 256, ["MT"] + LU, ["lg"])
         ts(f("ls" + tb, 16), i("l" + tb, 16), 1.0 / SC, None, A.mult, None, 16, LL, ["ls" + tb])
-        act(f("lb", 384), f("ls" + tb, 16).indirect(u("Boff", 24)), F.Identity, 78 + GA * 384, ["ls" + tb, "Boff"], ["lb"], bias=OFFS)
-        mm(T.PL[:, 0:384], b("ID", 128), b("C3", 384), True, False, 384, ["ID", "C3"], ["PL"])
+        act(f("lb", 384), f("ls" + tb, 16).indirect(u("Boff", 24)), F.Identity, 78 + GA * 384, ["ls" + tb, "Boff"], ["lb"], bias=OFFS - 8192, scale=SC)
+        mm(T.PL[:, 0:384], b("ID", 128), b("eqL", 384), True, False, 384, ["ID", "eqL"], ["PL"])
+        mm(T.PL[:, 0:384], b("ID", 128), b("gtL", 384), False, False, 384, ["ID", "gtL"], ["PL"])
         for mat, src in (("B0", nln), ("Ba", "lg")):
             mm(T.PL[:, 0:256], b(mat, 128), b(src, 256), False, False, 256, [mat, src], ["PL"])
             for c in range(8):
@@ -438,51 +527,63 @@ def build(g, T, dst_of, topo, core):
         for e, (lo, hi, st) in enumerate(((271, 384, 16), (31, 256, 32))):
             tt(f("Gl%d" % e, 8), b("Fl", 384, lo, hi, st), f("ls" + tb, 16, e, 16, 2), A.max, 8, ["Fl", "ls" + tb], ["Gl%d" % e])
             ts(u("no", 16, e, 16, 2), f("Gl%d" % e, 8), SC, f("dumL%d" % e, 1), A.mult, A.min, 8, ["Gl%d" % e, "dumL%d" % e], ["no%d" % e])
-        tt(f("dn", 256), T.DL[:, 256 * t:256 * t + 256], f("nn", 256), A.subtract, 256, DLT + ["nn"], ["dn"])
         box, land = T["box%d" % t], T["land%d" % t]
-        back = lambda c, a: slice(a + BW * (c // N) + c % N, a + BW * (c // N) + BW, N)
         for h in H:
-            tbh, a0, sh, K = "b%d%d" % (t, h), 16 * BW * h, str(h), "K%d" % h
-            sm = T.SM[:, BW * h:BW * h + BW]
-            c16 = lambda fn, name: fn(name, 16, N * h, N * h + N)
-            fp = lambda name: f(name, 256, BW * h, BW * h + BW)
-            mm(sm, b("ID", 128), b("MK", BW), True, False, BW, ["ID", "MK"], ["SM"])
-            mm(sm, b("B0l", 128), part(nlt, h), False, False, BW, ["B0l", nlt], ["SM"])
-            pick(tbh, N, K, "jB")
-            tg(part("y2n", h), T.MN[:, a0:a0 + 16 * BW].indirect(u("ku" + tbh, N)), part("y1T", h), A.subtract,
-               60 + GA * BW, toks("MN", a0) + ["ku" + tbh, "y1T"], ["y2n" + sh])
-            mm(sm, b("B1n", 128), part("y2n", h), False, True, BW, ["B1n", "y2n" + sh], ["SM"])
-            scan(fp("SR"), b("R0", 256, 0, BW), sm, A.mult, A.max, BW, ["R0", "SM"], ["SR" + sh])
-            tt(fp("K2"), f("IDX2", 256, 0, BW), T[K][:, 0:BW], A.subtract, BW, ["IDX2", K], ["K2" + sh], 1.0)
-            scan(fp("R2"), f("RB", 256, 0, BW), fp("K2"), A.add, A.min, BW, ["RB", "K2" + sh], ["R2" + sh])
-            cp(c16(i, "k2"), f("R2", 256, BW * h + 15, BW * h + BW, 16), N, ["R2" + sh], ["k2" + sh])
-            ts(c16(i, "k3"), c16(i, "k2"), 15, None, A.bitwise_and, None, N, ["k2" + sh], ["k3" + sh])
-            cp(c16(u, "k4"), c16(i, "k3"), N, ["k3" + sh], ["k4" + sh])
-            act(part("kg", h), f("seed", 64).indirect(c16(u, "k4")), F.Copy, 78 + GA * BW, ["seed", "k4" + sh], ["kg" + sh])
-            for c in range(N * h, N * h + N):
-                mm(T.PL[:, back(c, 256)], b("B2", 128), b("kg", 256, 16 * c, 16 * c + 16), True, True, 16, ["B2", "kg" + sh], ["PL"])
-            pl = T.PL[:, BW * h:BW * h + BW]
-            ts(pl, T.PL[:, 256 + BW * h:256 + BW * h + BW], f("j32", 1), None, A.is_equal, None, BW, ["PL", "j32"], ["PL"])
-            tt(fp("td"), pl, fp("dn"), A.mult, BW, ["PL", "dn"], ["td" + sh], 1.0)
-            for c in range(N * h + N - 2, N * h - 1, -2):
-                tg(T.OC[:, 0:2080].indirect(u("no", 16, c, c + 2)), f("nn", 256, 16 * c, 16 * c + 32), f("td", 256, 16 * c, 16 * c + 32),
-                   A.add, 60 + SCA * 32, ["no0", "no1", "nn", "td" + sh], ["OC"] + (OCP if t == 0 and c == 14 else []))
-        ts(b("rdy", 16), f("SR", 256, 15, 256, 16), f("th", 1), None, A.is_ge, None, 16, ["SR%d" % h for h in H] + ["th"], ["rdy"])
-        scan(b("Pp", 16), b("RN", 16), b("rdy", 16), A.mult, A.add, 16, ["RN", "rdy"], ["Pp"])
-        end = lambda x: b("Pp", 16, N * x + N - 1, N * x + N)
+            N, BW, L0, sh = NS[h], 16 * NS[h], 16 * C0[h], str(h)
+            sm = T.SM[:, L0:L0 + BW]
+            mm(sm, b("ID", 128), b("MK", WM, 0, BW), True, False, BW, ["ID", "MK"], ["SM"])
+            mm(sm, b("B0l", 128), part(nlt, h), False, False, BW, ["B0l"] + NT[h], ["SM"])
+            mm(sm, b("B1n", 128), part("y1T", h), False, True, BW, ["B1n"] + Y1T[h], ["SM"])
+            scan(f("SR", 256, L0, L0 + BW), b("R0", WM, 0, BW), sm, A.mult, A.max, BW, ["R0", "SM"], ["SR" + sh])
+            lin(f("Sc", 16, C0[h], C0[h] + N), f("SR", 256, L0 + 15, L0 + BW, 16), 1.0 / 256, f("n256", 1), N, ["SR" + sh, "n256"], ["Sc" + sh])
         for h in H:
+            N, BW, L0 = NS[h], 16 * NS[h], 16 * C0[h]
+            tbh, a0, sh, K = "b%d%d" % (t, h), 16 * L0, str(h), "K%d" % h
+            c16 = lambda fn, name: fn(name, 16, C0[h], C0[h] + N)
+            fp = lambda name: f(name, 256, L0, L0 + BW)
+            pick(tbh, N, K)
+            m2, src = part("mn2", h), T.MN[:, a0:a0 + 16 * BW].indirect(u("ku" + tbh, N))
+            either(lambda: act(m2, src, F.Copy, 78 + GA * BW, toks("MN", a0) + ["ku" + tbh], ["mn2" + sh]),
+                   lambda: op("V", lambda m2=m2, src=src: V.tensor_copy(m2, src), 60 + GA * BW, toks("MN", a0) + ["ku" + tbh], ["mn2" + sh]))
+            tt(c16(f, "Su"), f("R" + K, BW, 15, BW, 16), c16(f, "Sc"), A.add, N, ["R" + K, "Sc" + sh], ["Su" + sh])
+            ts(c16(i, "kb"), i("ki" + tbh, N), 1, None, A.bitwise_and, None, N, ["ki" + tbh], ["kb" + sh])
+            tt(c16(b, "rdy"), c16(f, "Su"), c16(i, "kb"), A.is_ge, N, ["Su" + sh, "kb" + sh], ["rdy" + sh])
+            scan(c16(b, "Pp"), b("R0", WM, 0, N), c16(b, "rdy"), A.mult, A.add, N, ["R0", "rdy" + sh], ["Pp" + sh])
+            tt(c16(b, "rD"), c16(b, "rdy"), c16(f, "D0"), A.mult, N, ["rdy" + sh, "D0" + sh], ["rD" + sh])
+            end = lambda x: b("Pp", 16, C0[x] + NS[x] - 1, C0[x] + NS[x])
+            a1 = T.SM[:, 272:272 + N]
+            for z, src in enumerate(("DD", "rD", "Pp")):
+                mm(a1, b("ID", 128), c16(b, src), z == 0, z == 2, N, ["ID", src + sh], ["SM"])
             for x in range(h + 1):
-                mm(T.SM[:, 256 + h:257 + h], b("TRI" if x == h else "B1", 128), end(x), x == 0, x == h, 1, ["TRI", "B1", "Pp"], ["SM"])
-        for x in range(NH):
-            mm(T.SM[:, 264:265], b("B1", 128), end(x), x == 0, x == NH - 1, 1, ["B1", "Pp"], ["SM"])
-        ts(f("nr", 16), f("SR", 256, 15, 256, 16), f("th", 1), None, A.is_lt, None, 16, ["SR%d" % h for h in H] + ["th"], ["nr"])
-        tt(f("nrD", 16), f("nr", 16), f("DD", 16), A.mult, 16, ["nr", "DD"], ["nrD"])
-        tt(f("a1", 16), b("Pp", 16), f("nrD", 16), A.add, 16, ["Pp", "nrD"], ["a1"])
-        for h in H:
-            ts(u("so", 16, N * h, N * h + N), f("a1", 16, N * h, N * h + N), T.SM[:, 256 + h:257 + h], -1.0, A.add, A.add, N, ["a1", "SM"], ["so%d" % h])
-        ts(box[:, 8:9], T.SM[:, 264:265], 64.0, None, A.min, None, 1, ["SM"], ["bc%d" % t])
-        op("V", lambda box=box: V.tensor_copy(box[:, 16:272].indirect(u("so", 16)), b("y2n", 256)), 60 + SCA * 256,
-           ["so%d" % h for h in H] + ["y2n%d" % h for h in H], ["box%d" % t])
+                mm(T.SM[:, 256:257], b("TRI" if x == h else "B1", 128), end(x), x == 0, x == h, 1, ["TRI", "B1", "Pp%d" % x], ["SM"])
+            if h == NH - 1:
+                for x in range(NH):
+                    mm(T.SM[:, 264:265], b("B1", 128), end(x), x == 0, x == NH - 1, 1, ["B1", "Pp%d" % x], ["SM"])
+            ts(c16(u, "so"), a1, T.SM[:, 256:257], -1.0, A.add, A.add, N, ["SM"], ["so" + sh])
+            if h == NH - 1:
+                ts(box[:, 8:9], T.SM[:, 264:265], 64.0, None, A.min, None, 1, ["SM"], ["bc%d" % t])
+            tg(box[:, 16:272].indirect(c16(u, "so")), m2, part("y1T", h), A.add, 60 + SCA * BW, ["so" + sh, "mn2" + sh] + Y1T[h], ["box%d" % t])
+            scan(fp("R2"), f("RC", WM, 0, BW), T[K][:, 0:BW], A.add, A.max, BW, ["RC", K], ["R2" + sh])
+            ts(c16(i, "k2"), f("R2", 256, L0 + 15, L0 + BW, 16), 1 / KS, BIG, A.mult, A.add, N, ["R2" + sh], ["k2" + sh])
+            ts(c16(i, "k3"), c16(i, "k2"), 1, 15, A.arith_shift_right, A.bitwise_and, N, ["k2" + sh], ["k3" + sh])
+            cp(c16(u, "k4"), c16(i, "k3"), N, ["k3" + sh], ["k4" + sh])
+            act(part("kg", h), b("OH", 16).indirect(c16(u, "k4")), F.Copy, 78 + GA * BW, ["OH", "k4" + sh], ["kg" + sh])
+            p0, p1 = 2 * L0, 2 * L0 + 2 * BW
+            for x, mat in enumerate(("I8", "I8n")):
+                o = T.PL[:, p0 + BW * x:p0 + BW * x + BW]
+                if x == 0:
+                    mm(o, f("G8", 128)[0:8, :], T.DF[0:8, 256 * t + L0:256 * t + L0 + BW], True, False, BW, ["G8", "DF0"], ["PL"], 4.0)
+                else:
+                    mm(o, f("IF", 128), fp("nn"), True, False, BW, ["IF", "nn"], ["PL"], 4.0)
+                for c in range(N):
+                    mm(T.PL[:, p0 + BW * x + c:p0 + BW * x + BW:N], b(mat, 128), b("kg", 256, L0 + 16 * c, L0 + 16 * c + 16), False, c == N - 1, 16,
+                       [mat, "kg" + sh], ["PL"])
+            either(lambda: act(f("pv", 512, p0, p1), T.PL[:, p0:p1], F.Relu, 78 + 2 * BW, ["PL"], ["pv" + sh]),
+                   lambda: ts(f("pv", 512, p0, p1), T.PL[:, p0:p1], 0.0, None, A.max, None, 2 * BW, ["PL"], ["pv" + sh]))
+        for c in range(14, -1, -2):
+            p0, BW = 16 * (c + C0[hof[c]]), 16 * NS[hof[c]]
+            tg(T.OC[:, 0:2080].indirect(u("no", 16, c, c + 2)), f("pv", 512, p0, p0 + 32), f("pv", 512, p0 + BW, p0 + BW + 32),
+               A.add, 60 + SCA * 32, ["no0", "no1", "pv%d" % hof[c]], ["OC"] + (OCP if t == 0 and c == 14 else []))
         dst = dst_of(t)
         rid, pid, _ = topo.addr(dst)
         m = 0
@@ -493,78 +594,104 @@ def build(g, T, dst_of, topo, core):
         if t + 2 < S:
             rep0(t + 2)
         for h in H:
-            mark("b%d%d" % (t, h), N, "MG", 16 * BW * h, sub(nlt, h), nlt, sub("agb", h), str(h))
+            mark("b%d%d" % (t, h), NS[h], "MG", 256 * C0[h], sub(nlt, h), NT[h], sub("agb", h), str(h), "X%d" % h)
         if t == S - 1:
             dma("S", T.yo[:], T.OC[:, 0:2048], ["OC"], ["yo"], 5000)
-        mm(T.X3[:, 256:512], b("ID", 128), b("OF", 256), True, False, 256, ["ID", "OF"], ["X3"])
-        mm(T.X3[:, 256:512], b("B0n", 128), b(nln, 256), False, False, 256, ["B0n", nln], ["X3"])
+            for k in range(8):
+                rep("AVG", T.YM[:, 32 + 512 * k:544 + 512 * k], MT(512 * k, 512 * k + 512), 1.0, 512, ["MT"], ["YM%d" % k] + ["mk"] * (k == 0), 1.0)
+        mm(T.X3[:, 256:512], b("B0n", 128), b(nln, 256), True, False, 256, ["B0n", nln], ["X3"])
         for c in range(16):
-            mm(T.X3[:, back(c, 256)], b("Ba", 128), b("agb", 256, 16 * c, 16 * c + 16), False, c == 15, 16, ["Ba", "agb%d" % (c // N)], ["X3"])
-        for x in range(2):
-            ya = T.YA[:, 512 * t + 256 * x:512 * t + 256 * x + 256]
-            if PAR["YA"][x] == "A":
-                act(f("yat", 256), T.X3[:, 256 * x:256 * x + 256], F.Relu, 78 + 256, ["X3"], ["yat"], bias=1.0, scale=SC)
-                act(ya, f("yat", 256), F.Identity, 78 + 256, ["yat"], ["YA%d%d" % (t, x)], bias=-1.0)
-            else:
-                ts(ya, T.X3[:, 256 * x:256 * x + 256], SC, -1.0, A.mult, A.max, 256, ["X3"], ["YA%d%d" % (t, x)])
+            mm(T.X3[:, back(c, 256)], b("Ba", 128), b("agb", 256, 16 * c, 16 * c + 16), False, c == 15, 16, ["Ba", "agb%d" % hof[c]], ["X3"])
+        ya_out(1)
         dma("S", T.ya[:, 512 * t:512 * t + 512], T.YA[0:128:16, 512 * t:512 * t + 512], ["YA%d0" % t, "YA%d1" % t], ["ya%d" % t], 2000)
         lt = ["land%d" % t]
-        mm(T.PU[:, 0:64], b("ID", 128), b("MK", BW, 0, 64), True, False, 64, ["ID", "MK"], ["PU"])
-        mm(T.PU[:, 0:64], b("Bwn", 128), land[:, 16:80], False, True, 64, ["Bwn"] + lt, ["PU"])
-        scan(f("UR", 64), b("R0", 256, 0, 64), T.PU[:, 0:64], A.mult, A.max, 64, ["R0", "PU"], ["UR"])
-        square(tr, f("UR", 64, 15, 64, 16), "UR", 4)
+        u_part(tr, lambda j: land[:, 16 + j:80:16], lt, "Zn", 4)
         yr = ["YRr%d" % k for k in range(16)]
+        rep("AV", b("yrp", 64), land[:, 16:80], -1.0, 64, lt, ["yrp"])
         for k in range(16):
-            rep(PAR["REPR"][k], T.YRr[:, k:1024:16], land[:, 16:80], -1.0, 64, lt, [yr[k]])
+            if k < PAR["REPR"]:
+                rep("GAV", T.YRr[:, k:1024:16], b("yrp", 64), 1.0, 64, ["yrp"], [yr[k]])
+            else:
+                rep("AV", T.YRr[:, k:1024:16], land[:, 16:80], -1.0, 64, lt, [yr[k]])
         place(tr, 4, "A%d" % t, t, "cr", tr, 0)
-        ts(b("NR", 64), f("SLOT", 64), land[:, 8:9], None, A.is_ge, None, 64, ["SLOT"] + lt, ["NR"])
+        ts(b("NR", 64), f("SLOT", 64), land[:, 8:9], None, A.is_lt, None, 64, ["SLOT"] + lt, ["NR"])
         if t + 1 < S:
             an = "A%d" % (t + 1)
-            mm(T.PU[:, 64:65], b("ON", 128), land[:, 8:9], True, True, 1, ["ON"] + lt, ["PU"])
-            cp(i("ai", 1), T.PU[:, 64:65], 1, ["PU"], ["ai"])
+            mm(T.SM[:, 300:301], b("ON", 128), land[:, 8:9], True, True, 1, ["ON"] + lt, ["SM"])
+            cp(i("ai", 1), T.SM[:, 300:301], 1, ["SM"], ["ai"])
             ts(i("aj", 1), i("ai", 1), 63, None, A.bitwise_and, None, 1, ["ai"], ["aj"])
-            ts(f(an, 1), i("aj", 1), -0.375, None, A.add, None, 1, ["aj"], [an])
+            ts(f(an, 1), i("aj", 1), AOFF, None, A.add, None, 1, ["aj"], [an])
             place0(t + 1)
-        main("cr", 0, 4, "Kr", "MNr", "MGr", "YRr", 0, yr, PAR["CHR"], 0, PAR["LAGR"])
-        pick(tr, 4, "Kr", "j64")
-        mark(tr, 4, "MGr", 0, lambda x, y: b("NR", 64, x, y), "NR", lambda x, y: b("agr", 64, x, y), "r")
-    dma("G", T.ym[:], T.MT[0:128:16, 0:4096], ["MT"], ["ym"], 2500)
+        main("cr", 0, 4, "SM", "MNr", "MGr", "YRr", 0, yr, PAR["CXR"], PAR["CMR"])
+        pick(tr, 4, "SM")
+        mark(tr, 4, "MGr", 0, lambda x, y: b("NR", 64, x, y), ["NR"], lambda x, y: b("agr", 64, x, y), "r", "X0", t == S - 1)
+    dma("S", T.ym[:], T.YM[0:128:16, 32:4128], ["YM"], ["ym"], 2000)
     return ops
 
 
 def graph(ops):
-    lastw, readers, bank = {}, {}, {}
+    lastw, readers, bank, opened = {}, {}, {}, {}
     deps = []
     for k, o in enumerate(ops):
         d = set()
         for x in o["r"] + o["w"]:
             if x in lastw and x[0] != "~":
-                d.add(lastw[x])
+                if o["acc"] is not None and x in BANKS:
+                    d.add(opened.setdefault(o["acc"], lastw[x][0]))
+                else:
+                    d.update(lastw[x])
         for x in o["w"]:
             d.update(readers.get(x, ()))
         d = {a: not (ops[a]["e"] == "P" and o["e"] == "P") for a in d}
         for x in sorted(set(o["r"] + o["w"])):
-            if x in BANKS or x[0] == "~":
+            if x[0] == "~":
                 if x in bank:
-                    d.setdefault(bank[x], ops[bank[x]]["e"] != o["e"])
+                    d.setdefault(bank[x], False)
                 bank[x] = k
+            elif x in BANKS and o["acc"] is None:
+                e = "?" if o["alt"] else o["e"]
+                was, now, before = bank.get(x, ("", [], []))
+                if e == was == "V":
+                    now.append(k)
+                else:
+                    before, bank[x] = now, (e, [k], now)
+                for a in before:
+                    d.setdefault(a, not (e == was and e in "PA"))
         for x in o["r"]:
             readers.setdefault(x, []).append(k)
         for x in o["w"]:
-            lastw[x] = k
+            lastw[x] = lastw[x] + [k] if o["acc"] is not None else [k]
             readers[x] = []
         d.pop(k, None)
         deps.append(d)
+    for t in range(S):
+        for x, nx, y, ny in PAR["FIRST"]:
+            a = [k for k, o in enumerate(ops) if o["t"] == t and o["w"][0].startswith(x)]
+            c = [k for k, o in enumerate(ops) if o["t"] == t and o["w"][0].startswith(y)]
+            if len(a) > nx and len(c) > ny:
+                deps[c[ny]].setdefault(a[nx], False)
     return deps
 
 
-def place_all(ops, pred, key, first):
-    start = [0.0] * len(ops)
-    busy = {e: [] for e in "VAPGS"}
-    for k in sorted(range(len(ops)), key=key):
-        c = ops[k]["c"]
-        s = max([first[k]] + [start[a] + ops[a]["c"] + d for a, d in pred[k]])
-        iv = busy[ops[k]["e"]]
+def plan(ops, deps, others):
+    n = len(ops)
+    pred = [[(a, (ops[a]["lat"] + PAR["SIG"]) if w else 0.0) for a, w in deps[k].items()] for k in range(n)]
+    succ = [[] for _ in range(n)]
+    for k in range(n):
+        for a, d in pred[k]:
+            succ[a].append((k, d))
+    lat = [o["lat"] for o in ops]
+    alts = [[(e, c) for e, c, _ in o["alt"]] for o in ops]
+    eng, cost = [o["e"] for o in ops], [o["c"] for o in ops]
+    names = [o["w"][0].rstrip("0123456789_") for o in ops]
+    weight = [1.0 if o["e"] in "GS" else o["c"] for o in ops]
+    seed = [PAR["SEED"]]
+
+    def rnd():
+        seed[0] = (seed[0] * 1103515245 + 12345) % 2147483648
+        return seed[0] / 2147483648.0
+
+    def gap(iv, s, c):
         lo, hi = 0, len(iv)
         while lo < hi:
             mid = (lo + hi) // 2
@@ -573,68 +700,161 @@ def place_all(ops, pred, key, first):
             else:
                 hi = mid
         while lo < len(iv) and iv[lo][0] < s + c:
-            s = max(s, iv[lo][1])
+            if iv[lo][1] > s:
+                s = iv[lo][1]
             lo += 1
-        iv.insert(lo, (s, s + c))
-        start[k] = s
-    return start
+        return s, lo
 
+    def place(win, val, start, eng, cost, busy, price):
+        for k in win:
+            for a, _ in pred[k]:
+                if a in val and val[a] > val[k]:
+                    val[k] = val[a]
+        for k in sorted(win, key=lambda k: (val[k], k)):
+            s = 0.0
+            for a, d in pred[k]:
+                x = start[a] + cost[a] + d
+                if x > s:
+                    s = x
+            if price is not None and alts[k]:
+                eng[k], cost[k] = min(alts[k], key=lambda z: gap(busy[z[0]], s, z[1])[0] + z[1] * price[z[0]])
+            iv = busy[eng[k]]
+            s, lo = gap(iv, s, cost[k])
+            iv.insert(lo, (s, s + cost[k]))
+            start[k] = s
 
-def order_key(pred, val):
-    val = list(val)
-    for k in range(len(val)):
-        for a, _ in pred[k]:
-            if val[k] < val[a]:
-                val[k] = val[a]
-    return lambda k: (val[k], k)
+    def settle(start, order):
+        free = dict.fromkeys("VAPGS", 0.0)
+        for k in order:
+            s = free[eng[k]]
+            for a, d in pred[k]:
+                x = start[a] + cost[a] + d
+                if x > s:
+                    s = x
+            start[k] = s
+            free[eng[k]] = s + cost[k]
+        tail = [0.0] * n
+        free = dict.fromkeys("VAPGS", 0.0)
+        for k in reversed(order):
+            s = max(lat[k], free[eng[k]])
+            for a, d in succ[k]:
+                x = tail[a] + d
+                if x > s:
+                    s = x
+            tail[k] = free[eng[k]] = s + cost[k]
+        return tail
 
+    def length(win, out, first, st, en, co):
+        ends = sorted(st[k] + co[k] + max(out[k], first[en[k]]) for k in win)
+        top = ends[-PAR["TOP"]:]
+        early = sum(weight[k] * (st[k] + co[k]) for k in win) / sum(weight[k] for k in win)
+        return ends[-1] + PAR["SOFT"] * sum(top) / len(top) + PAR["EARLY"] * early
 
-def plan(ops, deps):
-    n = len(ops)
-    pred = [[(a, (ops[a]["lat"] + PAR["SIG"]) if w else 0.0) for a, w in deps[k].items()] for k in range(n)]
-    succ = [[] for _ in range(n)]
-    for k in range(n):
-        for a, d in pred[k]:
-            succ[a].append((k, d))
-    lat = [o["lat"] for o in ops]
-    zero = [0.0] * n
-    back = [0.0] * n
+    hint = [list(x) for x in succ]
+    for kind in ("MN", "MG"):
+        run = [k for k in range(n) if names[k] in (kind, kind + "r")]
+        for a, k in zip(run, run[1:]):
+            hint[a].append((k, -PAR["HINT"][kind] * cost[a]))
+    tail = [0.0] * n
     for k in range(n - 1, -1, -1):
-        back[k] = max([lat[k]] + [back[x] + ops[x]["c"] + d for x, d in succ[k]])
-    seed = [PAR["SEED"]]
-
-    def rnd():
-        seed[0] = (seed[0] * 1103515245 + 12345) % 2147483648
-        return seed[0] / 2147483648.0
-
-    def fwd(val):
-        fw = place_all(ops, pred, order_key(pred, val), zero)
-        return max(fw[k] + ops[k]["c"] + lat[k] for k in range(n)), fw
-
-    def again(fw):
-        bw = place_all(ops, succ, lambda k: (-(fw[k] + ops[k]["c"]), -k), lat)
-        return fwd([-(bw[k] + ops[k]["c"]) for k in range(n)])
-
-    best = fwd([-(back[k] + ops[k]["c"]) for k in range(n)])
-    names = [o["w"][0].rstrip("0123456789_") for o in ops]
-    for _ in range(PAR["ROUNDS"]):
-        t0, wd, amp = rnd() * best[0], 2000 + 10000 * rnd(), PAR["NOISE"] * (0.2 + 3 * rnd() ** 2)
-        sh = {}
-        val = []
+        tail[k] = cost[k] + max([lat[k]] + [tail[x] + d for x, d in hint[k]])
+    start = [0.0] * n
+    place(range(n), {k: -tail[k] for k in range(n)}, start, eng, cost, {e: [] for e in "VAPGS"}, {"V": 2.0, "A": 1.0, "G": 1.0})
+    order = sorted(range(n), key=lambda k: (start[k], k))
+    tail = settle(start, order)
+    span = max(tail)
+    more = []
+    for o2, sig in others:
+        cs = [dict([(o["e"], o["c"])] + [(e, c) for e, c, _ in o["alt"]]) for o in o2]
+        pr = [[(a, (lat[a] + sig) if w else 0.0) for a, w in deps[k].items()] for k in range(n)]
+        su = [[] for _ in range(n)]
         for k in range(n):
-            s = best[1][k]
-            if t0 <= s < t0 + wd:
-                if names[k] not in sh:
-                    sh[names[k]] = amp * (rnd() - 0.5) if rnd() < 0.4 else 0.0
-                s += sh[names[k]]
-            val.append(s)
-        c = fwd(val)
-        if c[0] < best[0] + 600:
-            c2 = again(c[1])
-            if c2[0] < c[0]:
-                c = c2
-        if c[0] <= best[0]:
-            best = c
+            for a, d in pr[k]:
+                su[a].append((k, d))
+        more.append({"c": cs, "pred": pr, "succ": su})
+
+    def forward(z, seq, en, end, free):
+        for k in seq:
+            s = free[en[k]]
+            for a, d in z["pred"][k]:
+                if end[a] + d > s:
+                    s = end[a] + d
+            end[k] = free[en[k]] = s + z["c"][k][en[k]]
+
+    def settle_more():
+        for z in more:
+            z["end"], z["tail"] = [0.0] * n, [0.0] * n
+            forward(z, order, eng, z["end"], dict.fromkeys("VAPGS", 0.0))
+            free, tl = dict.fromkeys("VAPGS", 0.0), z["tail"]
+            for k in reversed(order):
+                s = max(lat[k], free[eng[k]])
+                for a, d in z["succ"][k]:
+                    if tl[a] + d > s:
+                        s = tl[a] + d
+                tl[k] = free[eng[k]] = s + z["c"][k][eng[k]]
+        return sum(max(z["tail"]) for z in more) * PAR["WELSE"]
+
+    def length_more(seq, st, en):
+        x = 0.0
+        seq = sorted(seq, key=lambda k: (st[k], k))
+        for z in more:
+            end = list(z["end"])
+            forward(z, seq, en, end, dict(z["free"]))
+            x += max(end[k] + max(z["out"][k], z["first"][en[k]]) for k in seq)
+        return x * PAR["WELSE"]
+
+    best = (span + settle_more(), list(start), list(eng), list(cost), span)
+    R = PAR["ROUNDS"]
+    for r in range(R):
+        m = int(PAR["WIN"] * (0.4 + rnd()))
+        i0 = max(0, int(rnd() * (n + m // 2)) - m // 2)
+        win, rest = sorted(order[i0:i0 + m]), order[i0 + m:]
+        held = {e: [(-1.0, start[order[max(0, i0 - 100)]])] for e in "VAPGS"}
+        for k in order[max(0, i0 - 100):i0]:
+            held[eng[k]].append((start[k], start[k] + cost[k]))
+        t2, out, first = {}, {}, dict.fromkeys("VAPGS", 0.0)
+        for k in reversed(rest[:200]):
+            first[eng[k]] = tail[k]
+        for k in reversed(win):
+            t2[k] = cost[k] + max([lat[k]] + [t2.get(a, tail[a]) + d for a, d in hint[k]])
+            out[k] = max([lat[k]] + [tail[a] + d for a, d in succ[k] if a not in t2])
+        seq = order[max(0, i0 - 100):i0 + m]
+        inside = set(order[:i0 + m])
+        for z in more:
+            z["free"], z["first"] = dict.fromkeys("VAPGS", 0.0), dict.fromkeys("VAPGS", 0.0)
+            for k in order[max(0, i0 - 400):max(0, i0 - 100)]:
+                z["free"][eng[k]] = z["end"][k]
+            for k in reversed(rest[:200]):
+                z["first"][eng[k]] = z["tail"][k]
+            z["out"] = {k: max([lat[k]] + [z["tail"][a] + d for a, d in z["succ"][k] if a not in inside]) for k in seq}
+        now = length(win, out, first, start, eng, cost)
+        bound = now + length_more(seq, start, eng) + PAR["TEMP"] * (1 - r / R) * rnd()
+        pick = None
+        for _ in range(PAR["TRIES"]):
+            mode, amp, mix, w2 = rnd(), PAR["NOISE"] * (0.1 + 2 * rnd() ** 2), rnd(), PAR["W2"] * rnd() ** 2
+            sh, val = {}, {}
+            for k in win:
+                key = names[k] if mode < 0.6 else k
+                if key not in sh:
+                    sh[key] = amp * (rnd() - 0.5) if rnd() < 0.3 else 0.0
+                val[k] = (1 - w2) * (mix * start[k] + (1 - mix) * (span - tail[k])) + w2 * (span - t2[k]) + sh[key]
+            price = {"V": 1 + 4 * rnd() ** 2, "A": 1 + 2 * rnd() ** 2, "G": 1.5 * rnd()} if rnd() < PAR["PICK"] else None
+            s2, e2, c2 = list(start), list(eng), list(cost)
+            place(win, val, s2, e2, c2, {e: list(v) for e, v in held.items()}, price)
+            x = length(win, out, first, s2, e2, c2)
+            if x < now + PAR["SKIP"]:
+                x += length_more(seq, s2, e2)
+                if x <= bound:
+                    bound, pick = x, (s2, e2, c2)
+        if pick:
+            start, eng[:], cost[:] = pick
+            order = sorted(order[:i0 + m], key=lambda k: (start[k], k)) + rest
+            tail = settle(start, order)
+            order.sort(key=lambda k: (start[k], k))
+            span = max(tail)
+            x = span + settle_more()
+            if x < best[0]:
+                best = (x, list(start), list(eng), list(cost), span)
     return best
 
 
@@ -646,12 +866,19 @@ def rank_program(g, core, T, topo):
     if rank is None:
         return
     n = len(T.cores)
-    ops = build(g, T, lambda t: T.cores[(rank + 1 + t % (n - 1)) % n], topo, core)
+    dst_of = lambda t: T.cores[(rank + 1 + t % (n - 1)) % n]
+    ops = build(g, T, dst_of, topo, core, PAR)
     deps = graph(ops)
     if "start" not in PLAN:
-        PLAN["start"] = plan(ops, deps)[1]
+        others = [(build(g, T, dst_of, topo, core, dict(PAR, **z)), z["SIG"]) for z in PAR["ELSE"]]
+        PLAN["start"], PLAN["eng"] = plan(ops, deps, others)[1:3]
     start = PLAN["start"]
+    for o, e in zip(ops, PLAN["eng"]):
+        for e2, _, fn in o["alt"]:
+            if e2 == e:
+                o["e"], o["fn"] = e, fn
     order = sorted(range(len(ops)), key=lambda k: (start[k], k))
+    closes = {ops[k]["acc"]: k for k in order}
     need = set(a for d in deps for a, w in d.items() if w)
     queue = {"V": g.vector, "A": g.scalar, "P": g.tensor, "G": g, "S": g.sync}
     total = {}
@@ -679,7 +906,7 @@ def rank_program(g, core, T, topo):
                 for s2, v2 in clock[a].items():
                     if kn.get(s2, 0) < v2:
                         kn[s2] = v2
-        ins = o["fn"]()
+        ins = o["fn"]() if o["acc"] is None else o["fn"](closes[o["acc"]] == k)
         remote = o["dma"] is not None and o["dma"].startswith("arr")
         clock[k] = {} if remote else dict(kn)
         if o["dma"] is not None:

from concourse.mybir import AluOpType, ActivationFunctionType

A = AluOpType
F = ActivationFunctionType
W, L, S = 4096, 2048, 3

SCRATCH = {
    "X": ("sbuf", [128, 4096], "bfloat16"),
    "OCI": ("sbuf", [128, 2048], "int32"),
    "OC": ("sbuf", [128, 2080], "float32"),
    "MT": ("sbuf", [128, 4160], "float32"),
    "YM": ("sbuf", [128, 4160], "bfloat16"),
    "DF": ("sbuf", [128, 784], "float32"),
    "MN": ("sbuf", [128, 4096], "bfloat16"),
    "MG": ("sbuf", [128, 4096], "bfloat16"),
    "MNr": ("sbuf", [128, 1024], "bfloat16"),
    "MGr": ("sbuf", [128, 1024], "bfloat16"),
    "YR0": ("sbuf", [128, 4096], "bfloat16"),
    "YR1": ("sbuf", [128, 4096], "bfloat16"),
    "YR2": ("sbuf", [128, 4096], "bfloat16"),
    "YRh": ("sbuf", [128, 4096], "bfloat16"),
    "YRr": ("sbuf", [128, 1024], "bfloat16"),
    "DL": ("sbuf", [128, 784], "int32"),
    "WI": ("sbuf", [128, 8], "int32"),
    "YA": ("sbuf", [128, 1536], "float32"),
    "box0": ("sbuf", [128, 528], "bfloat16"),
    "box1": ("sbuf", [128, 528], "bfloat16"),
    "box2": ("sbuf", [128, 528], "bfloat16"),
    "land0": ("sbuf", [128, 80], "bfloat16"),
    "land1": ("sbuf", [128, 80], "bfloat16"),
    "land2": ("sbuf", [128, 80], "bfloat16"),
    "AF": ("sbuf", [128, 8192], "float32"),
    "AB": ("sbuf", [128, 14336], "bfloat16"),
    "AI": ("sbuf", [128, 2048], "int32"),
    "AU": ("sbuf", [128, 4096], "uint16"),
    "K0": ("psum", [128, 512], "float32"),
    "K1": ("psum", [128, 512], "float32"),
    "X0": ("psum", [128, 512], "float32"),
    "X1": ("psum", [128, 512], "float32"),
    "PU": ("psum", [128, 512], "float32"),
    "X3": ("psum", [128, 512], "float32"),
    "PL": ("psum", [128, 512], "float32"),
    "SM": ("psum", [128, 512], "float32"),
}
SEMAPHORES = ["cV", "cA", "cP", "cG", "sent", "arr0", "arr1", "arr2"] + ["d%d" % i for i in range(24)]

BANKS = ("K0", "K1", "X0", "X1", "PU", "X3", "PL", "SM")
SC = 16384.0
OFFS = 2080.0
Z2 = 1.28125
BIG = 2097152.0
KS = 1.0 / 131072
AOFF = -10952.390625
PAR = {
    "NS": [10, 6],
    "CX": {(0, 0): [1, 1, 2, 2, 2, 4, 4], (0, 1): [1] * 12 + [2, 2], (1, 0): [2, 2, 4, 4, 4], (1, 1): [6, 6, 2, 2]},
    "CM": {(0, 0): [4, 4, 4, -2, -2], (0, 1): [4, 4, 4, 2, 2], (1, 0): [4, 4, 4, 2, 2], (1, 1): [4, 4, 4, 2, 2]},
    "CX0": [[6, 6, 4], [6, 6, 2, 2]], "CM0": [[4, 4, 4, 2, 2], [6, 6, 2, 2]],
    "CXR": [6, 6, 2, 2], "CMR": [6, 6, 2, 2],
    "REP": [8, 12], "REPR": 8, "NT": "A", "Y1T": "G", "YA": "AA", "ORD": False,
    "SIG": 220.0, "GA": 1.56, "SCA": 3.8, "PE": 0.45, "GF": 1.0, "UV": "ar", "ODD": 6,
    "ELSE": [{"GA": 1.1, "SCA": 2.5, "SIG": 160.0, "PE": 0.5}, {"GA": 1.9, "SCA": 5.0, "SIG": 300.0, "PE": 0.45}],
    "ROUNDS": 3400, "SEED": 1, "NOISE": 800.0, "TEMP": 60.0, "WIN": 200, "W2": 1.0, "PICK": 0.5, "WELSE": 0.5, "SKIP": 300.0,
    "TRIES": 5, "TOP": 12, "SOFT": 0.1, "EARLY": 0.05, "HINT": {"MN": 0.0, "MG": 0.2},
    "FIRST": [("ca", 0, "MNr", 0)],
}
NENG = 8


def build(g, T, dst_of, topo, core, PAR):
    ops = []
    now = [-1]
    arena = {}
    fill = {"AF": 0, "AB": 0, "AI": 0, "AU": 0}
    NS, GA, SCA = PAR["NS"], PAR["GA"], PAR["SCA"]
    NH, WM = len(NS), 16 * max(NS)
    H = list(range(NH))
    C0 = [sum(NS[:h]) for h in H]
    hof = [h for h in H for _ in range(NS[h])]

    def ap(kind, name, n, a=0, b=None, st=1):
        if name not in arena:
            arena[name] = fill[kind]
            fill[kind] += (n + 15) // 16 * 16
        o = arena[name]
        b = n if b is None else b
        return T[kind][:, o + a:o + b:st] if st != 1 else T[kind][:, o + a:o + b]

    def op(eng, fn, cost, r=(), w=(), lat=0.0, dma=None, acc=None):
        cost *= PAR["GF"] if eng == "G" else 1.0
        ops.append({"e": eng, "fn": fn, "c": cost, "r": list(r), "w": list(w), "lat": lat, "dma": dma, "acc": acc, "alt": [], "t": now[0]})

    def either(*calls):
        for c in calls:
            c()
        o = ops[-len(calls)]
        o["alt"] = [(x["e"], x["c"], x["fn"]) for x in ops[-len(calls):]]
        del ops[len(ops) - len(calls) + 1:]

    V, Ac, P = g.vector, g.scalar, g.tensor

    def ts(out, in0, s1, s2, o0, o1, n, r, w, f=1.0):
        if o1 is None:
            op("V", lambda: V.tensor_scalar(out, in0, s1, None, o0), max(64, n * f), r, w)
        else:
            op("V", lambda: V.tensor_scalar(out, in0, s1, s2, o0, o1), max(64, n * f), r, w)

    def tt(out, a, b, o, n, r, w, f=2.0):
        op("V", lambda: V.tensor_tensor(out, a, b, o), max(64, n * f), r, w)

    def tg(out, a, b, o, c, r, w):
        op("V", lambda: V.tensor_tensor(out, a, b, o), c, r, w)

    def cp(out, a, n, r, w, f=1.0):
        op("V", lambda: V.tensor_copy(out, a), max(64, n * f), r, w)

    def scan(out, d0, d1, o0, o1, n, r, w, f=1.0):
        op("V", lambda: V.tensor_tensor_scan(out, d0, d1, 0.0, o0, o1), max(64, n * f), r, w)

    def ms(a, v, n, w):
        op("V", lambda: V.memset(a, v), max(64, n), [], w)

    def act(out, a, fn, c, r, w, bias=0.0, scale=1.0):
        kw = {}
        if not (isinstance(bias, float) and bias == 0.0):
            kw["bias"] = bias
        if not (isinstance(scale, float) and scale == 1.0):
            kw["scale"] = scale
        op("A", lambda: Ac.activation(out, a, fn, **kw), c, r, w)

    def rep(eng, out, a, sign, n, r, w, f=0.5):
        if len(eng) > 1:
            either(*[lambda e=e: rep(e, out, a, sign, n, r, w, f) for e in eng])
        elif eng == "V":
            ts(out, a, sign, None, A.mult, None, n, r, w, f)
        elif eng == "A":
            act(out, a, F.Copy, 78 + n, r, w, scale=sign)
        else:
            op("G", lambda: g.affine_select(out, a, [[0, n]], A.is_gt, 0.0, 1, 0), 200 + 2 * n, r, w)

    def mm(out, l, rh, st, sp, n, r, w, f=1.0):
        fn, c = (lambda: P.matmul(out, l, rh, st, sp)), max(64, n) * PAR["PE"] * f + 8
        o = ops[-1]
        if o["e"] == "P" and o["acc"] is None and o["r"] == list(r) and o["w"] == list(w) and o["n"] < 16:
            o["fn"] = lambda a=o["fn"]: (a(), fn())[1]
            o["c"] += c
            o["n"] += 1
        else:
            op("P", fn, c, r, w)
            ops[-1]["n"] = 1

    nacc = [0]

    def mma(out, pairs, n, r, w):
        fn = lambda sp: [P.matmul(out, l, rh, False, sp and z == len(pairs) - 1) for z, (l, rh) in enumerate(pairs)][-1]
        op("P", fn, len(pairs) * (max(64, n) * PAR["PE"] + 8), r, w, acc=nacc[0])

    def iota(out, pat, n, w, cm=0, fl=True):
        if fl:
            op("G", lambda: g.iota(out, pat, 0, cm, allow_small_or_imprecise_dtypes=True), 150 + 2 * n, [], w)
        else:
            op("G", lambda: g.iota(out, pat, 0, cm), 150 + 2 * n, [], w)

    nd = [0]

    def dma(eng, out, in_, r, w, lat, grp=None):
        if grp is None:
            grp = "d%d" % nd[0]
            nd[0] += 1
        q = {"S": g.sync, "A": g.scalar, "G": g}[eng]
        op(eng, lambda: q.dma_start(out, in_), 900 if eng == "G" else 60, r, list(w) + ["~" + eng], lat=lat, dma=grp)

    f = lambda name, n, *a: ap("AF", name, n, *a)
    b = lambda name, n, *a: ap("AB", name, n, *a)
    i = lambda name, n, *a: ap("AI", name, n, *a)
    u = lambda name, n, *a: ap("AU", name, n, *a)
    MT = lambda x, y: T.MT[:, 32 + x:32 + y]

    dma("S", T.X[:, 3328:4096], T.xc[:, 3328:4096], [], ["Xl"], 2200)
    dma("A", T.WI[:, 0:1], T.wt[:], [], ["WI"], 2000)
    dma("A", T.YM[0:8, 0:4096], T.mk[:], [], ["mk"], 2400)
    dma("S", T.OCI[:, 0:1024], T.oc[:, 0:1024], [], ["OCI0"], 3800)
    dma("S", T.OCI[:, 1024:2048], T.oc[:, 1024:2048], [], ["OCI1"], 5400)
    dma("S", T.X[:, 0:3328], T.xc[:, 0:3328], [], ["Xr"], 8000)
    dma("A", T.DL[0:8, 0:768], T.dl[:], [], ["DL0"], 2200, "d23")
    dma("A", T.DL[0:8, 776:777], T.th[:], [], ["DL1"], 2200, "d23")

    iota(i("pi", 1), [[0, 1]], 1, ["pi"], 1, False)
    iota(f("I144", 144), [[1, 144]], 144, ["I144"])
    iota(f("IG", 128), [[16, 8], [0, 16]], 128, ["IG"])
    iota(f("II", 256), [[0, 16], [1, 16]], 256, ["II"])
    iota(b("I32", WM), [[32, WM // 16], [0, 16]], WM, ["I32"])
    iota(f("SLOT", 64), [[1, 4], [4, 16]], 64, ["SLOT"])
    ts(i("ji", 1), i("pi", 1), 15, None, A.bitwise_and, None, 1, ["pi"], ["ji"])
    ts(i("gi", 1), i("pi", 1), 112, None, A.bitwise_and, None, 1, ["pi"], ["gi"])

    def col(name, src, s1, o0):
        ts(f(name, 1), i(src, 1), s1, None, o0, None, 1, [src], [name])

    def lin(out, a, scale, bias, n, r, w):
        either(lambda: ts(out, a, scale, bias, A.mult, A.add, n, r, w), lambda: act(out, a, F.Identity, 78 + n, r, w, bias=bias, scale=scale))

    def acol(name, src, scale, bias, dep=()):
        lin(f(name, 1), f(src, 1), scale, bias, 1, [src] + list(dep), [name])

    col("g15", "gi", 15.0, A.add)
    col("jf", "ji", 1.0, A.mult)
    col("r0", "ji", 0.0, A.is_equal)
    col("r1", "ji", 1.0, A.is_equal)
    col("r2", "ji", 2.0, A.is_equal)
    col("r3", "ji", 3.0, A.is_equal)
    acol("gf", "g15", 1.0, -15.0)
    for n in sorted(set(NS + [4])):
        acol("jB%d" % n, "jf", 16.0 * n, 0.0)
    for h in H:
        acol("jN%d" % h, "jf", float(NS[h]), 16.0 * C0[h])
    for e in range(2):
        acol("dumA%d" % e, "jf", 1.0, 16.0 * e)
        acol("dumM%d" % e, "jf", 1.0, 4128.0 + 16 * e)
        acol("dumL%d" % e, "jf", 1.0, 2048.0 + 16 * e)
    acol("r3m", "r3", -KS, 0.0)
    acol("r0m", "r0", -1.0, f("r3m", 1), ["r3m"])
    acol("r03", "r0", 1.0, f("r3", 1), ["r3"])
    acol("r0l", "r0", 4096.0, 0.0)
    acol("r0n", "r0", 8192.0, 0.0)
    acol("r0p", "r0", -8192.0, 0.0)
    acol("r0z", "r03", Z2, 0.0)
    acol("nr0", "r03", -1.0, 1.0)
    acol("r12s", "r1", 64.0, f("r2", 1), ["r2"])
    tt(f("r12", 1), f("r1", 1), f("r2", 1), A.add, 1, ["r1", "r2"], ["r12"])
    ts(f("r12x", 1), f("r12", 1), 32.0, None, A.mult, None, 1, ["r12"], ["r12x"])
    cp(f("wp", 1), T.WI[:, 0:1], 1, ["WI"], ["wp"])
    ms(f("A0", 1), AOFF, 1, ["A0"])

    def Z(name, j):
        return b(name, 144, 15 - j, 143 - j)

    for name, val, dep in (("Zp", f("wp", 1), ["wp"]), ("Zs", -1.0 / 256, []), ("Zm", f("r0m", 1), ["r0m"])):
        ts(b(name, 144), f("I144", 144), f("g15", 1), val, A.is_equal, A.mult, 144, ["I144", "g15"] + dep, [name])
    rep("VA", b("Zn", 144), b("Zp", 144), -1.0, 144, ["Zp"], ["Zn"])
    ts(b("B1", 128), f("IG", 128), f("gf", 1), None, A.is_equal, None, 128, ["IG", "gf"], ["B1"])
    for name, val in (("Ba", "r12s"), ("B0", "r0p"), ("B0n", "r0n"), ("B0l", "r0l")):
        rep("VA", b(name, 128), b("B1", 128), f(val, 1), 128, ["B1", val], [name])
    op("G", lambda: g.affine_select(b("ID", 128), b("B1", 128), [[-1, 128]], A.is_equal, 0.0, 0, 1), 456, ["B1"], ["ID"])
    op("G", lambda: g.affine_select(b("TRI", 128), b("B1", 128), [[1, 128]], A.is_gt, 0.0, 0, -1), 456, ["B1"], ["TRI"])
    ts(b("I2k", WM), f("II", 256, 0, WM), 2.0, 1.0, A.mult, A.add, WM, ["II"], ["I2k"])
    for name, val in (("IK", KS), ("I4n", -4096.0), ("I8", 8192.0), ("I8n", -8192.0)):
        rep("VA", b(name, 128), b("ID", 128), val, 128, ["ID"], [name])
    rep("VAG", f("IF", 128), b("ID", 128), 1.0, 128, ["ID"], ["IF"], 1.0)
    ms(b("ON", 128), 1.0 / 16, 64, ["ON"])
    ms(b("on1", 32), 1.0, 64, ["on1"])
    ms(f("one", 128), 1.0, 128, ["one"])
    op("G", lambda: g.affine_select(f("G8", 128)[0:8, :], f("one", 128)[0:8, :], [[1, 8], [0, 16]], A.is_equal, 0.0, 0, -1), 456, ["one"], ["G8"])
    ts(T.DF[0:8, 0:768], T.DL[0:8, 0:768], -8192.0, None, A.add, None, 768, ["DL0", "DL1"], ["DF0"])
    cp(T.DF[0:8, 776:777], T.DL[0:8, 776:777], 1, ["DL0", "DL1"], ["DF1"])
    mm(T.SM[:, 300:301], f("G8", 128)[0:8, :], T.DF[0:8, 776:777], True, True, 1, ["G8", "DF1"], ["SM"], 4.0)
    ts(f("n256", 1), T.SM[:, 300:301], -1.0 / 256, 1.0, A.mult, A.add, 1, ["SM"], ["n256"])
    op("G", lambda: g.iota(f("IO", 16, 0, 15), [[-1, 15]], 14, 0, allow_small_or_imprecise_dtypes=True), 180, [], ["IOa"])
    ms(f("IO", 16, 15, 16), 15.0, 1, ["IOb"])
    ts(b("OH", 16), f("IO", 16), f("jf", 1), None, A.is_equal, None, 16, ["IOa", "IOb", "jf"], ["OH"])
    iota(f("IJ", 384, 0, 256), [[0, 8], [1, 32]], 256, ["IJa"])
    iota(f("IJ", 384, 256, 384), [[0, 8], [1, 16]], 128, ["IJb"])
    op("G", lambda: g.iota(f("IL", 384, 0, 256), [[0, 8], [1, 32]], -16, 0, allow_small_or_imprecise_dtypes=True), 662, [], ["ILa"])
    iota(f("IL", 384, 256, 384), [[0, 8], [1, 16]], 128, ["ILb"])
    op("G", lambda: g.iota(f("IB", 24, 0, 16), [[2, 8], [0, 2]], 1, 0, allow_small_or_imprecise_dtypes=True), 182, [], ["IBa"])
    iota(f("IB", 24, 16, 24), [[2, 8]], 8, ["IBb"])
    ts(b("eq", 160), f("IJ", 384, 0, 160), f("jf", 1), None, A.is_equal, None, 160, ["IJa", "jf"], ["eq"])
    ts(b("eq16", 160), f("II", 256, 0, 160), f("jf", 1), None, A.is_equal, None, 160, ["II", "jf"], ["eq16"])
    lin(b("CC", 480, 0, 160), b("eq", 160), SC, 6144.0 - SC, 160, ["eq"], ["CCa"])
    lin(b("CC", 480, 160, 320), b("eq16", 160), SC, 6144.0 - SC, 160, ["eq16"], ["CCb"])
    ms(f("C5", 160), 6144.0, 160, ["C5"])
    act(b("CC", 480, 320, 480), f("C5", 160), F.Silu, 1650 + 160, ["C5"], ["C6"])
    rep("GAV", b("CD", 480, 0, 240), b("CC", 480, 0, 240), 1.0, 240, ["CCa", "CCb"], ["CDa"])
    ms(b("CD", 480, 240, 480), 6144.0, 120, ["CDb"])
    lin(b("MK", WM), b("eq16", 160, 0, WM), BIG - 4096, -BIG, WM, ["eq16"], ["MK"])
    rep("VA", b("B1n", 128), b("B1", 128), -1.0, 128, ["B1"], ["B1n"])
    either(lambda: act(b("RL", 384), f("IJ", 384), F.Sign, 462, ["IJa", "IJb"], ["RL"]),
           lambda: ts(b("RL", 384), f("IJ", 384), 1.0, None, A.min, None, 384, ["IJa", "IJb"], ["RL"]))
    ts(b("eqL", 384), f("IL", 384), f("jf", 1), -8192.0, A.is_equal, A.mult, 384, ["ILa", "ILb", "jf"], ["eqL"])
    ts(b("gtL", 384), f("IL", 384), f("jf", 1), SC, A.is_gt, A.mult, 384, ["ILa", "ILb", "jf"], ["gtL"])
    ts(b("R0", WM), f("II", 256, 0, WM), 1.0, None, A.min, None, WM, ["II"], ["R0"])
    lin(b("RB", WM), b("R0", WM), -64.0, 64.0, WM, ["R0"], ["RB"])
    lin(f("RC", WM), b("R0", WM), 64.0 + 4 * KS, -64.0, WM, ["R0"], ["RC"])
    for h in H:
        n, sh = NS[h], str(h)
        c16 = lambda fn, name: fn(name, 16, C0[h], C0[h] + n)
        ts(c16(f, "jj"), f("I144", 144, 0, n), 16.0, f("jf", 1), A.mult, A.add, n, ["I144", "jf"], ["jj" + sh])
        ts(c16(i, "jq"), c16(f, "jj"), -(n - 1) / 2.0, 1.0 / n, A.add, A.mult, n, ["jj" + sh], ["jq" + sh])
        ts(c16(f, "jr"), c16(i, "jq"), (1.0 - 16 * n) / 16, float(C0[h]), A.mult, A.add, n, ["jq" + sh], ["jr" + sh])
        tt(c16(f, "js"), c16(f, "jr"), c16(f, "jj"), A.add, n, ["jr" + sh, "jj" + sh], ["js" + sh])
        ts(c16(u, "T0"), c16(f, "js"), 16.0, None, A.mult, None, n, ["js" + sh], ["T0" + sh])
        ts(c16(f, "D0"), f("I144", 144, 0, n), f("jN" + sh, 1), -256.0, A.add, A.add, n, ["I144", "jN" + sh], ["D0" + sh])
        ts(c16(u, "T1"), c16(f, "D0"), 256.0, None, A.add, None, n, ["D0" + sh], ["T1" + sh])
        rep("VA", c16(b, "DD"), c16(f, "D0"), -1.0, n, ["D0" + sh], ["DD" + sh])
    T0, T1 = ["T0%d" % h for h in H], ["T1%d" % h for h in H]
    cp(u("Boff", 24), f("IB", 24), 24, ["IBa", "IBb"], ["Boff"])
    for t in range(S):
        ms(T["box%d" % t][:, 0:80], 0.0, 40, ["box%d" % t, "bc%d" % t])

    ts(f("st1", 8), f("I144", 144, 0, 8), f("r1", 1), None, A.mult, None, 8, ["I144", "r1"], ["st1"])
    ts(f("st8", 8), f("I144", 144, 0, 8), f("r1", 1), 8.0, A.mult, A.mult, 8, ["I144", "r1"], ["st8"])
    ts(f("seed", 64), f("I144", 144, 0, 64), f("r2", 1), f("r12x", 1), A.mult, A.add, 64, ["I144", "r2", "r12x"], ["seed"])
    for k in range(8):
        lin(b("m0", 512, 64 * k, 64 * k + 64), f("seed", 64), 1.0, f("st1", 8, k, k + 1), 64, ["seed", "st1"], ["mta%d" % k])
    ts(f("I03", 128), f("II", 256, 0, 128), -1.5, None, A.add, None, 128, ["II"], ["I03"])
    tt(f("I04", 128), f("I03", 128), f("I03", 128), A.mult, 128, ["I03"], ["I04"])
    ts(f("I05", 128), f("I04", 128), 2.25, None, A.is_equal, None, 128, ["I04"], ["I05"])
    op("G", lambda: g.affine_select(b("S8", 128)[0:8, :], f("I05", 128)[0:8, :], [[1, 8], [0, 16]], A.is_equal, 0.0, 0, -1), 456, ["I05"], ["S8"])
    for k in range(7, -1, -1):
        bank, o, st = ("K0", "K1", "X3", "PL")[k % 4], MT(512 * k, 512 * k + 512), f("st8", 8, k, k + 1)
        mm(T[bank][:], b("S8", 128)[0:8, :], T.YM[0:8, 512 * k:512 * k + 512], True, False, 512, ["S8", "mk"], [bank])
        mm(T[bank][:], b("ID", 128), b("m0", 512), False, True, 512, ["ID"] + ["mta%d" % x for x in range(8)], [bank])
        either(lambda: act(o, T[bank][:], F.Identity, 78 + 512, [bank, "st8"], ["mtb%d" % k], bias=st),
               lambda: ts(o, T[bank][:], st, None, A.add, None, 512, [bank, "st8"], ["mtb%d" % k]))
    MTB = ["mtb%d" % k for k in range(8)]
    for k in range(8):
        rep("GV", T.OC[:, 256 * k:256 * k + 256], T.OCI[:, 256 * k:256 * k + 256], 1.0, 256, ["OCI%d" % (k // 4)], ["OCp%d" % k], 1.0)
    OCP = ["OCp%d" % k for k in range(8)]

    for t in range(S):
        B = W - 256 * (t + 1)
        act(b("yT%d" % t, 256), T.X[:, B:B + 256].indirect(u("T0", 16)), F.Copy, 78 + GA * 256, ["Xl"] + T0, ["yT%d" % t])
    YRT = {}

    def rep0(t):
        YRT[t] = ["YR%d_%d" % (t, k) for k in range(16)]
        for k in range(16):
            rep("VAG" if t == 0 else "G", T["YR%d" % t][:, k:4096:16], b("yT%d" % t, 256), 1.0, 256, ["yT%d" % t], [YRT[t][k]])

    def u_part(tag, r, rtok, zname, m):
        if tag[0] in PAR["UV"]:
            for j in range(16):
                mm(T.PU[:, 0:m], Z(zname, j), r(j), j == 0, j == 15, m, [zname] + rtok, ["PU"])
            act(b("fl" + tag, m), T.PU[:, 0:m], F.Identity, 78 + m, ["PU"], ["fl" + tag], bias=-128.5 * 4096 - 0.5, scale=-1.0)
            tt(f("w" + tag, m), T.PU[:, 0:m], b("fl" + tag, m), A.add, m, ["PU", "fl" + tag], ["w" + tag])
            act(f("q" + tag, m), f("w" + tag, m), F.Square, 78 + m, ["w" + tag], ["q" + tag], bias=592.0 + 129 * 4096)
            return
        for bank in ("PU", "PL"):
            for j in range(16):
                mm(T[bank][:, 0:m], Z(zname, j), r(j), j == 0, bank == "PU" and j == 15, m, [zname] + rtok, [bank])
        act(b("fl" + tag, m), T.PU[:, 0:m], F.Identity, 78 + m, ["PU"], ["fl" + tag], bias=128.5 + 1.0 / 8192, scale=1.0 / 4096)
        mm(T.PL[:, 0:m], b("I4n", 128), b("fl" + tag, m), False, True, m, ["I4n", "fl" + tag], ["PL"])
        act(f("q" + tag, m), T.PL[:, 0:m], F.Square, 78 + m, ["PL"], ["q" + tag], bias=592.0 + 129 * 4096)

    def place(tag, n, an, t, ctag, lt, a0, first=False):
        B = W - 256 * (t + 1)
        l, lu = i("l" + lt, 16, a0, a0 + n), u("lu" + lt, 16, a0, a0 + n)
        q, qt = f("q" + tag, n), "q" + tag
        ts(i("li" + tag, n), q, 1.0 / 32, f(an, 1), A.mult, A.add, n, [qt, an], ["li" + tag])
        ts(l, i("li" + tag, n), 2047, None, A.bitwise_and, None, n, ["li" + tag], ["l" + tag])
        cp(lu, l, n, ["l" + tag], ["lu" + tag])
        win = T.OCI[:, 0:2048] if first else T.OC[:, 0:2048]
        c = u(ctag, 16 * n)
        op("V", lambda: V.tensor_scalar(c, win.indirect(lu), B / 4096.0, -15.0 / 32, A.mult, A.add),
           60 + GA * 16 * n, ["lu" + tag] + (["OCI0", "OCI1"] if first else ["OC"] + OCP), [ctag])

    def keys(K, bw):
        return T.SM[:, 320:320 + bw] if K == "SM" else T[K][:, 0:bw]

    def main(ctag, c0, n, K, mn, mg, yr, a0, yrt, chunks, mchunks):
        bw = 16 * n
        o = keys(K, bw)
        mm(o, b("IK", 128), b("I32", WM, 0, bw), True, False, bw, ["IK", "I32", "I2k"], [K])
        mm(o, b("IK", 128), b("I2k", WM, 0, bw), False, False, bw, ["IK", "I32", "I2k"], [K])
        oV = ["~mV"] if PAR["ORD"] else []
        a = 0
        for c in chunks:
            e = a + c
            off = u(ctag, 16 * n, c0 + a * n, c0 + e * n)
            sl = slice(a0 + a * bw, a0 + e * bw)
            tg(T[mn][:, sl], T.X[:, 0:4096].indirect(off), T[yr][:, sl], A.min, 60 + GA * c * bw,
               [ctag, "Xl", "Xr"] + yrt, ["%s%d_%d" % (mn, a0, x) for x in range(a, e)] + oV)
            a = e
        a = 0
        for c in mchunks:
            e = a + abs(c)
            off = u(ctag, 16 * n, c0 + a * n, c0 + e * n)
            sl = slice(a0 + a * bw, a0 + e * bw)
            wt_ = ["%s%d_%d" % (mg, a0, x) for x in range(a, e)]
            o1, src = T[mg][:, sl], MT(0, 4096).indirect(off)
            onV = lambda: op("V", lambda o1=o1, src=src: V.tensor_copy(o1, src), 60 + GA * abs(c) * bw, [ctag, "MT"] + MTB, wt_)
            if c < 0:
                onV()
            else:
                either(lambda: act(o1, src, F.Copy, 78 + GA * c * bw, [ctag, "MT"] + MTB, wt_), onV)
            a = e
        nacc[0] += 1
        for src, zn, cs in ((mn, "Zs", chunks), (mg, "Zm", mchunks)):
            a = 0
            for c in cs:
                e = a + abs(c)
                mma(o, [(Z(zn, x), T[src][:, a0 + x * bw:a0 + (x + 1) * bw]) for x in range(a, e)], bw,
                    [zn] + ["%s%d_%d" % (src, a0, x) for x in range(a, e)], [K])
                a = e

    def pick(tag, n, K):
        bw, jn = 16 * n, "jB%d" % n
        scan(f("R" + K, bw), b("RB", WM, 0, bw), keys(K, bw), A.add, A.min, bw, ["RB", K], ["R" + K])
        ts(i("ki" + tag, n), f("R" + K, bw, 15, bw, 16), 1 / KS, BIG, A.mult, A.add, n, ["R" + K], ["ki" + tag])
        ts(i("kx" + tag, n), i("ki" + tag, n), 1, 255, A.arith_shift_right, A.bitwise_and, n, ["ki" + tag], ["kx" + tag])
        ts(u("ku" + tag, n), i("kx" + tag, n), f(jn, 1), None, A.add, None, n, ["kx" + tag, jn], ["ku" + tag])

    def toks(name, a0):
        return ["%s%d_%d" % (name, a0, x) for x in range(16)]

    def mark(tag, n, mg, a0, nl, nlt, ag, s, XX, final=False):
        bw = 16 * n
        at = "ag" + tag[0] + s
        X_ = T[XX]
        odd = n > PAR["ODD"]
        wb = bw // 2 if odd else bw
        x1 = [X_[:, 0:bw], X_[:, 160:160 + wb]]
        x2 = [X_[:, 320:320 + bw], X_[:, 240:240 + wb] if odd else X_[:, 320:320 + bw]]

        def spread(mat, src, tok, last):
            for c in range(n // 2 * odd):
                for x in (160, 240):
                    mm(X_[:, x + 16 * c:x + 16 * c + 16], b(mat, 128), src(32 * c + 16, 32 * c + 32), False, False, 16, [mat] + tok, [XX])
            for x in ((0, 320) if odd else (0, 160, 320)):
                mm(X_[:, x:x + bw], b(mat, 128), src(0, bw), False, last and x == 320, bw, [mat] + tok, [XX])

        cc = "CD" if odd else "CC"
        mm(X_[:, 0:320 + bw], b("ID", 128), b(cc, 480, 0, 320 + bw), True, False, 320 + bw, ["ID", "CCa", "CCb", "C6", "CDa", "CDb"], [XX])
        spread("B0", nl, nlt, False)
        act(ag(0, bw), T[mg][:, a0:a0 + 16 * bw].indirect(u("ku" + tag, n)), F.Identity, 78 + GA * bw, toks(mg, a0) + ["ku" + tag, "nr0", "r0z"], [at],
            bias=f("r0z", 1), scale=f("nr0", 1))
        spread("Ba", ag, [at], True)
        if not final:
            rep("GAV", f("agf" + s, bw), ag(0, bw), 1.0, bw, [at], ["agf" + s], 1.0)
        for e, w, st, rx in ((0, bw, 32, b("RL", 384, 0, bw)), (1, wb, 16 if odd else 32, b("RL", 384, 256, 256 + wb))):
            z = "%d%s" % (e, s)
            scan(f("H" + z, w), rx, x1[e], A.mult, A.max, w, ["RL", XX], ["H" + z])
            tt(b("E" + z, w), x2[e], f("H" + z, w), A.not_equal, w, [XX, "H" + z], ["E" + z], 1.0)
            scan(f("Fs" + z, w), b("E" + z, w), x1[e], A.mult, A.max, w, [XX, "E" + z], ["Fs" + z])
            ts(u("mo" + tag, n, e, n, 2), f("Fs" + z, w, st - 1, w, st), f("dumA%d" % e, 1), f("dumM%d" % e, 1), A.max, A.min, n,
               ["Fs" + z, "dumA%d" % e, "dumM%d" % e], ["mo%d" % e + tag])
        for c in range(n // 2):
            off = u("mo" + tag, n, 2 * c, 2 * c + 2)
            if final:
                op("V", lambda off=off: V.tensor_copy(T.YM[:, 0:4160].indirect(off), b("on1", 32)), 60 + SCA * 32,
                   ["mo0" + tag, "mo1" + tag, "on1"], ["YM"] + ["YM%d" % k for k in range(8)])
            else:
                act(T.MT[:, 0:4160].indirect(off), f("agf" + s, bw, 32 * c, 32 * c + 32), F.Silu,
                    78 + SCA * 32, ["mo0" + tag, "mo1" + tag, "agf" + s], ["MT"] + MTB)
                del MTB[:]

    def turn(eng, name, src, stok):
        if eng == "A":
            act(b(name, 256), b(src, 256).indirect(u("T1", 16)), F.Copy, 78 + GA * 256, sorted(set(stok)) + T1, [name])
            return [[name]] * NH
        for c in range(16):
            rep(eng, b(name, 256, 16 * c, 16 * c + 16), b(src, 256)[:, back(c)], 1.0, 16, [stok[hof[c]]], [name + "_%d" % c])
        return [[name + "_%d" % c for c in range(16) if hof[c] == h] for h in H]

    def back(c, a=0):
        h = hof[c]
        return slice(a + 15 * C0[h] + c, a + 16 * (C0[h] + NS[h]), NS[h])

    def lanes0(t):
        u_part("a%d" % t, lambda j: b("yT%d" % t, 256, j, 256, 16), ["yT%d" % t], "Zp", 16)

    def place0(t):
        place("a%d" % t, 16, "A%d" % t, t, "ca", "a%d" % t, 0, t == 0)

    rep0(0)
    lanes0(0)
    place0(0)
    rep0(1)
    for t in range(S):
        B = W - 256 * (t + 1)
        tr = "r%d" % t
        now[0] = t
        nln, nlt = "NL%d" % t, "NT%d" % t
        part = lambda name, h: b(name, 256, 16 * C0[h], 16 * (C0[h] + NS[h]))
        sub = lambda name, h: (lambda x, y: b(name, 256, 16 * C0[h] + x, 16 * C0[h] + y))
        rep("GAV", b(nln, 256), MT(B, B + 256), 1.0, 256, ["MT"] + MTB, [nln], 1.0)
        NT = turn(PAR["NT"], nlt, nln, [nln] * NH)
        for h in H:
            main("ca", 16 * C0[h], NS[h], "K%d" % h, "MN", "MG", "YR%d" % t, 256 * C0[h], YRT[t], PAR["CX"][0, h] if t else PAR["CX0"][h],
                 PAR["CM"][0, h] if t else PAR["CM0"][h])
        if t + 1 < S:
            lanes0(t + 1)
        yrt = {}
        for h in H:
            N, BW, L0 = NS[h], 16 * NS[h], 16 * C0[h]
            ta, tb, a0 = "a%d%d" % (t, h), "b%d%d" % (t, h), 16 * L0
            pick(ta, N, "K%d" % h)
            tg(part("y1n", h), T.MN[:, a0:a0 + 16 * BW].indirect(u("ku" + ta, N)), T.X[:, B + L0:B + L0 + BW], A.subtract,
               60 + GA * BW, toks("MN", a0) + ["ku" + ta, "Xl"], ["y1n%d" % h])
            mark(ta, N, "MG", a0, sub(nln, h), [nln], sub("aga", h), str(h), "X%d" % h)
            u_part(tb, lambda j: b("y1n", 256, L0 + j, L0 + BW, 16), ["y1n%d" % h], "Zn", N)
            yrt[h] = ["YRh%d_%d" % (h, k) for k in range(16)]
            rep("AV", part("y1p", h), part("y1n", h), -1.0, BW, ["y1n%d" % h], ["y1p%d" % h])
            for k in range(16):
                e, src, sign = ("GAV", "y1p", 1.0) if k < PAR["REP"][h] else ("AV", "y1n", -1.0)
                rep(e, T.YRh[:, a0 + k:a0 + 16 * BW:16], part(src, h), sign, BW, [src + str(h)], [yrt[h][k]])
            place(tb, N, "A%d" % t, t, "cb%d" % h, "b%d" % t, C0[h])
        Y1T = turn(PAR["Y1T"], "y1T", "y1n", ["y1n%d" % h for h in H])
        mm(T.X3[:, 0:256], b("B0n", 128), b(nln, 256), True, False, 256, ["B0n", nln], ["X3"])
        mm(T.X3[:, 0:256], b("Ba", 128), b("aga", 256), False, True, 256, ["Ba"] + ["aga%d" % h for h in H], ["X3"])

        def ya_out(x):
            ya = T.YA[:, 512 * t + 256 * x:512 * t + 256 * x + 256]
            if PAR["YA"][x] == "A":
                act(f("yat", 256), T.X3[:, 256 * x:256 * x + 256], F.Relu, 78 + 256, ["X3"], ["yat"], bias=1.0 - OFFS - 8192)
                act(ya, f("yat", 256), F.Identity, 78 + 256, ["yat"], ["YA%d%d" % (t, x)], bias=-1.0)
            else:
                ts(ya, T.X3[:, 256 * x:256 * x + 256], -OFFS - 8192, -1.0, A.add, A.max, 256, ["X3"], ["YA%d%d" % (t, x)])

        ya_out(0)
        for h in H:
            main("cb%d" % h, 0, NS[h], "K%d" % h, "MN", "MG", "YRh", 256 * C0[h], yrt[h], PAR["CX"][1, h], PAR["CM"][1, h])
        tb = "b%d" % t
        LU, LL = ["lu%s%d" % (tb, h) for h in H], ["l%s%d" % (tb, h) for h in H]
        act(f("nn", 256), T.OC[:, 0:2048].indirect(u("lu" + tb, 16)), F.Copy, 78 + GA * 256, ["OC"] + OCP + LU, ["nn"])
        act(b("lg", 256), MT(0, 2048).indirect(u("lu" + tb, 16)), F.Copy, 78 + GA * 256, ["MT"] + LU, ["lg"])
        ts(f("ls" + tb, 16), i("l" + tb, 16), 1.0 / SC, None, A.mult, None, 16, LL, ["ls" + tb])
        act(f("lb", 384), f("ls" + tb, 16).indirect(u("Boff", 24)), F.Identity, 78 + GA * 384, ["ls" + tb, "Boff"], ["lb"], bias=OFFS - 8192, scale=SC)
        mm(T.PL[:, 0:384], b("ID", 128), b("eqL", 384), True, False, 384, ["ID", "eqL"], ["PL"])
        mm(T.PL[:, 0:384], b("ID", 128), b("gtL", 384), False, False, 384, ["ID", "gtL"], ["PL"])
        for mat, src in (("B0", nln), ("Ba", "lg")):
            mm(T.PL[:, 0:256], b(mat, 128), b(src, 256), False, False, 256, [mat, src], ["PL"])
            for c in range(8):
                mm(T.PL[:, 256 + 16 * c:272 + 16 * c], b(mat, 128), b(src, 256, 32 * c, 32 * c + 16), False, mat == "Ba" and c == 7, 16, [mat, src], ["PL"])
        tt(b("El", 384), T.PL[:, 0:384], f("lb", 384), A.is_equal, 384, ["PL", "lb"], ["El"], 1.0)
        scan(b("Fl", 384), b("RL", 384), b("El", 384), A.mult, A.max, 384, ["RL", "El"], ["Fl"], 0.5)
        for e, (lo, hi, st) in enumerate(((271, 384, 16), (31, 256, 32))):
            tt(f("Gl%d" % e, 8), b("Fl", 384, lo, hi, st), f("ls" + tb, 16, e, 16, 2), A.max, 8, ["Fl", "ls" + tb], ["Gl%d" % e])
            ts(u("no", 16, e, 16, 2), f("Gl%d" % e, 8), SC, f("dumL%d" % e, 1), A.mult, A.min, 8, ["Gl%d" % e, "dumL%d" % e], ["no%d" % e])
        box, land = T["box%d" % t], T["land%d" % t]
        for h in H:
            N, BW, L0, sh = NS[h], 16 * NS[h], 16 * C0[h], str(h)
            sm = T.SM[:, L0:L0 + BW]
            mm(sm, b("ID", 128), b("MK", WM, 0, BW), True, False, BW, ["ID", "MK"], ["SM"])
            mm(sm, b("B0l", 128), part(nlt, h), False, False, BW, ["B0l"] + NT[h], ["SM"])
            mm(sm, b("B1n", 128), part("y1T", h), False, True, BW, ["B1n"] + Y1T[h], ["SM"])
            scan(f("SR", 256, L0, L0 + BW), b("R0", WM, 0, BW), sm, A.mult, A.max, BW, ["R0", "SM"], ["SR" + sh])
            lin(f("Sc", 16, C0[h], C0[h] + N), f("SR", 256, L0 + 15, L0 + BW, 16), 1.0 / 256, f("n256", 1), N, ["SR" + sh, "n256"], ["Sc" + sh])
        for h in H:
            N, BW, L0 = NS[h], 16 * NS[h], 16 * C0[h]
            tbh, a0, sh, K = "b%d%d" % (t, h), 16 * L0, str(h), "K%d" % h
            c16 = lambda fn, name: fn(name, 16, C0[h], C0[h] + N)
            fp = lambda name: f(name, 256, L0, L0 + BW)
            pick(tbh, N, K)
            m2, src = part("mn2", h), T.MN[:, a0:a0 + 16 * BW].indirect(u("ku" + tbh, N))
            either(lambda: act(m2, src, F.Copy, 78 + GA * BW, toks("MN", a0) + ["ku" + tbh], ["mn2" + sh]),
                   lambda: op("V", lambda m2=m2, src=src: V.tensor_copy(m2, src), 60 + GA * BW, toks("MN", a0) + ["ku" + tbh], ["mn2" + sh]))
            tt(c16(f, "Su"), f("R" + K, BW, 15, BW, 16), c16(f, "Sc"), A.add, N, ["R" + K, "Sc" + sh], ["Su" + sh])
            ts(c16(i, "kb"), i("ki" + tbh, N), 1, None, A.bitwise_and, None, N, ["ki" + tbh], ["kb" + sh])
            tt(c16(b, "rdy"), c16(f, "Su"), c16(i, "kb"), A.is_ge, N, ["Su" + sh, "kb" + sh], ["rdy" + sh])
            scan(c16(b, "Pp"), b("R0", WM, 0, N), c16(b, "rdy"), A.mult, A.add, N, ["R0", "rdy" + sh], ["Pp" + sh])
            tt(c16(b, "rD"), c16(b, "rdy"), c16(f, "D0"), A.mult, N, ["rdy" + sh, "D0" + sh], ["rD" + sh])
            end = lambda x: b("Pp", 16, C0[x] + NS[x] - 1, C0[x] + NS[x])
            a1 = T.SM[:, 272:272 + N]
            for z, src in enumerate(("DD", "rD", "Pp")):
                mm(a1, b("ID", 128), c16(b, src), z == 0, z == 2, N, ["ID", src + sh], ["SM"])
            for x in range(h + 1):
                mm(T.SM[:, 256:257], b("TRI" if x == h else "B1", 128), end(x), x == 0, x == h, 1, ["TRI", "B1", "Pp%d" % x], ["SM"])
            if h == NH - 1:
                for x in range(NH):
                    mm(T.SM[:, 264:265], b("B1", 128), end(x), x == 0, x == NH - 1, 1, ["B1", "Pp%d" % x], ["SM"])
            ts(c16(u, "so"), a1, T.SM[:, 256:257], -1.0, A.add, A.add, N, ["SM"], ["so" + sh])
            if h == NH - 1:
                ts(box[:, 8:9], T.SM[:, 264:265], 64.0, None, A.min, None, 1, ["SM"], ["bc%d" % t])
            tg(box[:, 16:272].indirect(c16(u, "so")), m2, part("y1T", h), A.add, 60 + SCA * BW, ["so" + sh, "mn2" + sh] + Y1T[h], ["box%d" % t])
            scan(fp("R2"), f("RC", WM, 0, BW), T[K][:, 0:BW], A.add, A.max, BW, ["RC", K], ["R2" + sh])
            ts(c16(i, "k2"), f("R2", 256, L0 + 15, L0 + BW, 16), 1 / KS, BIG, A.mult, A.add, N, ["R2" + sh], ["k2" + sh])
            ts(c16(i, "k3"), c16(i, "k2"), 1, 15, A.arith_shift_right, A.bitwise_and, N, ["k2" + sh], ["k3" + sh])
            cp(c16(u, "k4"), c16(i, "k3"), N, ["k3" + sh], ["k4" + sh])
            act(part("kg", h), b("OH", 16).indirect(c16(u, "k4")), F.Copy, 78 + GA * BW, ["OH", "k4" + sh], ["kg" + sh])
            p0, p1 = 2 * L0, 2 * L0 + 2 * BW
            for x, mat in enumerate(("I8", "I8n")):
                o = T.PL[:, p0 + BW * x:p0 + BW * x + BW]
                if x == 0:
                    mm(o, f("G8", 128)[0:8, :], T.DF[0:8, 256 * t + L0:256 * t + L0 + BW], True, False, BW, ["G8", "DF0"], ["PL"], 4.0)
                else:
                    mm(o, f("IF", 128), fp("nn"), True, False, BW, ["IF", "nn"], ["PL"], 4.0)
                for c in range(N):
                    mm(T.PL[:, p0 + BW * x + c:p0 + BW * x + BW:N], b(mat, 128), b("kg", 256, L0 + 16 * c, L0 + 16 * c + 16), False, c == N - 1, 16,
                       [mat, "kg" + sh], ["PL"])
            either(lambda: act(f("pv", 512, p0, p1), T.PL[:, p0:p1], F.Relu, 78 + 2 * BW, ["PL"], ["pv" + sh]),
                   lambda: ts(f("pv", 512, p0, p1), T.PL[:, p0:p1], 0.0, None, A.max, None, 2 * BW, ["PL"], ["pv" + sh]))
        for c in range(14, -1, -2):
            p0, BW = 16 * (c + C0[hof[c]]), 16 * NS[hof[c]]
            tg(T.OC[:, 0:2080].indirect(u("no", 16, c, c + 2)), f("pv", 512, p0, p0 + 32), f("pv", 512, p0 + BW, p0 + BW + 32),
               A.add, 60 + SCA * 32, ["no0", "no1", "pv%d" % hof[c]], ["OC"] + (OCP if t == 0 and c == 14 else []))
        dst = dst_of(t)
        rid, pid, _ = topo.addr(dst)
        m = 0
        for e in topo.engines(core, dst)[0::2][:NENG]:
            m |= 1 << e
        op("G", lambda box=box, land=land, t=t, pid=pid, rid=rid, m=m: g.remote_dma(land[:, 8:80], box[:, 8:80], T.sem["arr%d" % t], T.sem.sent, pid, rid, m),
           300, ["box%d" % t, "bc%d" % t], ["land%d" % t], lat=2500, dma="arr%d" % t)
        if t + 2 < S:
            rep0(t + 2)
        for h in H:
            mark("b%d%d" % (t, h), NS[h], "MG", 256 * C0[h], sub(nlt, h), NT[h], sub("agb", h), str(h), "X%d" % h)
        if t == S - 1:
            dma("S", T.yo[:], T.OC[:, 0:2048], ["OC"], ["yo"], 5000)
            for k in range(8):
                rep("AVG", T.YM[:, 32 + 512 * k:544 + 512 * k], MT(512 * k, 512 * k + 512), 1.0, 512, ["MT"], ["YM%d" % k] + ["mk"] * (k == 0), 1.0)
        mm(T.X3[:, 256:512], b("B0n", 128), b(nln, 256), True, False, 256, ["B0n", nln], ["X3"])
        for c in range(16):
            mm(T.X3[:, back(c, 256)], b("Ba", 128), b("agb", 256, 16 * c, 16 * c + 16), False, c == 15, 16, ["Ba", "agb%d" % hof[c]], ["X3"])
        ya_out(1)
        dma("S", T.ya[:, 512 * t:512 * t + 512], T.YA[0:128:16, 512 * t:512 * t + 512], ["YA%d0" % t, "YA%d1" % t], ["ya%d" % t], 2000)
        lt = ["land%d" % t]
        u_part(tr, lambda j: land[:, 16 + j:80:16], lt, "Zn", 4)
        yr = ["YRr%d" % k for k in range(16)]
        rep("AV", b("yrp", 64), land[:, 16:80], -1.0, 64, lt, ["yrp"])
        for k in range(16):
            if k < PAR["REPR"]:
                rep("GAV", T.YRr[:, k:1024:16], b("yrp", 64), 1.0, 64, ["yrp"], [yr[k]])
            else:
                rep("AV", T.YRr[:, k:1024:16], land[:, 16:80], -1.0, 64, lt, [yr[k]])
        place(tr, 4, "A%d" % t, t, "cr", tr, 0)
        ts(b("NR", 64), f("SLOT", 64), land[:, 8:9], None, A.is_lt, None, 64, ["SLOT"] + lt, ["NR"])
        if t + 1 < S:
            an = "A%d" % (t + 1)
            mm(T.SM[:, 300:301], b("ON", 128), land[:, 8:9], True, True, 1, ["ON"] + lt, ["SM"])
            cp(i("ai", 1), T.SM[:, 300:301], 1, ["SM"], ["ai"])
            ts(i("aj", 1), i("ai", 1), 63, None, A.bitwise_and, None, 1, ["ai"], ["aj"])
            ts(f(an, 1), i("aj", 1), AOFF, None, A.add, None, 1, ["aj"], [an])
            place0(t + 1)
        main("cr", 0, 4, "SM", "MNr", "MGr", "YRr", 0, yr, PAR["CXR"], PAR["CMR"])
        pick(tr, 4, "SM")
        mark(tr, 4, "MGr", 0, lambda x, y: b("NR", 64, x, y), ["NR"], lambda x, y: b("agr", 64, x, y), "r", "X0", t == S - 1)
    dma("S", T.ym[:], T.YM[0:128:16, 32:4128], ["YM"], ["ym"], 2000)
    return ops


def graph(ops):
    lastw, readers, bank, opened = {}, {}, {}, {}
    deps = []
    for k, o in enumerate(ops):
        d = set()
        for x in o["r"] + o["w"]:
            if x in lastw and x[0] != "~":
                if o["acc"] is not None and x in BANKS:
                    d.add(opened.setdefault(o["acc"], lastw[x][0]))
                else:
                    d.update(lastw[x])
        for x in o["w"]:
            d.update(readers.get(x, ()))
        d = {a: not (ops[a]["e"] == "P" and o["e"] == "P") for a in d}
        for x in sorted(set(o["r"] + o["w"])):
            if x[0] == "~":
                if x in bank:
                    d.setdefault(bank[x], False)
                bank[x] = k
            elif x in BANKS and o["acc"] is None:
                e = "?" if o["alt"] else o["e"]
                was, now, before = bank.get(x, ("", [], []))
                if e == was == "V":
                    now.append(k)
                else:
                    before, bank[x] = now, (e, [k], now)
                for a in before:
                    d.setdefault(a, not (e == was and e in "PA"))
        for x in o["r"]:
            readers.setdefault(x, []).append(k)
        for x in o["w"]:
            lastw[x] = lastw[x] + [k] if o["acc"] is not None else [k]
            readers[x] = []
        d.pop(k, None)
        deps.append(d)
    for t in range(S):
        for x, nx, y, ny in PAR["FIRST"]:
            a = [k for k, o in enumerate(ops) if o["t"] == t and o["w"][0].startswith(x)]
            c = [k for k, o in enumerate(ops) if o["t"] == t and o["w"][0].startswith(y)]
            if len(a) > nx and len(c) > ny:
                deps[c[ny]].setdefault(a[nx], False)
    return deps


def plan(ops, deps, others):
    n = len(ops)
    pred = [[(a, (ops[a]["lat"] + PAR["SIG"]) if w else 0.0) for a, w in deps[k].items()] for k in range(n)]
    succ = [[] for _ in range(n)]
    for k in range(n):
        for a, d in pred[k]:
            succ[a].append((k, d))
    lat = [o["lat"] for o in ops]
    alts = [[(e, c) for e, c, _ in o["alt"]] for o in ops]
    eng, cost = [o["e"] for o in ops], [o["c"] for o in ops]
    names = [o["w"][0].rstrip("0123456789_") for o in ops]
    weight = [1.0 if o["e"] in "GS" else o["c"] for o in ops]
    seed = [PAR["SEED"]]

    def rnd():
        seed[0] = (seed[0] * 1103515245 + 12345) % 2147483648
        return seed[0] / 2147483648.0

    def gap(iv, s, c):
        lo, hi = 0, len(iv)
        while lo < hi:
            mid = (lo + hi) // 2
            if iv[mid][1] <= s:
                lo = mid + 1
            else:
                hi = mid
        while lo < len(iv) and iv[lo][0] < s + c:
            if iv[lo][1] > s:
                s = iv[lo][1]
            lo += 1
        return s, lo

    def place(win, val, start, eng, cost, busy, price):
        for k in win:
            for a, _ in pred[k]:
                if a in val and val[a] > val[k]:
                    val[k] = val[a]
        for k in sorted(win, key=lambda k: (val[k], k)):
            s = 0.0
            for a, d in pred[k]:
                x = start[a] + cost[a] + d
                if x > s:
                    s = x
            if price is not None and alts[k]:
                eng[k], cost[k] = min(alts[k], key=lambda z: gap(busy[z[0]], s, z[1])[0] + z[1] * price[z[0]])
            iv = busy[eng[k]]
            s, lo = gap(iv, s, cost[k])
            iv.insert(lo, (s, s + cost[k]))
            start[k] = s

    def settle(start, order):
        free = dict.fromkeys("VAPGS", 0.0)
        for k in order:
            s = free[eng[k]]
            for a, d in pred[k]:
                x = start[a] + cost[a] + d
                if x > s:
                    s = x
            start[k] = s
            free[eng[k]] = s + cost[k]
        tail = [0.0] * n
        free = dict.fromkeys("VAPGS", 0.0)
        for k in reversed(order):
            s = max(lat[k], free[eng[k]])
            for a, d in succ[k]:
                x = tail[a] + d
                if x > s:
                    s = x
            tail[k] = free[eng[k]] = s + cost[k]
        return tail

    def length(win, out, first, st, en, co):
        ends = sorted(st[k] + co[k] + max(out[k], first[en[k]]) for k in win)
        top = ends[-PAR["TOP"]:]
        early = sum(weight[k] * (st[k] + co[k]) for k in win) / sum(weight[k] for k in win)
        return ends[-1] + PAR["SOFT"] * sum(top) / len(top) + PAR["EARLY"] * early

    hint = [list(x) for x in succ]
    for kind in ("MN", "MG"):
        run = [k for k in range(n) if names[k] in (kind, kind + "r")]
        for a, k in zip(run, run[1:]):
            hint[a].append((k, -PAR["HINT"][kind] * cost[a]))
    tail = [0.0] * n
    for k in range(n - 1, -1, -1):
        tail[k] = cost[k] + max([lat[k]] + [tail[x] + d for x, d in hint[k]])
    start = [0.0] * n
    place(range(n), {k: -tail[k] for k in range(n)}, start, eng, cost, {e: [] for e in "VAPGS"}, {"V": 2.0, "A": 1.0, "G": 1.0})
    order = sorted(range(n), key=lambda k: (start[k], k))
    tail = settle(start, order)
    span = max(tail)
    more = []
    for o2, sig in others:
        cs = [dict([(o["e"], o["c"])] + [(e, c) for e, c, _ in o["alt"]]) for o in o2]
        pr = [[(a, (lat[a] + sig) if w else 0.0) for a, w in deps[k].items()] for k in range(n)]
        su = [[] for _ in range(n)]
        for k in range(n):
            for a, d in pr[k]:
                su[a].append((k, d))
        more.append({"c": cs, "pred": pr, "succ": su})

    def forward(z, seq, en, end, free):
        for k in seq:
            s = free[en[k]]
            for a, d in z["pred"][k]:
                if end[a] + d > s:
                    s = end[a] + d
            end[k] = free[en[k]] = s + z["c"][k][en[k]]

    def settle_more():
        for z in more:
            z["end"], z["tail"] = [0.0] * n, [0.0] * n
            forward(z, order, eng, z["end"], dict.fromkeys("VAPGS", 0.0))
            free, tl = dict.fromkeys("VAPGS", 0.0), z["tail"]
            for k in reversed(order):
                s = max(lat[k], free[eng[k]])
                for a, d in z["succ"][k]:
                    if tl[a] + d > s:
                        s = tl[a] + d
                tl[k] = free[eng[k]] = s + z["c"][k][eng[k]]
        return sum(max(z["tail"]) for z in more) * PAR["WELSE"]

    def length_more(seq, st, en):
        x = 0.0
        seq = sorted(seq, key=lambda k: (st[k], k))
        for z in more:
            end = list(z["end"])
            forward(z, seq, en, end, dict(z["free"]))
            x += max(end[k] + max(z["out"][k], z["first"][en[k]]) for k in seq)
        return x * PAR["WELSE"]

    best = (span + settle_more(), list(start), list(eng), list(cost), span)
    R = PAR["ROUNDS"]
    for r in range(R):
        m = int(PAR["WIN"] * (0.4 + rnd()))
        i0 = max(0, int(rnd() * (n + m // 2)) - m // 2)
        win, rest = sorted(order[i0:i0 + m]), order[i0 + m:]
        held = {e: [(-1.0, start[order[max(0, i0 - 100)]])] for e in "VAPGS"}
        for k in order[max(0, i0 - 100):i0]:
            held[eng[k]].append((start[k], start[k] + cost[k]))
        t2, out, first = {}, {}, dict.fromkeys("VAPGS", 0.0)
        for k in reversed(rest[:200]):
            first[eng[k]] = tail[k]
        for k in reversed(win):
            t2[k] = cost[k] + max([lat[k]] + [t2.get(a, tail[a]) + d for a, d in hint[k]])
            out[k] = max([lat[k]] + [tail[a] + d for a, d in succ[k] if a not in t2])
        seq = order[max(0, i0 - 100):i0 + m]
        inside = set(order[:i0 + m])
        for z in more:
            z["free"], z["first"] = dict.fromkeys("VAPGS", 0.0), dict.fromkeys("VAPGS", 0.0)
            for k in order[max(0, i0 - 400):max(0, i0 - 100)]:
                z["free"][eng[k]] = z["end"][k]
            for k in reversed(rest[:200]):
                z["first"][eng[k]] = z["tail"][k]
            z["out"] = {k: max([lat[k]] + [z["tail"][a] + d for a, d in z["succ"][k] if a not in inside]) for k in seq}
        now = length(win, out, first, start, eng, cost)
        bound = now + length_more(seq, start, eng) + PAR["TEMP"] * (1 - r / R) * rnd()
        pick = None
        for _ in range(PAR["TRIES"]):
            mode, amp, mix, w2 = rnd(), PAR["NOISE"] * (0.1 + 2 * rnd() ** 2), rnd(), PAR["W2"] * rnd() ** 2
            sh, val = {}, {}
            for k in win:
                key = names[k] if mode < 0.6 else k
                if key not in sh:
                    sh[key] = amp * (rnd() - 0.5) if rnd() < 0.3 else 0.0
                val[k] = (1 - w2) * (mix * start[k] + (1 - mix) * (span - tail[k])) + w2 * (span - t2[k]) + sh[key]
            price = {"V": 1 + 4 * rnd() ** 2, "A": 1 + 2 * rnd() ** 2, "G": 1.5 * rnd()} if rnd() < PAR["PICK"] else None
            s2, e2, c2 = list(start), list(eng), list(cost)
            place(win, val, s2, e2, c2, {e: list(v) for e, v in held.items()}, price)
            x = length(win, out, first, s2, e2, c2)
            if x < now + PAR["SKIP"]:
                x += length_more(seq, s2, e2)
                if x <= bound:
                    bound, pick = x, (s2, e2, c2)
        if pick:
            start, eng[:], cost[:] = pick
            order = sorted(order[:i0 + m], key=lambda k: (start[k], k)) + rest
            tail = settle(start, order)
            order.sort(key=lambda k: (start[k], k))
            span = max(tail)
            x = span + settle_more()
            if x < best[0]:
                best = (x, list(start), list(eng), list(cost), span)
    return best


PLAN = {}


def rank_program(g, core, T, topo):
    rank = T.rank_of(core)
    if rank is None:
        return
    n = len(T.cores)
    dst_of = lambda t: T.cores[(rank + 1 + t % (n - 1)) % n]
    ops = build(g, T, dst_of, topo, core, PAR)
    deps = graph(ops)
    if "start" not in PLAN:
        others = [(build(g, T, dst_of, topo, core, dict(PAR, **z)), z["SIG"]) for z in PAR["ELSE"]]
        PLAN["start"], PLAN["eng"] = plan(ops, deps, others)[1:3]
    start = PLAN["start"]
    for o, e in zip(ops, PLAN["eng"]):
        for e2, _, fn in o["alt"]:
            if e2 == e:
                o["e"], o["fn"] = e, fn
    order = sorted(range(len(ops)), key=lambda k: (start[k], k))
    closes = {ops[k]["acc"]: k for k in order}
    need = set(a for d in deps for a, w in d.items() if w)
    queue = {"V": g.vector, "A": g.scalar, "P": g.tensor, "G": g, "S": g.sync}
    total = {}
    for o in ops:
        if o["dma"] is not None:
            total[o["dma"]] = total.get(o["dma"], 0) + (NENG if o["dma"].startswith("arr") else 16)
    count = {"cV": 0, "cA": 0, "cP": 0, "cG": 0}
    sig = {}
    known = {e: {} for e in queue}
    clock = {}
    for k in order:
        o = ops[k]
        e = o["e"]
        kn = known[e]
        want = {}
        for a, w in deps[k].items():
            if w:
                s, v = sig[a]
                if v > want.get(s, (0, None))[0]:
                    want[s] = (v, a)
        for s, (v, a) in sorted(want.items(), key=lambda z: -start[z[1][1]]):
            if kn.get(s, 0) < v:
                queue[e].wait_ge(T.sem[s], v)
                kn[s] = v
                for s2, v2 in clock[a].items():
                    if kn.get(s2, 0) < v2:
                        kn[s2] = v2
        ins = o["fn"]() if o["acc"] is None else o["fn"](closes[o["acc"]] == k)
        remote = o["dma"] is not None and o["dma"].startswith("arr")
        clock[k] = {} if remote else dict(kn)
        if o["dma"] is not None:
            if not remote:
                ins.then_inc(T.sem[o["dma"]], 16)
            sig[k] = (o["dma"], total[o["dma"]])
        elif k in need:
            s = "c" + e
            count[s] += 1
            ins.then_inc(T.sem[s], 1)
            sig[k] = (s, count[s])
    for s, v in list(count.items()) + list(total.items()):
        if known["G"].get(s, 0) < v:
            g.wait_ge(T.sem[s], v)
    g.wait_ge(T.sem.sent, S * NENG)
